import numpy as np, ml_dtypes
CORES = [8,9,10,11,12,13]
N = 6
BF = ml_dtypes.bfloat16
def gentries(a):
    return np.ascontiguousarray(a.reshape(8, 16, -1).transpose(0, 2, 1)).reshape(8, -1)
def gtable(e):
    e = np.asarray(e); return np.ascontiguousarray(e.reshape(8, -1, 16).transpose(0, 2, 1)).reshape(128, -1).astype(np.int32)
def f(rng, *shape):
    return (rng.standard_normal(shape, dtype=np.float32) * np.exp2(rng.integers(-2, 3, shape[:-1] + (1,)))).astype(BF)
def wide(rng, *shape):
    v = f(rng, *shape).astype(np.float32); k = shape[:-2] + (1, shape[-1])
    return (v * np.exp2(rng.integers(-6, 7, k)) * (rng.random(k) > 0.0625)).astype(BF)
M, Q, V, TOP = 512, 256, 6, 15
def far_maps(rng):
    p = np.argsort(rng.random((N, 8, M)), axis=-1)
    return np.where(rng.random(p.shape) < 0.125, rng.integers(0, M, p.shape), p).astype(np.int32)
def lists(a):
    return np.stack([gtable(u) for u in a])
def setup_inputs(rng):
    return {"nx": far_maps(rng), "v": f(rng, N, 128, M), "x": lists(rng.integers(0, M, (N, 8, Q))), "e": lists(rng.integers(0, TOP + 1, (N, 8, V * Q)))}
def setup_inputs_ends(rng):
    d = setup_inputs(rng); k = rng.choice(np.array([0, TOP]), (N, 8, V, Q))
    k[:, :, :, 0] = 0; k[:, :, :, 1] = TOP; k[:, :, :, Q - 1] = 0; k[:, :, V - 1, Q - 1] = TOP
    d["e"] = lists(k.reshape(N, 8, V * Q))
    return d
def setup_inputs_still(rng):
    d = setup_inputs(rng); a = np.array(d["nx"]); s = int(rng.integers(0, 4)); p = np.arange(M)
    for r in range(N):
        h = (r + s) % 4; c = rng.choice(np.arange(2, M - 1), 8, replace=False)
        if h == 0:
            a[r] = p
        elif h == 1:
            c[0] = 0; c[1] = M - 1; a[r] = rng.permutation(c)[:, None]
        elif h == 2:
            c[0] = 1; c[1] = M - 1; a[r] = (p + rng.permutation(c)[:, None]) % M
        else:
            c[0] = 1; c[1] = M - 1; a[r] = p ^ rng.permutation(c)[:, None]
    d["nx"] = a; return d
def setup_inputs_alike(rng):
    d = setup_inputs(rng); k = rng.integers(0, TOP + 1, (N, 8, V, Q // 2))
    z = np.where((np.arange(N)[:, None] + np.arange(8)) % 2 == 0, M - 1, 0)
    d["x"] = lists(np.repeat(z[:, :, None], Q, axis=2)); d["e"] = lists(np.concatenate([k, k], -1).reshape(N, 8, V * Q)); return d
def setup_inputs_spread(rng):
    d = setup_inputs(rng)
    d["nx"] = np.floor(M * rng.random((N, 8, M)) ** 3).astype(np.int32)
    d["v"] = wide(rng, N, 128, M)
    d["x"] = lists(np.floor(M * rng.random((N, 8, Q)) ** 2)); d["e"] = lists(np.floor((TOP + 1) * rng.random((N, 8, V * Q)) ** 3)); return d
def check_inputs(d):
    bad = []
    for name, top in (("nx", M - 1), ("x", M - 1), ("e", TOP)):
        if np.min(d[name]) < 0 or np.max(d[name]) > top: bad.append("range of " + name)
    if not np.isfinite(d["v"].astype(np.float32)).all(): bad.append("finite v")
    return bad
def reference(nx, v, x, e):
    y = np.zeros((N, 128, Q), np.float32); g = np.arange(8)[:, None]; g3 = np.arange(8)[:, None, None]; i3 = np.arange(16)[None, :, None]
    for r in range(N):
        p = gentries(x[r]).astype(np.int64); k = gentries(e[r]).reshape(8, V, Q); s = np.zeros((8, 16, Q), np.float64)
        for t in range(V):
            q = (r + t) % N; vq = v[q].astype(np.float64).reshape(8, 16, M)
            for i in range(TOP):
                go = i < k[:, t]
                s = s + np.where(go[:, None, :], vq[g3, i3, p[:, None, :]], 0.0)
                p = np.where(go, nx[q][g, p], p)
        y[r] = s.reshape(128, Q).astype(np.float32)
    return {"y": y}

@@ -1,0 +1,397 @@
+import numpy as np
+from concourse.bass import DstId, RemoteDMATransfer
+from concourse.mybir import dt, AluOpType, AxisListType, ActivationFunctionType
+
+NR = 6
+NPOOL = 110
+BF, F32, I32, U16 = "bfloat16", "float32", "int32", "uint16"
+SCRATCH = {}
+for _n, _c, _d in (("nx16", 256, I32), ("nxb", 256, BF), ("nxl", 32, I32), ("nxt", 32, I32), ("e128", 96, I32), ("ebf", 96, BF),
+                   ("e16b", 768, BF), ("x128", 16, I32), ("vbf", 512, BF), ("ones", 256, BF), ("c256", 64, BF), ("o15", 256, BF),
+                   ("G16", 256, BF), ("Gb", 256, BF), ("ID1", 128, BF), ("idr", 512, BF),
+                   ("CV", 144, BF), ("C7", 144, BF), ("L4", 128, BF), ("bV", 64, BF), ("IDN", 128, BF), ("IDF", 128, F32),
+                   ("D4", 64, F32), ("pc", 2, I32), ("ci", 2, I32), ("bt", 4, I32),
+                   ("icol", 1, F32), ("n15", 1, F32), ("acol", 4, F32), ("bcol", 4, F32), ("EL", 96, I32), ("ea", 96, I32),
+                   ("E1", 96, F32), ("E2", 96, F32), ("QL", 384, F32), ("xf1", 96, F32), ("xi1", 96, U16), ("xf2", 96, F32),
+                   ("xi2", 96, U16), ("W", 512, BF), ("mask", 1280, BF), ("TT", 9728, F32), ("P4", 512, F32), ("yb", 256, F32)):
+    SCRATCH[_n] = ("sbuf", [128, _c], _d)
+for _n in range(6):
+    for _b, _c, _d, _k in (("A", 512, BF, (0, 1, 2, 3)), ("B", 512, BF, (0, 1, 2, 3)), ("U", 512, BF, (1, 2, 3)),
+                           ("vs", 512, BF, (1, 2, 3)), ("scl", 128, F32, (1, 2, 3)), ("lst", 32, U16, (0, 1, 2, 3)),
+                           ("Wl", 512, BF, (1, 2, 3, 4)), ("r1_", 256, F32, range(6)), ("rr", 256, F32, range(6)),
+                           ("pl", 16, U16, range(5)), ("R", 256, BF, range(5)), ("scv", 64, F32, range(1, 6)),
+                           ("rl", 256, F32, range(1, 6))):
+        if _n in _k:
+            SCRATCH["%s%d" % (_b, _n)] = ("sbuf", [128, _c], _d)
+for _n in ("psL0", "psL1", "psL2", "psL3", "psE0", "psE1", "psE2", "psT"):
+    SCRATCH[_n] = ("psum", [128, 512], F32)
+
+SEMAPHORES = (["s%d" % k for k in range(NPOOL)] + ["loc", "earr"] + ["w%d" % k for k in range(1, 5)]
+              + ["rq%d" % k for k in range(1, 6)] + ["rs%d" % k for k in range(1, 6)])
+
+
+def rank_program(g, core, T, topo):
+    rank = T.rank_of(core)
+    if rank is None:
+        return
+    queues = {"g": g, "v": g.vector, "s": g.scalar, "t": g.tensor, "y": g.sync}
+    ops = []
+    Op, AF = AluOpType, ActivationFunctionType
+
+    def add(q, calls, deps=(), rem=(), step=1):
+        if not isinstance(calls, list):
+            calls = [calls]
+        ops.append((q, calls, list(deps), list(rem), step))
+        return len(ops) - 1
+
+    V, S, P, Y = g.vector, g.scalar, g.tensor, g.sync
+
+    def vec(fn, *deps, rem=()):
+        return add("v", fn, deps, rem)
+
+    def sca(fn, *deps, rem=()):
+        return add("s", fn, deps, rem)
+
+    def pe(fns, *deps):
+        return add("t", fns, deps)
+
+    def gp(fn, *deps):
+        return add("g", fn, deps)
+
+    def slot(k):
+        return T.TT[:, 512 * k:512 * k + 512]
+
+    def pt(e):
+        return slot(3 + e)
+
+    d_nx = add("y", lambda: Y.dma_start(T.nx16[0:16, :], T.nx[:, :]), step=16)
+    d_l = [add("s", lambda: S.dma_start(T.nxl[:, 0:16], T.nx[0::2, :]), step=16),
+           add("y", lambda: Y.dma_start(T.nxl[:, 16:32], T.nx[1::2, :]), step=16)]
+    d_e = add("s", lambda: S.dma_start(T.e128[:, :], T.e[:, :]), step=16)
+    d_v = add("s", lambda: S.dma_start(T.vbf[:, :], T.v[:, :]), step=16)
+    d_e0 = add("y", lambda: Y.dma_start(T.EL[:, 0:16], T.e[:, 0:16]), step=16)
+    d_x = add("y", lambda: Y.dma_start(T.x128[:, :], T.x[:, :]), step=16)
+
+    k_pc = gp(lambda: g.iota(T.pc[:, :], [[1, 2]], 0, 1))
+    m_o = vec(lambda: V.memset(T.o15[0:16, :], 1.0))
+    m_o = vec(lambda: V.memset(T.o15[0:16, 15::16], 0.0), m_o)
+    k_Gb = gp(lambda: g.affine_select(T.Gb[0:16, :], T.o15[0:16, :], [[-1, 2], [-2, 8], [0, 16]], Op.is_equal, 0.0, 0, 1), m_o)
+    s_id = sca(lambda: S.activation(T.ID1[0:1, :], T.o15[0:1, 0:128], AF.Copy, bias=1.0, scale=-1.0), m_o)
+    m1 = vec(lambda: V.memset(T.ones[:, :], 1.0))
+    v_ci = vec(lambda: V.tensor_scalar(T.ci[:, :], T.pc[:, :], 15, None, Op.bitwise_and), k_pc)
+    v_bt = [vec(lambda n=n: V.tensor_scalar(T.bt[:, n:n + 1], T.pc[:, 0:1], n, 1, Op.logical_shift_right, Op.bitwise_and), k_pc)
+            for n in range(2)]
+    v_n15 = vec(lambda: V.tensor_scalar(T.n15[:, :], T.ci[:, 1:2], 1.0, None, Op.is_ge), v_ci)
+    v_r0 = vec(lambda: V.tensor_tensor_scan(T.idr[0:1, 0:256], T.ones[0:1, :], T.ones[0:1, :], -257.0, Op.mult, Op.add), m1)
+    v_bt += [vec(lambda n=n: V.tensor_scalar(T.bt[:, n:n + 1], T.pc[:, 0:1], n, 1, Op.logical_shift_right, Op.bitwise_and), k_pc)
+             for n in range(2, 4)]
+    v_ac = vec(lambda: V.tensor_scalar(T.acol[:, :], T.bt[:, :], T.n15[:, 0:1], None, Op.mult), v_n15, *v_bt)
+    s_c256 = sca(lambda: S.activation(T.c256[0:4, :], T.ones[0:4, 0:64], AF.Copy, bias=256.0, scale=0.0), m1)
+    s_D4 = sca(lambda: S.activation(T.D4[:, :], T.ones[:, 0:64], AF.Copy), m1)
+    s_c7 = sca(lambda: S.activation(T.C7[:, :], T.ones[:, 0:144], AF.Copy, scale=0.0), m1)
+    s_D4 = sca(lambda: S.activation(T.D4[:, 0::4], T.ones[:, 0:16], AF.Copy, scale=0.0), s_D4)
+    s_r1 = sca(lambda: S.activation(T.idr[0:1, 256:512], T.idr[0:1, 0:256], AF.Copy, bias=256.0), v_r0)
+    s_G = sca(lambda: S.activation(T.G16[0:16, :], T.Gb[0:16, :], AF.Copy), k_Gb)
+    v_bc = sca(lambda: S.activation(T.bcol[:, :], T.acol[:, :], AF.Copy, bias=1.0, scale=-1.0), v_ac)
+    k_I = gp(lambda: g.affine_select(T.IDN[:, :], T.ones[:, 0:128], [[-1, 128]], Op.is_equal, 0.0, 0, 1), m1)
+    k_L4 = gp(lambda: g.affine_select(T.L4[0:4, :], T.ones[0:4, 0:128], [[0, 8], [-1, 4], [0, 4]], Op.is_equal, 0.0, 0, 1), m1)
+    k_bV = gp(lambda: g.affine_select(T.bV[0:4, :], T.c256[0:4, :], [[0, 16], [-1, 4]], Op.is_equal, -2048.0, 0, 1), s_c256)
+    s_c7 = [sca(lambda q=q: S.activation(T.C7[:, 4 * q + 3:128:16], T.IDN[:, 7::16], AF.Copy), k_I, s_c7) for q in range(4)]
+    s_G = sca(lambda: S.activation(T.G16[0:16, 15::16], T.Gb[0:16, 14::16], AF.Copy), s_G)
+
+    c7s = [T.C7[:, 3 - s:131 - s] for s in range(4)]
+    cvs = [T.CV[:, 3 - s:131 - s] for s in range(4)]
+
+    def bias(k, *deps):
+        b = T["psL%d" % k]
+        pe([lambda: P.matmul(b[:, 0:64], T.L4[0:4, :], T.bV[0:4, :], start=True, stop=False)], *deps)
+
+    def extract(k, rows, cls, *deps):
+        b = T["psL%d" % k]
+        return pe([lambda s=s: P.matmul(b[:, 0:64], cls[s], rows[:, s::4], start=False, stop=(s == 3)) for s in range(4)], *deps)
+
+    def scan(out, k, *deps):
+        return vec(lambda: V.tensor_tensor_scan(out, T.D4[:, :], T["psL%d" % k][:, 0:64], 0.0, Op.mult, Op.max), *deps)
+
+    v_nx = vec(lambda: V.tensor_scalar(T.nxb[0:16, :], T.nx16[0:16, :], -256.0, None, Op.add), d_nx)
+    for h in (0, 1):
+        pe([lambda h=h: P.matmul(T["psE%d" % h][:, 0:256], T.ID1[0:1, :], T.idr[0:1, 256 * h:256 * h + 256], start=True, stop=False)],
+           s_id, v_r0, *([s_r1] if h else []))
+    t_0 = [pe([lambda h=h: P.matmul(T["psE%d" % h][:, 0:256], T.Gb[0:16, 128 * h:128 * h + 128], T.nxb[0:16, :], start=False, stop=True)],
+              v_nx, k_Gb) for h in (0, 1)]
+    v_eb = vec(lambda: V.tensor_copy(T.ebf[:, :], T.e128[:, :]), d_e)
+    d_8 = add("y", lambda: Y.dma_start(T.e16b[0:16, :], T.ebf[:, :]), [v_eb], step=16)
+    v_tr = vec(lambda: V.transpose(T.nxt[:, :], T.nxl[:, :]), *d_l)
+    s_A0 = sca(lambda: S.activation(T.A0[:, 0:256], T.psE0[:, 0:256], AF.Copy, scale=T.acol[:, 0:1]), t_0[0], v_ac)
+    v_l0 = vec(lambda: V.tensor_copy(T.lst0[:, :], T.nxt[:, :]), v_tr)
+    v_A0 = vec(lambda: V.tensor_scalar(T.A0[:, 256:512], T.psE1[:, 0:256], T.acol[:, 0:1], None, Op.mult), t_0[1], v_ac)
+    v_B0 = vec(lambda: V.tensor_scalar(T.B0[:, 0:256], T.psE0[:, 0:256], T.bcol[:, 0:1], None, Op.mult), s_A0, v_bc)
+    s_B0 = sca(lambda: S.activation(T.B0[:, 256:512], T.psE1[:, 0:256], AF.Copy, scale=T.bcol[:, 0:1]), v_A0, v_bc)
+
+    loc = [0]
+
+    def eng(d):
+        return len(topo.engines(core, d))
+
+    n_arr = eng([c for c in T.cores if c != core][0])
+
+    def send(dst_rank, out, in_, sem, deps):
+        d = T.cores[dst_rank]
+        rid, pid, _ = topo.addr(d)
+        loc[0] += eng(d)
+        add("g", lambda: g.remote_dma(out, in_, T.sem[sem], T.sem.loc, pid, rid, topo.mask(core, d)), deps, step=0)
+
+    parts, es = [], topo.engines(core, [c for c in T.cores if c != core][0])
+    for t in range(1, NR):
+        d, n = T.cores[(rank + t) % NR], len(es) // (4 if t < 4 else 8)
+        o = sum(p[1] for p in parts)
+        parts.append((RemoteDMATransfer(dst_ids=[DstId(rid=topo.addr(d)[0], pnc=topo.addr(d)[1])],
+                                        dma_engine_mask=sum(1 << x for x in es[o:o + n]), remote_sem=T.sem["earr"],
+                                        srcs=[T.e128[:, 16 * t:16 * t + 16]], dsts=[T.EL[:, 16 * t:16 * t + 16]]), n))
+    loc[0] += n_arr
+    add("g", lambda: g.remote_dma_fused([p[0] for p in parts], local_sem=T.sem.loc), [d_e], step=0)
+    z_h = []
+
+    def zero(a):
+        z_h.append(gp(lambda: g.iota(pt(4 * a), [[0, 512]], 0, 0, allow_small_or_imprecise_dtypes=True)))
+
+    zero(0)
+
+    s_v1 = sca(lambda: S.activation(T.vs1[:, :], T.vbf[:, :].indirect(T.lst0[:, :]), AF.Copy), v_l0, d_v)
+    vs = [T.vbf, T.vs1, T.vs2, T.vs3]
+
+    def plus(k, i, *deps):
+        return pe([lambda: P.matmul(T.psT[:, :], T.IDN[:, :], vs[i][:, :], start=(i == 0), stop=(i == k - 1))], *deps)
+
+    bias(0, k_L4, k_bV)
+    bias(1)
+    plus(2, 0, k_I, d_v)
+    t_cv = pe([lambda: P.matmul(T.psL3[:, 0:128], T.G16[0:16, 0:128], T.G16[0:16, 0:128], start=True, stop=True)], s_G)
+    l_h = [v_l0]
+    a_h, b_h = [s_A0, v_A0], [v_B0, s_B0]
+    e_h = []
+
+    def e_block(u, lo, hi, *deps):
+        ps, w = T["psE%d" % u], 32 if u < 2 else 16
+        e_h.append(pe([lambda i=i: P.matmul(ps[:, i:16 * w:16], T.G16[0:16, 128 * (i // 8):128 * (i // 8) + 128],
+                                            T.e16b[0:16, 96 * (i % 8) + 32 * u:96 * (i % 8) + 32 * u + w], start=True, stop=True)
+                       for i in range(lo, hi)], d_8, s_G, s_B0, v_B0, *deps))
+
+    for n in range(4):
+        A, B, L = T["A%d" % n], T["B%d" % n], T["lst%d" % n]
+        U = T["U%d" % (n + 1)] if n < 3 else T.W
+        k = 2 * (n % 2)
+        u_h = [vec(lambda A=A, B=B, U=U, L=L, h=h: V.tensor_tensor(U[:, 256 * h:256 * h + 256],
+                                                                  A[:, :].indirect(L[:, 16 * h:16 * h + 16]),
+                                                                  B[:, 256 * h:256 * h + 256], Op.add),
+                   *a_h, b_h[h], l_h[n]) for h in (0, 1)]
+        if n == 3:
+            break
+        A1, B1 = T["A%d" % (n + 1)], T["B%d" % (n + 1)]
+        x_ = [extract(k + h, U[:, 256 * h:256 * h + 256], c7s, u_h[h], *s_c7) for h in (0, 1)]
+        b_h = [sca(lambda U=U, B1=B1, n=n, h=h: S.activation(B1[:, 256 * h:256 * h + 256], U[:, 256 * h:256 * h + 256], AF.Copy,
+                                                            scale=T.bcol[:, n + 1:n + 2]), u_h[h], v_bc) for h in (0, 1)]
+        scb = T["scl%d" % (n + 1)]
+        sc = [scan(scb[:, 0:64], k, x_[0], s_D4)]
+        a_h = [vec(lambda U=U, A1=A1, n=n: V.tensor_scalar(A1[:, :], U[:, :], T.acol[:, n + 1:n + 2], None, Op.mult), *u_h, v_ac)]
+        sc.append(scan(scb[:, 64:128], k + 1, x_[1]))
+        l_h.append(vec(lambda n=n, scb=scb: V.tensor_copy(T["lst%d" % (n + 1)][:, :], scb[:, 3::4]), *sc))
+        if n == 0:
+            k_cv = sca(lambda: S.activation(T.CV[:, :], T.C7[:, :], AF.Copy, scale=0.0), *s_c7)
+            k_cv = sca(lambda: S.activation(T.CV[:, 3:128:4], T.psL3[:, 3:128:4], AF.Copy), k_cv, t_cv)
+            bias(2)
+            t_P = plus(2, 1, s_v1)
+            s_P2 = sca(lambda: S.activation(pt(2), T.psT[:, :], AF.Copy), t_P)
+            y_P3 = add("y", lambda: Y.dma_start(pt(3), pt(2)), [s_P2], step=16)
+            bias(3, k_cv)
+            e_block(0, 0, 4)
+        if n == 1:
+            bias(0)
+            bias(1)
+            s_v2 = sca(lambda: S.activation(T.vs2[:, :], T.vbf[:, :].indirect(T.lst1[:, :]), AF.Copy), l_h[1])
+            e_block(0, 4, 12)
+        if n == 2:
+            bias(2)
+            bias(3)
+            s_v3 = sca(lambda: S.activation(T.vs3[:, :], T.vs1[:, :].indirect(T.lst1[:, :]), AF.Copy), l_h[1])
+            e_block(0, 12, 16)
+            e_block(1, 0, 16)
+            plus(4, 0, s_P2)
+    w_h = u_h
+    for t in (1, 2, 3, 4):
+        send((rank - t) % NR, T["Wl%d" % t][:, :], T.W[:, :], "w%d" % t, w_h)
+
+    pt_h = {2: s_P2}
+    pt_h[3] = add("g", lambda: g.dma_start(pt(3), T.vs2[:, :], accum_op=Op.add), [y_P3, s_v2], step=16)
+    zero(1)
+    q_h = {}
+
+    def move(e, frm, m):
+        L = T["lst%d" % m]
+        src, d = (T.vbf[:, :], d_v) if frm == 1 else (pt(frm), pt_h[frm])
+        pt_h[e] = sca(lambda: S.activation(pt(e), src.indirect(L[:, :]), AF.Copy), d, l_h[m])
+
+    def build_add(e, m, plus_e, h):
+        L, o, i = T["lst%d" % m], 512 * (3 - e // 4) + 256 * h, 512 * (3 - plus_e // 4) + 256 * h
+        q_h[e, h] = vec(lambda: V.tensor_tensor(T.TT[:, o:o + 256], T.P4[:, :].indirect(L[:, 16 * h:16 * h + 16]), T.TT[:, i:i + 256],
+                                                Op.add), *([s_P4, d_P4] if plus_e == 4 else [q_h[plus_e, h], d_P4]), l_h[m])
+
+    msk = {}
+
+    def mask(t, *deps):
+        msk[t] = vec(lambda: V.tensor_scalar(T.mask[:, 256 * t:256 * t + 256], T["psE%d" % (t // 2)][:, 256 * (t % 2):256 * (t % 2) + 256],
+                                             T.icol[:, 0:1], None, Op.is_equal), *deps)
+
+    v_ic = vec(lambda: V.tensor_copy(T.icol[:, :], T.ci[:, 1:2]), v_ci)
+    v_x = vec(lambda: V.tensor_copy(T.pl0[:, :], T.x128[:, :]), d_x)
+    mask(0, e_h[2], v_ic)
+    x_h, E_h = {}, []
+
+    def expo():
+        a = vec(lambda: V.tensor_scalar(T.ea[:, :], T.EL[:, :], 2, None, Op.logical_shift_right), d_e0, rem=[("earr", n_arr)])
+        i1 = vec(lambda: V.tensor_scalar(T.E1[:, :], T.EL[:, :], 512.0, None, Op.mult), d_e0)
+        E_h.extend([i1, vec(lambda: V.tensor_scalar(T.E2[:, :], T.ea[:, :], -512.0, 1536.0, Op.mult, Op.add), a)])
+        E_h.append(vec(lambda: V.tensor_copy(T.QL[:, 3:64:4], T.x128[:, :]), d_x))
+
+    def index(lo, hi):
+        c = slice(16 * lo, 16 * hi + 16)
+        src, rem = T.QL[:, 64 * lo + 3:64 * hi + 64:4], [("rq%d" % t, n_arr) for t in range(max(lo, 1), hi + 1)]
+        i1 = vec(lambda: V.tensor_tensor(T.xf1[:, c], src, T.E1[:, c], Op.add), *E_h, rem=rem)
+        i2 = vec(lambda: V.tensor_tensor(T.xf2[:, c], src, T.E2[:, c], Op.add))
+        x1 = vec(lambda: V.tensor_copy(T.xi1[:, c], T.xf1[:, c]), i1)
+        x2 = vec(lambda: V.tensor_copy(T.xi2[:, c], T.xf2[:, c]), i2)
+        for t in range(lo, hi + 1):
+            x_h[t] = [x1, x2]
+
+    r_1, r_2 = {}, {}
+
+    def term(t, which, on):
+        w = T.TT[:, 1536:9728] if which == 1 else T.TT[:, 0:2048]
+        i = w.indirect(T["xi%d" % which][:, 16 * t:16 * t + 16])
+        deps = [x_h[t][which - 1]] + ([z_h[0], s_P4] + [q_h[e, h] for e in (8, 12) for h in (0, 1)] if which == 2 else
+                                      [*z_h, *pt_h.values()])
+        r, o = T["r1_%d" % t], T["rr%d" % t]
+        if t not in r_1:
+            r_1[t] = (sca(lambda: S.activation(r[:, :], i, AF.Copy), *deps) if on == "s" else
+                      vec(lambda: V.tensor_copy(r[:, :], i), *deps))
+        else:
+            r_2[t] = (sca(lambda: S.activation(o[:, :], i, AF.Copy), *deps) if on == "s" else
+                      vec(lambda: V.tensor_tensor(o[:, :], i, r[:, :], Op.add), r_1[t], *deps))
+            if t:
+                send((rank - t) % NR, T["rl%d" % t][:, :], o[:, :], "rs%d" % t, [r_2[t]])
+
+    p_h = {0: v_x}
+    for t in range(5):
+        Wt = T.W if t == 0 else T["Wl%d" % t]
+        R, pl, k = T["R%d" % t], T["pl%d" % t], (2 + t) % 4
+        r_h = vec(lambda R=R, Wt=Wt, pl=pl, t=t: V.tensor_tensor(R[:, :], Wt[:, :].indirect(pl[:, :]), T.mask[:, 256 * t:256 * t + 256],
+                                                                  Op.mult),
+                  *w_h, p_h[t], msk[t], rem=[("w%d" % t, n_arr)] if t else [])
+        tl = extract(k, R, cvs, r_h, k_cv)
+        if t in (0, 1, 2):
+            bias((4 + t) % 4)
+        if t == 0:
+            plus(4, 1)
+            plus(4, 2, s_v2)
+            t_P = plus(4, 3, s_v3)
+            for e, frm, m in ((5, 1, 2), (6, 2, 2), (9, 1, 3)):
+                move(e, frm, m)
+            s_P4 = sca(lambda: S.activation(slot(2), T.psT[:, :], AF.Copy), t_P)
+            d_P4 = add("y", lambda: Y.dma_start(T.P4[:, :], slot(2)), [s_P4], step=16)
+            for e, frm, m in ((13, 5, 3), (10, 2, 3), (14, 6, 3)):
+                move(e, frm, m)
+            pt_h[1] = sca(lambda: S.activation(pt(1), T.vbf[:, :], AF.Copy), d_v)
+            for e, frm, m in ((7, 3, 2), (11, 3, 3), (15, 7, 3)):
+                move(e, frm, m)
+            mask(1, e_h[3])
+        elif t == 1:
+            e_block(2, 0, 8)
+            mask(3, e_h[3])
+        elif t == 2:
+            e_block(2, 8, 16)
+            expo()
+        elif t == 3:
+            mask(4, e_h[5])
+        else:
+            build_add(8, 2, 4, 0)
+        scb = T["scv%d" % (t + 1)]
+        sc = scan(scb[:, :], k, tl, s_D4)
+        if t < 4:
+            p_h[t + 1] = vec(lambda t=t, scb=scb: V.tensor_copy(T["pl%d" % (t + 1)][:, :], scb[:, 3::4]), sc)
+        send((rank + t + 1) % NR, T.QL[:, 64 * (t + 1):64 * (t + 2)], scb[:, :], "rq%d" % (t + 1), [sc])
+        if t < 2:
+            zero(t + 2)
+        if t == 0:
+            mask(2, e_h[3])
+
+    index(0, 3)
+    term(1, 1, "s")
+    build_add(8, 2, 4, 1)
+    build_add(12, 3, 8, 0)
+    term(2, 1, "s")
+    term(0, 1, "s")
+    build_add(12, 3, 8, 1)
+    v_If = vec(lambda: V.tensor_copy(T.IDF[:, :], T.IDN[:, :]), k_I)
+    term(3, 1, "s")
+    term(1, 2, "v")
+    index(4, 5)
+    term(2, 2, "v")
+    term(4, 1, "s")
+    term(5, 1, "s")
+    term(3, 2, "v")
+    term(4, 2, "v")
+    term(5, 2, "v")
+    term(0, 2, "s")
+    acc = pe([lambda: P.matmul(T.psE0[:, 0:256], T.IDF[:, :], T.r1_0[:, :], start=True, stop=False)], r_1[0], v_If)
+    acc = pe([lambda: P.matmul(T.psE0[:, 0:256], T.IDF[:, :], T.rr0[:, :], start=False, stop=True)], r_2[0])
+    for t in (1, 2, 3, 4, 5):
+        o = T.psE0[:, 0:256] if t != 5 else T.yb[:, :]
+        acc = vec(lambda o=o, t=t: V.tensor_tensor(o, T.psE0[:, 0:256], T["rl%d" % t][:, :], Op.add), acc, rem=[("rs%d" % t, n_arr)])
+    d_y = add("y", lambda: Y.dma_start(T.y[:, :], T.yb[:, :]), [acc], step=16)
+    add("y", [], [d_y])
+
+    known = {q: set() for q in queues}
+    seen_rem = {q: set() for q in queues}
+    waits, at_issue = [], []
+    for k, (q, calls, deps, rem, step) in enumerate(ops):
+        w = []
+        for d in deps:
+            if d not in known[q]:
+                w.append(d)
+                known[q] |= at_issue[d]
+                known[q].add(d)
+        w = [d for d in w if not any(d in at_issue[o] for o in w if o != d)]
+        waits.append(w)
+        at_issue.append(set(known[q]))
+    wanted = set(d for w in waits for d in w)
+    count, last, sem_of, owner = {}, {}, {}, {}
+    free = list(range(NPOOL))
+    for k, (q, calls, deps, rem, step) in enumerate(ops):
+        eq = queues[q]
+        for d in waits[k]:
+            eq.wait_ge(T.sem["s%d" % sem_of[d][0]], sem_of[d][1])
+        for name, val in rem:
+            if name not in seen_rem[q]:
+                eq.wait_ge(T.sem[name], val)
+                seen_rem[q].add(name)
+        if k in wanted:
+            s = None
+            if step == 1:
+                for c in owner.get(q, []):
+                    if last[c] in at_issue[k]:
+                        s = c
+                        break
+            if s is None:
+                s = free.pop(0)
+                count[s] = 0
+                if step == 1:
+                    owner.setdefault(q, []).append(s)
+            for fn in calls:
+                fn().then_inc(T.sem["s%d" % s], step)
+                count[s] += step
+            last[s] = k
+            sem_of[k] = (s, count[s])
+        else:
+            for fn in calls:
+                fn()
+    g.wait_ge(T.sem.loc, loc[0])

@@ -2,354 +2,353 @@ import numpy as np
 from concourse.bass import DstId, RemoteDMATransfer
 from concourse.mybir import dt, AluOpType, AxisListType, ActivationFunctionType
 
+OPT = dict(
+    LV="g0 l1p g1 A0 s0 A1 l0 s1",
+    VO="ea R0 EE e5 P8a s0 xf p0 P8b  R1 b0 c0 X X0 s1 b1 p1 c1  R2 X1 P12a P12b s2 b2 p2 c2  R3 X2 s3 b3 p3 c3  "
+       "R4 X3 a1 s4 b4 p4 c4 X4 a2 a3  R5 a4 b5 X5 a5",
+    SO="m0 k4 M8 m1 m2 M12 m3 k2 m4 k3 m5 b1 b2 b0 a0 b3 b4 b5",
+    G="a1 a2 a3 p5 a4 r1 r2 r3 r4 r5",
+    PT={4: "ra0 rb0", 5: "rl1 rl2"}, LT="345")
 NR = 6
-NPOOL = 110
+NPOOL = 120
+ZB = 16
+WIN = ZB + 3 * 512
+FR = 4096.0
 BF, F32, I32, U16 = "bfloat16", "float32", "int32", "uint16"
 SCRATCH = {}
-for _n, _c, _d in (("nx16", 256, I32), ("nxb", 256, BF), ("nxl", 32, I32), ("nxt", 32, I32), ("e128", 96, I32), ("ebf", 96, BF),
-                   ("e16b", 768, BF), ("x128", 16, I32), ("vbf", 512, BF), ("ones", 256, BF), ("c256", 64, BF), ("o15", 256, BF),
-                   ("G16", 256, BF), ("Gb", 256, BF), ("ID1", 128, BF), ("idr", 512, BF),
-                   ("CV", 144, BF), ("C7", 144, BF), ("L4", 128, BF), ("bV", 64, BF), ("IDN", 128, BF), ("IDF", 128, F32),
-                   ("D4", 64, F32), ("pc", 2, I32), ("ci", 2, I32), ("bt", 4, I32),
-                   ("icol", 1, F32), ("n15", 1, F32), ("acol", 4, F32), ("bcol", 4, F32), ("EL", 96, I32), ("ea", 96, I32),
-                   ("E1", 96, F32), ("E2", 96, F32), ("QL", 384, F32), ("xf1", 96, F32), ("xi1", 96, U16), ("xf2", 96, F32),
-                   ("xi2", 96, U16), ("W", 512, BF), ("mask", 1280, BF), ("TT", 9728, F32), ("P4", 512, F32), ("yb", 256, F32)):
+for _n, _c, _d in (("nx16", 256, I32), ("nxb", 256, BF), ("nxl", 32, I32), ("nxt", 32, I32), ("ex", 128, I32), ("eu", 128, U16),
+                   ("pr", 16, U16), ("xf0", 16, F32), ("vbf", 512, BF), ("ones", 256, BF), ("c256", 64, BF),
+                   ("odd", 256, BF), ("Gb", 256, BF), ("ID1", 128, BF), ("idr", 512, BF),
+                   ("CV", 144, BF), ("CB", 144, BF), ("CO", 144, BF), ("C7", 144, BF), ("L4", 128, BF), ("bV", 64, BF),
+                   ("IDN", 128, BF), ("IDF", 128, F32), ("D4", 64, F32), ("pc", 2, I32), ("ci", 2, I32), ("bt", 4, I32), ("c3", 1, I32),
+                   ("icol", 1, F32), ("n15", 1, F32), ("c15", 1, F32), ("setc", 1, F32), ("ocol", 1, F32), ("acol", 4, F32),
+                   ("bcol", 4, F32), ("en", 16, F32), ("m1", 16, F32), ("DM", 16, F32), ("MT", 16, BF), ("ea", 96, I32),
+                   ("EE", 96, F32), ("XU", 192, U16), ("XR", 192, U16), ("W", 512, BF), ("mask", 1536, BF),
+                   ("TT", 2 * WIN, F32), ("yb", 256, F32)):
     SCRATCH[_n] = ("sbuf", [128, _c], _d)
 for _n in range(6):
     for _b, _c, _d, _k in (("A", 512, BF, (0, 1, 2, 3)), ("B", 512, BF, (0, 1, 2, 3)), ("U", 512, BF, (1, 2, 3)),
                            ("vs", 512, BF, (1, 2, 3)), ("scl", 128, F32, (1, 2, 3)), ("lst", 32, U16, (0, 1, 2, 3)),
-                           ("Wl", 512, BF, (1, 2, 3, 4)), ("r1_", 256, F32, range(6)), ("rr", 256, F32, range(6)),
-                           ("pl", 16, U16, range(5)), ("R", 256, BF, range(5)), ("scv", 64, F32, range(1, 6)),
+                           ("Wl", 512, BF, (1, 2, 3, 4)), ("ra", 256, F32, range(6)), ("rb", 256, F32, range(6)),
+                           ("pl", 16, U16, range(1, 6)), ("R", 256, BF, range(6)), ("sa", 64, F32, range(5)), ("sb", 128, F32, range(6)),
                            ("rl", 256, F32, range(1, 6))):
         if _n in _k:
             SCRATCH["%s%d" % (_b, _n)] = ("sbuf", [128, _c], _d)
 for _n in ("psL0", "psL1", "psL2", "psL3", "psE0", "psE1", "psE2", "psT"):
     SCRATCH[_n] = ("psum", [128, 512], F32)
 
-SEMAPHORES = (["s%d" % k for k in range(NPOOL)] + ["loc", "earr"] + ["w%d" % k for k in range(1, 5)]
-              + ["rq%d" % k for k in range(1, 6)] + ["rs%d" % k for k in range(1, 6)])
+SEMAPHORES = (["s%d" % k for k in range(NPOOL)] + ["loc", "e5", "p5", "w1a"] + ["w%d" % k for k in range(1, 5)]
+              + ["rp%d" % k for k in range(1, 5)] + ["rq%d" % k for k in range(1, 6)] + ["rs%d" % k for k in range(1, 6)])
 
 
 def rank_program(g, core, T, topo):
     rank = T.rank_of(core)
     if rank is None:
         return
-    queues = {"g": g, "v": g.vector, "s": g.scalar, "t": g.tensor, "y": g.sync}
-    ops = []
-    Op, AF = AluOpType, ActivationFunctionType
-
-    def add(q, calls, deps=(), rem=(), step=1):
-        if not isinstance(calls, list):
-            calls = [calls]
-        ops.append((q, calls, list(deps), list(rem), step))
-        return len(ops) - 1
-
     V, S, P, Y = g.vector, g.scalar, g.tensor, g.sync
+    Op, AF = AluOpType, ActivationFunctionType
+    queues = {"g": g, "v": V, "s": S, "t": P, "y": Y}
+    order = {q: [] for q in queues}
 
-    def vec(fn, *deps, rem=()):
-        return add("v", fn, deps, rem)
+    def adder(q, step=1):
+        def add(name, calls, deps="", rem=(), step=step):
+            order[q].append((name, calls if isinstance(calls, list) else [calls], deps.split(), list(rem), step))
+        return add
 
-    def sca(fn, *deps, rem=()):
-        return add("s", fn, deps, rem)
+    vec, sca, pe, gp = adder("v"), adder("s"), adder("t"), adder("g")
+    y_dma, s_dma, g_dma, g_rem = adder("y", 16), adder("s", 16), adder("g", 16), adder("g", 0)
 
-    def pe(fns, *deps):
-        return add("t", fns, deps)
+    def col(e):
+        return ZB + 512 * (e - 1) if e < 4 else WIN + ZB + 512 * (e // 4 - 1)
 
-    def gp(fn, *deps):
-        return add("g", fn, deps)
+    def pt(e, lo=0, hi=512):
+        return T.TT[:, col(e) + lo:col(e) + hi]
 
-    def slot(k):
-        return T.TT[:, 512 * k:512 * k + 512]
+    def half(t, h):
+        return t[:, 256 * h:256 * h + 256]
 
-    def pt(e):
-        return slot(3 + e)
+    es = topo.engines(core, [c for c in T.cores if c != core][0])
+    n_arr = len(es)
+    U = [None, T.U1, T.U2, T.U3, T.W]
+    vs = [T.vbf, T.vs1, T.vs2, T.vs3]
+    bank_l = ["psL%d" % (2 * (n % 2) + h) for n in range(3) for h in (0, 1)]
+    bank_a = ["psL%d" % (2 + t % 2) for t in range(5)]
+    bank_b = ["psL%d" % (t % 2) for t in range(6)]
+    bank_p = {2: "psT", 3: "psE2", 4: "psE0"}
 
-    d_nx = add("y", lambda: Y.dma_start(T.nx16[0:16, :], T.nx[:, :]), step=16)
-    d_l = [add("s", lambda: S.dma_start(T.nxl[:, 0:16], T.nx[0::2, :]), step=16),
-           add("y", lambda: Y.dma_start(T.nxl[:, 16:32], T.nx[1::2, :]), step=16)]
-    d_e = add("s", lambda: S.dma_start(T.e128[:, :], T.e[:, :]), step=16)
-    d_v = add("s", lambda: S.dma_start(T.vbf[:, :], T.v[:, :]), step=16)
-    d_e0 = add("y", lambda: Y.dma_start(T.EL[:, 0:16], T.e[:, 0:16]), step=16)
-    d_x = add("y", lambda: Y.dma_start(T.x128[:, :], T.x[:, :]), step=16)
+    def term(name):
+        which, t = name[0], int(name[1])
+        own = t == 0 or name == "a5"
+        c = 32 * t + (16 if which == "a" else 0)
+        w = T.TT[:, WIN:2 * WIN] if which == "b" else T.TT[:, 0:WIN + ZB]
+        i = w.indirect((T.XU if own else T.XR)[:, c:c + 16])
+        deps = "z1 P4 P8a P8b P12a P12b" if which == "b" else "z0 z1 P1 P2 P3"
+        deps += {"b0": " X", "a0": " X0", "a5": " X5"}.get(name, "")
+        rem = [] if own else [("r%s%d" % ("p" if which == "a" else "q", t), n_arr if name == "b1" else n_arr // 2)]
+        o = T["r" + name]
+        if which == "b" or t == 0:
+            sca("r" + name, lambda: S.activation(o[:, :], i, AF.Copy), deps, rem)
+        else:
+            vec("r" + name, lambda: V.tensor_tensor(o[:, :], i, T["rb%d" % t][:, :], Op.add), deps + " rb%d" % t, rem)
 
-    k_pc = gp(lambda: g.iota(T.pc[:, :], [[1, 2]], 0, 1))
-    m_o = vec(lambda: V.memset(T.o15[0:16, :], 1.0))
-    m_o = vec(lambda: V.memset(T.o15[0:16, 15::16], 0.0), m_o)
-    k_Gb = gp(lambda: g.affine_select(T.Gb[0:16, :], T.o15[0:16, :], [[-1, 2], [-2, 8], [0, 16]], Op.is_equal, 0.0, 0, 1), m_o)
-    s_id = sca(lambda: S.activation(T.ID1[0:1, :], T.o15[0:1, 0:128], AF.Copy, bias=1.0, scale=-1.0), m_o)
-    m1 = vec(lambda: V.memset(T.ones[:, :], 1.0))
-    v_ci = vec(lambda: V.tensor_scalar(T.ci[:, :], T.pc[:, :], 15, None, Op.bitwise_and), k_pc)
-    v_bt = [vec(lambda n=n: V.tensor_scalar(T.bt[:, n:n + 1], T.pc[:, 0:1], n, 1, Op.logical_shift_right, Op.bitwise_and), k_pc)
-            for n in range(2)]
-    v_n15 = vec(lambda: V.tensor_scalar(T.n15[:, :], T.ci[:, 1:2], 1.0, None, Op.is_ge), v_ci)
-    v_r0 = vec(lambda: V.tensor_tensor_scan(T.idr[0:1, 0:256], T.ones[0:1, :], T.ones[0:1, :], -257.0, Op.mult, Op.add), m1)
-    v_bt += [vec(lambda n=n: V.tensor_scalar(T.bt[:, n:n + 1], T.pc[:, 0:1], n, 1, Op.logical_shift_right, Op.bitwise_and), k_pc)
-             for n in range(2, 4)]
-    v_ac = vec(lambda: V.tensor_scalar(T.acol[:, :], T.bt[:, :], T.n15[:, 0:1], None, Op.mult), v_n15, *v_bt)
-    s_c256 = sca(lambda: S.activation(T.c256[0:4, :], T.ones[0:4, 0:64], AF.Copy, bias=256.0, scale=0.0), m1)
-    s_D4 = sca(lambda: S.activation(T.D4[:, :], T.ones[:, 0:64], AF.Copy), m1)
-    s_c7 = sca(lambda: S.activation(T.C7[:, :], T.ones[:, 0:144], AF.Copy, scale=0.0), m1)
-    s_D4 = sca(lambda: S.activation(T.D4[:, 0::4], T.ones[:, 0:16], AF.Copy, scale=0.0), s_D4)
-    s_r1 = sca(lambda: S.activation(T.idr[0:1, 256:512], T.idr[0:1, 0:256], AF.Copy, bias=256.0), v_r0)
-    s_G = sca(lambda: S.activation(T.G16[0:16, :], T.Gb[0:16, :], AF.Copy), k_Gb)
-    v_bc = sca(lambda: S.activation(T.bcol[:, :], T.acol[:, :], AF.Copy, bias=1.0, scale=-1.0), v_ac)
-    k_I = gp(lambda: g.affine_select(T.IDN[:, :], T.ones[:, 0:128], [[-1, 128]], Op.is_equal, 0.0, 0, 1), m1)
-    k_L4 = gp(lambda: g.affine_select(T.L4[0:4, :], T.ones[0:4, 0:128], [[0, 8], [-1, 4], [0, 4]], Op.is_equal, 0.0, 0, 1), m1)
-    k_bV = gp(lambda: g.affine_select(T.bV[0:4, :], T.c256[0:4, :], [[0, 16], [-1, 4]], Op.is_equal, -2048.0, 0, 1), s_c256)
-    s_c7 = [sca(lambda q=q: S.activation(T.C7[:, 4 * q + 3:128:16], T.IDN[:, 7::16], AF.Copy), k_I, s_c7) for q in range(4)]
-    s_G = sca(lambda: S.activation(T.G16[0:16, 15::16], T.Gb[0:16, 14::16], AF.Copy), s_G)
+    y_dma("nx16", lambda: Y.dma_start(T.nx16[0:16, :], T.nx[:, :]))
+    y_dma("e", lambda: Y.dma_start(T.ex[:, 0:96], T.e[:, :]))
+    y_dma("x", lambda: Y.dma_start(T.ex[:, 96:112], T.x[:, :]))
+    y_dma("y", lambda: Y.dma_start(T.y[:, :], T.yb[:, :]), "yb")
+    y_dma("end", [], "y")
 
-    c7s = [T.C7[:, 3 - s:131 - s] for s in range(4)]
-    cvs = [T.CV[:, 3 - s:131 - s] for s in range(4)]
+    def scan(name, out, b, deps):
+        vec(name, lambda: V.tensor_tensor_scan(out, T.D4[:, :], T[b][:, 0:64], 0.0, Op.mult, Op.max), "D4 " + deps)
 
-    def bias(k, *deps):
-        b = T["psL%d" % k]
-        pe([lambda: P.matmul(b[:, 0:64], T.L4[0:4, :], T.bV[0:4, :], start=True, stop=False)], *deps)
+    vec("odd0", lambda: V.memset(T.odd[0:16, :], 1.0))
+    vec("ones", lambda: V.memset(T.ones[:, :], 1.0))
+    vec("odd1", lambda: V.memset(T.odd[0:16, 0::2], 0.0), "odd0")
+    vec("odd2", lambda: V.memset(T.odd[0:16, 15::16], 0.0))
+    vec("idr0", lambda: V.tensor_tensor_scan(T.idr[:, 0:256], T.ones[:, :], T.ones[:, :], -257.0, Op.mult, Op.add), "ones")
+    vec("ci", lambda: V.tensor_scalar(T.ci[:, :], T.pc[:, :], 15, None, Op.bitwise_and), "pc")
+    vec("c3", lambda: V.tensor_scalar(T.c3[:, :], T.pc[:, 1:2], 3, None, Op.bitwise_and))
+    for n in range(1, 4):
+        vec("bt%d" % n, lambda n=n: V.tensor_scalar(T.bt[:, n:n + 1], T.pc[:, 0:1], n, 1, Op.logical_shift_right, Op.bitwise_and))
+    vec("setc", lambda: V.tensor_scalar(T.setc[:, :], T.c3[:, :], 0.0, FR, Op.is_equal, Op.mult), "c3")
+    vec("ocol", lambda: V.tensor_scalar(T.ocol[:, :], T.c3[:, :], 512.0, None, Op.mult))
+    vec("n15", lambda: V.tensor_scalar(T.n15[:, :], T.ci[:, 1:2], 1.0, None, Op.is_ge), "ci")
+    vec("c15", lambda: V.tensor_scalar(T.c15[:, :], T.ci[:, 1:2], 0.0, None, Op.is_equal))
+    vec("icol", lambda: V.tensor_copy(T.icol[:, :], T.ci[:, 1:2]))
+    vec("en", lambda: V.tensor_tensor_scan(T.en[:, :], T.ones[:, 0:16], T.ones[:, 0:16], -1.0, Op.mult, Op.add))
+    vec("acol", lambda: V.tensor_scalar(T.acol[:, 1:4], T.bt[:, 1:4], T.n15[:, 0:1], None, Op.mult), "n15 bt1 bt2 bt3")
+    vec("nxb", lambda: V.tensor_scalar(T.nxb[0:16, :], T.nx16[0:16, :], -256.0, None, Op.add), "nx16")
+    vec("DM0", lambda: V.tensor_scalar(T.DM[:, :], T.D4[:, 0:16], T.setc[:, 0:1], 1.0 / FR, Op.mult, Op.mult), "D4 setc")
+    vec("m1", lambda: V.tensor_scalar(T.m1[:, :], T.en[:, :], T.icol[:, 0:1], None, Op.is_equal), "en icol")
+    vec("nxt", lambda: V.transpose(T.nxt[:, :], T.nxl[:, :]), "nxl0 nxl1")
+    vec("DM", lambda: V.tensor_scalar(T.DM[:, 1::4], T.DM[:, 1::4], 1.0 / FR, None, Op.mult), "DM0")
+    vec("lst0", lambda: V.tensor_copy(T.lst0[:, :], T.nxt[:, :]), "nxt")
+    vec("MT", lambda: V.tensor_tensor_scan(T.MT[:, :], T.DM[:, :], T.m1[:, :], 0.0, Op.mult, Op.add), "DM m1")
+    vec("A0b", lambda: V.tensor_copy(half(T.A0, 1), T.psE1[:, 0:256]), "nx1")
 
-    def extract(k, rows, cls, *deps):
-        b = T["psL%d" % k]
-        return pe([lambda s=s: P.matmul(b[:, 0:64], cls[s], rows[:, s::4], start=False, stop=(s == 3)) for s in range(4)], *deps)
+    def compose(n, h):
+        A, B, L = T["A%d" % n], T["B%d" % n], T["lst%d" % n]
+        vec("U%d%d" % (n + 1, h), lambda: V.tensor_tensor(half(U[n + 1], h), A[:, :].indirect(L[:, 16 * h:16 * h + 16]), half(B, h), Op.add),
+            "A0a A0b B0 lst0" if n == 0 else "A%d0 A%d1 B%d%d lst%d%d" % (n, n, n, h, n, h))
 
-    def scan(out, k, *deps):
-        return vec(lambda: V.tensor_tensor_scan(out, T.D4[:, :], T["psL%d" % k][:, 0:64], 0.0, Op.mult, Op.max), *deps)
+    def window(m, h):
+        vec("A%d%d" % (m, h), lambda: V.tensor_scalar(half(T["A%d" % m], h), half(U[m], h), T.acol[:, m:m + 1], None, Op.mult),
+            "U%d%d acol" % (m, h))
 
-    v_nx = vec(lambda: V.tensor_scalar(T.nxb[0:16, :], T.nx16[0:16, :], -256.0, None, Op.add), d_nx)
+    def scan_l(m, h):
+        scan("scl%d%d" % (m, h), T["scl%d" % m][:, 64 * h:64 * h + 64], bank_l[2 * m - 2 + h], "xl%d%d" % (m, h))
+
+    def to_list(m, h):
+        vec("lst%d%d" % (m, h), lambda: V.tensor_copy(T["lst%d" % m][:, 16 * h:16 * h + 16], T["scl%d" % m][:, 64 * h + 3:64 * h + 64:4]),
+            "scl%d%d" % (m, h))
+
+    for n in range(4):
+        for a in OPT["LV"].split():
+            m, h = n + 1 - (a[-1] == "p"), int(a[1])
+            if a[0] == "g":
+                compose(n, h)
+            elif 0 < m < 4:
+                {"A": window, "s": scan_l, "l": to_list}[a[0]](m, h)
+        if n == 1:
+            vec("eu", lambda: V.tensor_copy(T.eu[:, 0:112], T.ex[:, 0:112]), "e x")
+
+    def visit(t):
+        Wt = T.W if t in (0, 5) else T["Wl%d" % t]
+        pl = T.pr[:, :] if t == 5 else T["pl%d" % t][:, :] if t else T.eu[:, 96:112]
+        vec("R%d" % t, lambda: V.tensor_tensor(T["R%d" % t][:, :], Wt[:, :].indirect(pl), half(T.mask, t), Op.mult),
+            "U40 U41 %s mask%d" % ("pl%d" % t if 0 < t < 5 else "eu", t),
+            [(s, n_arr) for s in {0: [], 1: ["w1a", "w1"], 5: ["p5"]}.get(t, ["w%d" % t])])
+
+    def scan_a(t):
+        scan("sa%d" % t, T["sa%d" % t][:, :], bank_a[t], "xa%d" % t)
+
+    def place(t):
+        vec("pl%d" % (t + 1), lambda: V.tensor_scalar(T["pl%d" % (t + 1)][:, :], T["sa%d" % t][:, 3::4], 0.25, None, Op.add), "sa%d" % t)
+
+    def add_a(t):
+        vec("sc%d" % t, lambda: V.tensor_tensor(T["sb%d" % t][:, 67::4], T["sa%d" % t][:, 3::4], T.EE[:, 16 * t + 16:16 * t + 32], Op.add),
+            "sa%d EE" % t)
+
+    def scan_b(t):
+        scan("sb%d" % t, T["sb%d" % t][:, 0:64], bank_b[t], "xb%d" % t)
+
+    def offsets(t):
+        sbt, c, n = T["sb%d" % t], 32 * t + 16, 128 if t < 5 else 64
+        vec("X%d" % t, lambda: V.tensor_scalar(T.XU[:, c:c + n // 4], sbt[:, 3:n:4], ZB - 511.75, float(WIN), Op.add, Op.min),
+            "sb%d" % t + (" sc%d" % t if t < 5 else ""))
+
+    def add4(e, h):
+        o = pt(e, 256 * h, 256 * h + 256)
+        vec("P%d%s" % (e, "ab"[h]), lambda: V.tensor_tensor(o, o, half(T.psE0, h), Op.add), "M%d P4" % e)
+
+    small = {
+        "ea": lambda: vec("ea", lambda: V.tensor_scalar(T.ea[:, :], T.ex[:, 0:96], 2, None, Op.logical_shift_right), "e"),
+        "EE": lambda: vec("EE", lambda: V.tensor_scalar(T.EE[:, :], T.ea[:, :], 512.0, None, Op.mult), "ea"),
+        "xf": lambda: vec("xf0", lambda: V.tensor_tensor(T.xf0[:, :], T.ex[:, 96:112], T.EE[:, 0:16], Op.add), "x EE"),
+        "X": lambda: vec("X", lambda: V.tensor_scalar(T.XU[:, 0:16], T.xf0[:, :], ZB - 511.75, None, Op.add), "xf0"),
+        "e5": lambda: vec("eu5", lambda: V.tensor_copy(T.eu[:, 112:128], T.ex[:, 112:128]), "", [("e5", n_arr)]),
+    }
+    for a in OPT["VO"].split():
+        if a in small:
+            small[a]()
+        elif a[0] == "P":
+            add4(int(a[1:-1]), "ab".index(a[-1]))
+        elif a[0] == "a":
+            term(a)
+        else:
+            {"R": visit, "s": scan_a, "p": place, "c": add_a, "b": scan_b, "X": offsets}[a[0]](int(a[1]))
+    last = "acc"
+    for t in OPT["LT"]:
+        o = T.psE1[:, 0:256] if t != "5" else T.yb[:, :]
+        name = "acc" + t if t != "5" else "yb"
+        vec(name, lambda o=o, t=t: V.tensor_tensor(o, T.psE1[:, 0:256], T["rl" + t][:, :], Op.add), last, [("rs" + t, n_arr)])
+        last = name
+
+    def act(name, out, in_, deps, **k):
+        sca(name, lambda: S.activation(out, in_, AF.Copy, **k), deps)
+
+    def mask(t):
+        c = 16 * t if t < 5 else 112
+        act("mask%d" % t, half(T.mask, t), T.MT[:, :].indirect(T.eu[:, c:c + 16]), "MT eu" if t < 5 else "MT eu5")
+
+    def keep(k):
+        act("P%d" % k, pt(k), T[bank_p[k]][:, :], "sum%d%d" % (k, k - 1))
+
+    def moved(e):
+        act("M%d" % e, pt(e), pt(e - 4).indirect(T.lst2[:, :]), "P4 lst20 lst21" if e == 8 else "P8a P8b")
+
+    s_dma("nxl0", lambda: S.dma_start(T.nxl[:, 0:16], T.nx[0::2, :]))
+    s_dma("nxl1", lambda: S.dma_start(T.nxl[:, 16:32], T.nx[1::2, :]))
+    s_dma("vs0", lambda: S.dma_start(T.vbf[:, :], T.v[:, :]))
+    act("ID10", T.ID1[0:1, :], T.ones[0:1, 0:128], "ones")
+    act("C70", T.C7[:, :], T.ones[:, 0:144], "", scale=0.0)
+    act("ID1", T.ID1[0:1, 1::2], T.ones[0:1, 0:64], "ID10", scale=0.0)
+    act("idr1", T.idr[:, 256:512], T.idr[:, 0:256], "idr0", bias=256.0)
+    act("CV0", T.CV[:, :], T.ones[:, 0:144], "", scale=0.0)
+    act("D40", T.D4[:, :], T.ones[:, 0:64], "")
+    act("c256", T.c256[0:4, :], T.ones[0:4, 0:64], "", bias=256.0, scale=0.0)
+    act("D4", T.D4[:, 0::4], T.ones[:, 0:16], "D40", scale=0.0)
+    act("z0", T.TT[:, 0:ZB], T.ones[:, 0:ZB], "", scale=0.0)
+    act("z1", T.TT[:, WIN:WIN + ZB], T.ones[:, 0:ZB], "", scale=0.0)
+    act("bcol", T.bcol[:, 1:4], T.acol[:, 1:4], "acol", bias=1.0, scale=-1.0)
+    act("B0", T.B0[:, :], T.idr[:, :], "c15 idr0 idr1", scale=T.c15[:, 0:1])
+    act("A0a", half(T.A0, 0), T.psE0[:, 0:256], "nx0")
+    for m in (1, 2, 3):
+        if m == 3:
+            act("CB", T.CB[:, :], T.CV[:, :], "CV setc", scale=T.setc[:, 0:1])
+            act("CO", T.CO[:, :], T.CV[:, :], "ocol", scale=T.ocol[:, 0:1])
+        act("vs%d" % m, vs[m][:, :], vs[m - 1][:, :].indirect(T.lst0[:, :]), "lst0 vs%d" % (m - 1))
+        for h in (0, 1):
+            act("B%d%d" % (m, h), half(T["B%d" % m], h), half(U[m], h), "U%d%d bcol" % (m, h), scale=T.bcol[:, m:m + 1])
+    for a in OPT["SO"].split():
+        if a[0] in "ab":
+            term(a)
+        else:
+            {"m": mask, "k": keep, "M": moved}[a[0]](int(a[1:]))
+
+    def bias(b, deps=""):
+        pe(None, lambda: P.matmul(T[b][:, 0:64], T.L4[0:4, :], T.bV[0:4, :], start=True, stop=False), deps)
+
+    def extract(name, b, rows, c, deps, stop=True):
+        pe(name, [lambda s=s: P.matmul(T[b][:, 0:64], c[:, 3 - s:131 - s], rows[:, s::4], start=False, stop=(stop and s == 3))
+                  for s in range(4)], deps)
+
+    def plus(k, i, deps=""):
+        pe("sum%d%d" % (k, i), lambda: P.matmul(T[bank_p[k]][:, :], T.IDN[:, :], vs[i][:, :], start=(i == 0), stop=(i == k - 1)),
+           "IDN vs%d %s" % (i, deps))
+
     for h in (0, 1):
-        pe([lambda h=h: P.matmul(T["psE%d" % h][:, 0:256], T.ID1[0:1, :], T.idr[0:1, 256 * h:256 * h + 256], start=True, stop=False)],
-           s_id, v_r0, *([s_r1] if h else []))
-    t_0 = [pe([lambda h=h: P.matmul(T["psE%d" % h][:, 0:256], T.Gb[0:16, 128 * h:128 * h + 128], T.nxb[0:16, :], start=False, stop=True)],
-              v_nx, k_Gb) for h in (0, 1)]
-    v_eb = vec(lambda: V.tensor_copy(T.ebf[:, :], T.e128[:, :]), d_e)
-    d_8 = add("y", lambda: Y.dma_start(T.e16b[0:16, :], T.ebf[:, :]), [v_eb], step=16)
-    v_tr = vec(lambda: V.transpose(T.nxt[:, :], T.nxl[:, :]), *d_l)
-    s_A0 = sca(lambda: S.activation(T.A0[:, 0:256], T.psE0[:, 0:256], AF.Copy, scale=T.acol[:, 0:1]), t_0[0], v_ac)
-    v_l0 = vec(lambda: V.tensor_copy(T.lst0[:, :], T.nxt[:, :]), v_tr)
-    v_A0 = vec(lambda: V.tensor_scalar(T.A0[:, 256:512], T.psE1[:, 0:256], T.acol[:, 0:1], None, Op.mult), t_0[1], v_ac)
-    v_B0 = vec(lambda: V.tensor_scalar(T.B0[:, 0:256], T.psE0[:, 0:256], T.bcol[:, 0:1], None, Op.mult), s_A0, v_bc)
-    s_B0 = sca(lambda: S.activation(T.B0[:, 256:512], T.psE1[:, 0:256], AF.Copy, scale=T.bcol[:, 0:1]), v_A0, v_bc)
+        pe(None, lambda h=h: P.matmul(T["psE%d" % h][:, 0:256], T.ID1[0:1, :], T.idr[0:1, 256 * h:256 * h + 256], start=True, stop=False),
+           "ID1 idr%d" % h)
+    for h in (0, 1):
+        pe("nx%d" % h, lambda h=h: P.matmul(T["psE%d" % h][:, 0:256], T.Gb[0:16, 128 * h:128 * h + 128], T.nxb[0:16, :],
+                                            start=False, stop=True), "nxb Gb")
+    plus(4, 0, "A0a")
+    for k in range(4):
+        bias("psL%d" % k, "L4 bV")
+    for n in range(3):
+        for h in (0, 1):
+            extract("xl%d%d" % (n + 1, h), bank_l[2 * n + h], half(U[n + 1], h), T.C7, "U%d%d C7" % (n + 1, h))
+        plus(4, n + 1)
+        for h in (0, 1):
+            bias(bank_l[2 * n + h], "scl%d%d" % (n + 1, h))
+    for t in range(6):
+        extract(None, bank_b[t], half(T.mask, t), T.CO, "mask%d CO" % t, stop=False)
+        if t == 0:
+            plus(2, 0)
+            plus(2, 1)
+            plus(3, 0)
+        if t < 5:
+            extract("xa%d" % t, bank_a[t], T["R%d" % t], T.CV, "R%d CV" % t)
+        extract("xb%d" % t, bank_b[t], T["R%d" % t], T.CB, "R%d CB" % t)
+        if 0 < t < 5:
+            bias(bank_b[t + 1], "sb%d" % (t - 1))
+        if t < 3:
+            bias(bank_a[t], "sa%d" % t)
+        if t == 0:
+            plus(3, 1)
+            plus(3, 2)
+        for r in OPT["PT"].get(t, "").split():
+            first, end = r == "ra0", r == OPT["PT"][5].split()[-1]
+            pe("acc" if end else None,
+               lambda r=r, first=first, end=end: P.matmul(T.psE1[:, 0:256], T.IDF[:, :], T[r][:, :], start=first, stop=end),
+               "IDF A0b" + ("" if r[1] == "l" else " " + r), [("rs" + r[2], n_arr)] if r[1] == "l" else [])
 
     loc = [0]
 
-    def eng(d):
-        return len(topo.engines(core, d))
-
-    n_arr = eng([c for c in T.cores if c != core][0])
-
     def send(dst_rank, out, in_, sem, deps):
-        d = T.cores[dst_rank]
+        d = T.cores[dst_rank % NR]
         rid, pid, _ = topo.addr(d)
-        loc[0] += eng(d)
-        add("g", lambda: g.remote_dma(out, in_, T.sem[sem], T.sem.loc, pid, rid, topo.mask(core, d)), deps, step=0)
+        loc[0] += n_arr
+        g_rem(None, lambda: g.remote_dma(out, in_, T.sem[sem], T.sem.loc, pid, rid, topo.mask(core, d)), deps)
 
-    parts, es = [], topo.engines(core, [c for c in T.cores if c != core][0])
-    for t in range(1, NR):
-        d, n = T.cores[(rank + t) % NR], len(es) // (4 if t < 4 else 8)
-        o = sum(p[1] for p in parts)
-        parts.append((RemoteDMATransfer(dst_ids=[DstId(rid=topo.addr(d)[0], pnc=topo.addr(d)[1])],
-                                        dma_engine_mask=sum(1 << x for x in es[o:o + n]), remote_sem=T.sem["earr"],
-                                        srcs=[T.e128[:, 16 * t:16 * t + 16]], dsts=[T.EL[:, 16 * t:16 * t + 16]]), n))
-    loc[0] += n_arr
-    add("g", lambda: g.remote_dma_fused([p[0] for p in parts], local_sem=T.sem.loc), [d_e], step=0)
-    z_h = []
+    def ask(t):
+        n, trs = n_arr // 2, []
+        for k in (0, 1):
+            rid, pid, _ = topo.addr(T.cores[(rank + t + k) % NR])
+            c = 32 * t + 16 + 16 * k
+            trs.append(RemoteDMATransfer(dst_ids=[DstId(rid=rid, pnc=pid)], dma_engine_mask=sum(1 << x for x in es[n * k:n * k + n]),
+                                         remote_sem=T.sem["r%s%d" % ("pq"[k], t + k)], srcs=[T.XU[:, c:c + 16]], dsts=[T.XR[:, c:c + 16]]))
+        loc[0] += n_arr
+        g_rem(None, lambda: g.remote_dma_fused(trs, local_sem=T.sem.loc), "X%d" % t)
 
-    def zero(a):
-        z_h.append(gp(lambda: g.iota(pt(4 * a), [[0, 512]], 0, 0, allow_small_or_imprecise_dtypes=True)))
+    def select(name, out, in_, pattern, op, fill, base, cm, deps):
+        gp(name, lambda: g.affine_select(out, in_, pattern, op, fill, base, cm), deps)
 
-    zero(0)
-
-    s_v1 = sca(lambda: S.activation(T.vs1[:, :], T.vbf[:, :].indirect(T.lst0[:, :]), AF.Copy), v_l0, d_v)
-    vs = [T.vbf, T.vs1, T.vs2, T.vs3]
-
-    def plus(k, i, *deps):
-        return pe([lambda: P.matmul(T.psT[:, :], T.IDN[:, :], vs[i][:, :], start=(i == 0), stop=(i == k - 1))], *deps)
-
-    bias(0, k_L4, k_bV)
-    bias(1)
-    plus(2, 0, k_I, d_v)
-    t_cv = pe([lambda: P.matmul(T.psL3[:, 0:128], T.G16[0:16, 0:128], T.G16[0:16, 0:128], start=True, stop=True)], s_G)
-    l_h = [v_l0]
-    a_h, b_h = [s_A0, v_A0], [v_B0, s_B0]
-    e_h = []
-
-    def e_block(u, lo, hi, *deps):
-        ps, w = T["psE%d" % u], 32 if u < 2 else 16
-        e_h.append(pe([lambda i=i: P.matmul(ps[:, i:16 * w:16], T.G16[0:16, 128 * (i // 8):128 * (i // 8) + 128],
-                                            T.e16b[0:16, 96 * (i % 8) + 32 * u:96 * (i % 8) + 32 * u + w], start=True, stop=True)
-                       for i in range(lo, hi)], d_8, s_G, s_B0, v_B0, *deps))
-
-    for n in range(4):
-        A, B, L = T["A%d" % n], T["B%d" % n], T["lst%d" % n]
-        U = T["U%d" % (n + 1)] if n < 3 else T.W
-        k = 2 * (n % 2)
-        u_h = [vec(lambda A=A, B=B, U=U, L=L, h=h: V.tensor_tensor(U[:, 256 * h:256 * h + 256],
-                                                                  A[:, :].indirect(L[:, 16 * h:16 * h + 16]),
-                                                                  B[:, 256 * h:256 * h + 256], Op.add),
-                   *a_h, b_h[h], l_h[n]) for h in (0, 1)]
-        if n == 3:
-            break
-        A1, B1 = T["A%d" % (n + 1)], T["B%d" % (n + 1)]
-        x_ = [extract(k + h, U[:, 256 * h:256 * h + 256], c7s, u_h[h], *s_c7) for h in (0, 1)]
-        b_h = [sca(lambda U=U, B1=B1, n=n, h=h: S.activation(B1[:, 256 * h:256 * h + 256], U[:, 256 * h:256 * h + 256], AF.Copy,
-                                                            scale=T.bcol[:, n + 1:n + 2]), u_h[h], v_bc) for h in (0, 1)]
-        scb = T["scl%d" % (n + 1)]
-        sc = [scan(scb[:, 0:64], k, x_[0], s_D4)]
-        a_h = [vec(lambda U=U, A1=A1, n=n: V.tensor_scalar(A1[:, :], U[:, :], T.acol[:, n + 1:n + 2], None, Op.mult), *u_h, v_ac)]
-        sc.append(scan(scb[:, 64:128], k + 1, x_[1]))
-        l_h.append(vec(lambda n=n, scb=scb: V.tensor_copy(T["lst%d" % (n + 1)][:, :], scb[:, 3::4]), *sc))
-        if n == 0:
-            k_cv = sca(lambda: S.activation(T.CV[:, :], T.C7[:, :], AF.Copy, scale=0.0), *s_c7)
-            k_cv = sca(lambda: S.activation(T.CV[:, 3:128:4], T.psL3[:, 3:128:4], AF.Copy), k_cv, t_cv)
-            bias(2)
-            t_P = plus(2, 1, s_v1)
-            s_P2 = sca(lambda: S.activation(pt(2), T.psT[:, :], AF.Copy), t_P)
-            y_P3 = add("y", lambda: Y.dma_start(pt(3), pt(2)), [s_P2], step=16)
-            bias(3, k_cv)
-            e_block(0, 0, 4)
-        if n == 1:
-            bias(0)
-            bias(1)
-            s_v2 = sca(lambda: S.activation(T.vs2[:, :], T.vbf[:, :].indirect(T.lst1[:, :]), AF.Copy), l_h[1])
-            e_block(0, 4, 12)
-        if n == 2:
-            bias(2)
-            bias(3)
-            s_v3 = sca(lambda: S.activation(T.vs3[:, :], T.vs1[:, :].indirect(T.lst1[:, :]), AF.Copy), l_h[1])
-            e_block(0, 12, 16)
-            e_block(1, 0, 16)
-            plus(4, 0, s_P2)
-    w_h = u_h
-    for t in (1, 2, 3, 4):
-        send((rank - t) % NR, T["Wl%d" % t][:, :], T.W[:, :], "w%d" % t, w_h)
-
-    pt_h = {2: s_P2}
-    pt_h[3] = add("g", lambda: g.dma_start(pt(3), T.vs2[:, :], accum_op=Op.add), [y_P3, s_v2], step=16)
-    zero(1)
-    q_h = {}
-
-    def move(e, frm, m):
-        L = T["lst%d" % m]
-        src, d = (T.vbf[:, :], d_v) if frm == 1 else (pt(frm), pt_h[frm])
-        pt_h[e] = sca(lambda: S.activation(pt(e), src.indirect(L[:, :]), AF.Copy), d, l_h[m])
-
-    def build_add(e, m, plus_e, h):
-        L, o, i = T["lst%d" % m], 512 * (3 - e // 4) + 256 * h, 512 * (3 - plus_e // 4) + 256 * h
-        q_h[e, h] = vec(lambda: V.tensor_tensor(T.TT[:, o:o + 256], T.P4[:, :].indirect(L[:, 16 * h:16 * h + 16]), T.TT[:, i:i + 256],
-                                                Op.add), *([s_P4, d_P4] if plus_e == 4 else [q_h[plus_e, h], d_P4]), l_h[m])
-
-    msk = {}
-
-    def mask(t, *deps):
-        msk[t] = vec(lambda: V.tensor_scalar(T.mask[:, 256 * t:256 * t + 256], T["psE%d" % (t // 2)][:, 256 * (t % 2):256 * (t % 2) + 256],
-                                             T.icol[:, 0:1], None, Op.is_equal), *deps)
-
-    v_ic = vec(lambda: V.tensor_copy(T.icol[:, :], T.ci[:, 1:2]), v_ci)
-    v_x = vec(lambda: V.tensor_copy(T.pl0[:, :], T.x128[:, :]), d_x)
-    mask(0, e_h[2], v_ic)
-    x_h, E_h = {}, []
-
-    def expo():
-        a = vec(lambda: V.tensor_scalar(T.ea[:, :], T.EL[:, :], 2, None, Op.logical_shift_right), d_e0, rem=[("earr", n_arr)])
-        i1 = vec(lambda: V.tensor_scalar(T.E1[:, :], T.EL[:, :], 512.0, None, Op.mult), d_e0)
-        E_h.extend([i1, vec(lambda: V.tensor_scalar(T.E2[:, :], T.ea[:, :], -512.0, 1536.0, Op.mult, Op.add), a)])
-        E_h.append(vec(lambda: V.tensor_copy(T.QL[:, 3:64:4], T.x128[:, :]), d_x))
-
-    def index(lo, hi):
-        c = slice(16 * lo, 16 * hi + 16)
-        src, rem = T.QL[:, 64 * lo + 3:64 * hi + 64:4], [("rq%d" % t, n_arr) for t in range(max(lo, 1), hi + 1)]
-        i1 = vec(lambda: V.tensor_tensor(T.xf1[:, c], src, T.E1[:, c], Op.add), *E_h, rem=rem)
-        i2 = vec(lambda: V.tensor_tensor(T.xf2[:, c], src, T.E2[:, c], Op.add))
-        x1 = vec(lambda: V.tensor_copy(T.xi1[:, c], T.xf1[:, c]), i1)
-        x2 = vec(lambda: V.tensor_copy(T.xi2[:, c], T.xf2[:, c]), i2)
-        for t in range(lo, hi + 1):
-            x_h[t] = [x1, x2]
-
-    r_1, r_2 = {}, {}
-
-    def term(t, which, on):
-        w = T.TT[:, 1536:9728] if which == 1 else T.TT[:, 0:2048]
-        i = w.indirect(T["xi%d" % which][:, 16 * t:16 * t + 16])
-        deps = [x_h[t][which - 1]] + ([z_h[0], s_P4] + [q_h[e, h] for e in (8, 12) for h in (0, 1)] if which == 2 else
-                                      [*z_h, *pt_h.values()])
-        r, o = T["r1_%d" % t], T["rr%d" % t]
-        if t not in r_1:
-            r_1[t] = (sca(lambda: S.activation(r[:, :], i, AF.Copy), *deps) if on == "s" else
-                      vec(lambda: V.tensor_copy(r[:, :], i), *deps))
+    gp("pc", lambda: g.iota(T.pc[:, :], [[1, 2]], 0, 1))
+    select("Gb", T.Gb[0:16, :], T.odd[0:16, :], [[-1, 2], [-2, 8], [0, 16]], Op.is_equal, 0.0, 0, 1, "odd1 odd2")
+    select("IDN", T.IDN[:, :], T.ones[:, 0:128], [[-1, 128]], Op.is_equal, 0.0, 0, 1, "ones")
+    select("L4", T.L4[0:4, :], T.ones[0:4, 0:128], [[0, 8], [-1, 4], [0, 4]], Op.is_equal, 0.0, 0, 1, "")
+    select("bV", T.bV[0:4, :], T.c256[0:4, :], [[0, 16], [-1, 4]], Op.is_equal, -512.0 * FR, 0, 1, "c256")
+    select("CV1", T.CV[:, 3:128:4], T.ones[:, 0:32], [[-16, 8], [0, 4]], Op.is_ge, 0.0, 0, 1, "CV0")
+    select("C7", T.C7[:, 3:128:4], T.ones[:, 0:32], [[-16, 8], [0, 4]], Op.is_equal, 0.0, -7, 1, "C70")
+    select("CV", T.CV[:, 3:128:4], T.CV[:, 3:128:4], [[16, 8], [0, 4]], Op.is_ge, 0.0, 15, -1, "CV1")
+    send(rank + 5, T.ex[:, 112:128], T.ex[:, 80:96], "e5", "e")
+    g_dma("P1", lambda: g.dma_start(pt(1), T.v[:, :]))
+    select("IDF", T.IDF[:, :], T.ones[:, 0:128], [[-1, 128]], Op.is_equal, 0.0, 0, 1, "")
+    send(rank - 1, half(T.Wl1, 0), half(T.W, 0), "w1a", "U40")
+    send(rank - 1, half(T.Wl1, 1), half(T.W, 1), "w1", "U41")
+    for t in (2, 3, 4):
+        send(rank - t, T["Wl%d" % t][:, :], T.W[:, :], "w%d" % t, "U40 U41")
+    send(rank + 1, T.XR[:, 32:48], T.XU[:, 32:48], "rq1", "X0")
+    for a in OPT["G"].split():
+        t = int(a[1])
+        if a[0] == "a":
+            ask(t)
+        elif a[0] == "p":
+            send(rank + 5, T.pr[:, :], T.pl5[:, :], "p5", "pl5")
         else:
-            r_2[t] = (sca(lambda: S.activation(o[:, :], i, AF.Copy), *deps) if on == "s" else
-                      vec(lambda: V.tensor_tensor(o[:, :], i, r[:, :], Op.add), r_1[t], *deps))
-            if t:
-                send((rank - t) % NR, T["rl%d" % t][:, :], o[:, :], "rs%d" % t, [r_2[t]])
+            send(rank - t, T["rl%d" % t][:, :], T["ra%d" % t][:, :], "rs%d" % t, "ra%d" % t)
 
-    p_h = {0: v_x}
-    for t in range(5):
-        Wt = T.W if t == 0 else T["Wl%d" % t]
-        R, pl, k = T["R%d" % t], T["pl%d" % t], (2 + t) % 4
-        r_h = vec(lambda R=R, Wt=Wt, pl=pl, t=t: V.tensor_tensor(R[:, :], Wt[:, :].indirect(pl[:, :]), T.mask[:, 256 * t:256 * t + 256],
-                                                                  Op.mult),
-                  *w_h, p_h[t], msk[t], rem=[("w%d" % t, n_arr)] if t else [])
-        tl = extract(k, R, cvs, r_h, k_cv)
-        if t in (0, 1, 2):
-            bias((4 + t) % 4)
-        if t == 0:
-            plus(4, 1)
-            plus(4, 2, s_v2)
-            t_P = plus(4, 3, s_v3)
-            for e, frm, m in ((5, 1, 2), (6, 2, 2), (9, 1, 3)):
-                move(e, frm, m)
-            s_P4 = sca(lambda: S.activation(slot(2), T.psT[:, :], AF.Copy), t_P)
-            d_P4 = add("y", lambda: Y.dma_start(T.P4[:, :], slot(2)), [s_P4], step=16)
-            for e, frm, m in ((13, 5, 3), (10, 2, 3), (14, 6, 3)):
-                move(e, frm, m)
-            pt_h[1] = sca(lambda: S.activation(pt(1), T.vbf[:, :], AF.Copy), d_v)
-            for e, frm, m in ((7, 3, 2), (11, 3, 3), (15, 7, 3)):
-                move(e, frm, m)
-            mask(1, e_h[3])
-        elif t == 1:
-            e_block(2, 0, 8)
-            mask(3, e_h[3])
-        elif t == 2:
-            e_block(2, 8, 16)
-            expo()
-        elif t == 3:
-            mask(4, e_h[5])
-        else:
-            build_add(8, 2, 4, 0)
-        scb = T["scv%d" % (t + 1)]
-        sc = scan(scb[:, :], k, tl, s_D4)
-        if t < 4:
-            p_h[t + 1] = vec(lambda t=t, scb=scb: V.tensor_copy(T["pl%d" % (t + 1)][:, :], scb[:, 3::4]), sc)
-        send((rank + t + 1) % NR, T.QL[:, 64 * (t + 1):64 * (t + 2)], scb[:, :], "rq%d" % (t + 1), [sc])
-        if t < 2:
-            zero(t + 2)
-        if t == 0:
-            mask(2, e_h[3])
-
-    index(0, 3)
-    term(1, 1, "s")
-    build_add(8, 2, 4, 1)
-    build_add(12, 3, 8, 0)
-    term(2, 1, "s")
-    term(0, 1, "s")
-    build_add(12, 3, 8, 1)
-    v_If = vec(lambda: V.tensor_copy(T.IDF[:, :], T.IDN[:, :]), k_I)
-    term(3, 1, "s")
-    term(1, 2, "v")
-    index(4, 5)
-    term(2, 2, "v")
-    term(4, 1, "s")
-    term(5, 1, "s")
-    term(3, 2, "v")
-    term(4, 2, "v")
-    term(5, 2, "v")
-    term(0, 2, "s")
-    acc = pe([lambda: P.matmul(T.psE0[:, 0:256], T.IDF[:, :], T.r1_0[:, :], start=True, stop=False)], r_1[0], v_If)
-    acc = pe([lambda: P.matmul(T.psE0[:, 0:256], T.IDF[:, :], T.rr0[:, :], start=False, stop=True)], r_2[0])
-    for t in (1, 2, 3, 4, 5):
-        o = T.psE0[:, 0:256] if t != 5 else T.yb[:, :]
-        acc = vec(lambda o=o, t=t: V.tensor_tensor(o, T.psE0[:, 0:256], T["rl%d" % t][:, :], Op.add), acc, rem=[("rs%d" % t, n_arr)])
-    d_y = add("y", lambda: Y.dma_start(T.y[:, :], T.yb[:, :]), [acc], step=16)
-    add("y", [], [d_y])
-
+    ops, index, head = [], {}, {q: 0 for q in queues}
+    while any(head[q] < len(order[q]) for q in queues):
+        before = len(ops)
+        for q in queues:
+            while head[q] < len(order[q]) and all(d in index for d in order[q][head[q]][2]):
+                name, calls, deps, rem, step = order[q][head[q]]
+                index[name] = len(ops)
+                ops.append((q, calls, [index[d] for d in deps], rem, step))
+                head[q] += 1
+        assert len(ops) > before
     known = {q: set() for q in queues}
     seen_rem = {q: set() for q in queues}
     waits, at_issue = [], []

@@ -3,12 +3,11 @@ from concourse.bass import DstId, RemoteDMATransfer
 from concourse.mybir import dt, AluOpType, AxisListType, ActivationFunctionType
 
 OPT = dict(
-    LV="g0 l1p g1 A0 s0 A1 l0 s1",
-    VO="ea R0 EE e5 P8a s0 xf p0 P8b  R1 b0 c0 X X0 s1 b1 p1 c1  R2 X1 P12a P12b s2 b2 p2 c2  R3 X2 s3 b3 p3 c3  "
-       "R4 X3 a1 s4 b4 p4 c4 X4 a2 a3  R5 a4 b5 X5 a5",
-    SO="m0 k4 M8 m1 m2 M12 m3 k2 m4 k3 m5 b1 b2 b0 a0 b3 b4 b5",
-    G="a1 a2 a3 p5 a4 r1 r2 r3 r4 r5",
-    PT={4: "ra0 rb0", 5: "rl1 rl2"}, LT="345")
+    LV="g00 l1p g01 g1 A0 s0 A1 l0 f s1", FILL=("eu", "ea", "EE", "xf"),
+    VO="R00 R01 X s00 P0 s01 p00 b0 p01  R10 R11 P1 s10 c0 s11 p10 X0 b1 p11  R20 R21 c1 e5 s20 X1 Q0 s21 p20 b2 p21  "
+       "R30 R31 c2 Q1 s30 s31 X2 p30 p31  c3 b3 R4 X3 a1 s4 b4 p4 c4 X4 a2 a3  R5 a4 b5 X5 a50 a51",
+    SO="v1 B10 B11 v2 B20 m0 B21 v3 B30 C0 B31 k4 M8 m1 m2 k1 M12 m3 k2 m4 k3 b1 m5 b2 b3 a0 b4 b0 b5",
+    G="w2 w3 w4 c1 a0 a1 a2 a3 p5 a4 r1 r2 r3 r4 l0 l1")
 NR = 6
 NPOOL = 120
 ZB = 16
@@ -16,29 +15,30 @@ WIN = ZB + 3 * 512
 FR = 4096.0
 BF, F32, I32, U16 = "bfloat16", "float32", "int32", "uint16"
 SCRATCH = {}
-for _n, _c, _d in (("nx16", 256, I32), ("nxb", 256, BF), ("nxl", 32, I32), ("nxt", 32, I32), ("ex", 128, I32), ("eu", 128, U16),
+for _n, _c, _d in (("nx32", 128, I32), ("nxb", 128, BF), ("nxl", 32, I32), ("nxt", 32, I32), ("ex", 128, I32), ("eu", 128, U16),
                    ("pr", 16, U16), ("xf0", 16, F32), ("vbf", 512, BF), ("ones", 256, BF), ("c256", 64, BF),
-                   ("odd", 256, BF), ("Gb", 256, BF), ("ID1", 128, BF), ("idr", 512, BF),
-                   ("CV", 144, BF), ("CB", 144, BF), ("CO", 144, BF), ("C7", 144, BF), ("L4", 128, BF), ("bV", 64, BF),
-                   ("IDN", 128, BF), ("IDF", 128, F32), ("D4", 64, F32), ("pc", 2, I32), ("ci", 2, I32), ("bt", 4, I32), ("c3", 1, I32),
+                   ("Gb", 512, BF), ("ID1", 128, BF), ("idr", 512, BF),
+                   ("CV", 144, BF), ("CB", 144, BF), ("CO", 144, BF), ("C7", 144, BF), ("C2", 144, BF),
+                   ("L4", 128, BF), ("b4", 64, BF), ("D4", 64, F32), ("L8", 128, BF), ("b8", 64, BF), ("D8", 64, F32),
+                   ("IDN", 128, BF), ("IDF", 128, F32), ("pc", 2, I32), ("ci", 2, I32), ("bt", 4, I32), ("c3", 1, I32),
                    ("icol", 1, F32), ("n15", 1, F32), ("c15", 1, F32), ("setc", 1, F32), ("ocol", 1, F32), ("acol", 4, F32),
                    ("bcol", 4, F32), ("en", 16, F32), ("m1", 16, F32), ("DM", 16, F32), ("MT", 16, BF), ("ea", 96, I32),
                    ("EE", 96, F32), ("XU", 192, U16), ("XR", 192, U16), ("W", 512, BF), ("mask", 1536, BF),
-                   ("TT", 2 * WIN, F32), ("yb", 256, F32)):
+                   ("TA", WIN + ZB, F32), ("TB", WIN, F32), ("yb", 256, F32)):
     SCRATCH[_n] = ("sbuf", [128, _c], _d)
 for _n in range(6):
     for _b, _c, _d, _k in (("A", 512, BF, (0, 1, 2, 3)), ("B", 512, BF, (0, 1, 2, 3)), ("U", 512, BF, (1, 2, 3)),
                            ("vs", 512, BF, (1, 2, 3)), ("scl", 128, F32, (1, 2, 3)), ("lst", 32, U16, (0, 1, 2, 3)),
                            ("Wl", 512, BF, (1, 2, 3, 4)), ("ra", 256, F32, range(6)), ("rb", 256, F32, range(6)),
-                           ("pl", 16, U16, range(1, 6)), ("R", 256, BF, range(6)), ("sa", 64, F32, range(5)), ("sb", 128, F32, range(6)),
+                           ("pl", 16, U16, range(1, 6)), ("R", 256, BF, range(6)), ("sa", 128, F32, range(5)), ("sb", 128, F32, range(6)),
                            ("rl", 256, F32, range(1, 6))):
         if _n in _k:
             SCRATCH["%s%d" % (_b, _n)] = ("sbuf", [128, _c], _d)
 for _n in ("psL0", "psL1", "psL2", "psL3", "psE0", "psE1", "psE2", "psT"):
     SCRATCH[_n] = ("psum", [128, 512], F32)
 
-SEMAPHORES = (["s%d" % k for k in range(NPOOL)] + ["loc", "e5", "p5", "w1a"] + ["w%d" % k for k in range(1, 5)]
-              + ["rp%d" % k for k in range(1, 5)] + ["rq%d" % k for k in range(1, 6)] + ["rs%d" % k for k in range(1, 6)])
+SEMAPHORES = (["s%d" % k for k in range(NPOOL)] + ["loc", "e5", "p5", "w1a", "rs5a", "rs5b"] + ["w%d" % k for k in range(1, 5)]
+              + ["rp%d" % k for k in range(1, 5)] + ["rq%d" % k for k in range(1, 6)] + ["rs%d" % k for k in range(1, 5)])
 
 
 def rank_program(g, core, T, topo):
@@ -56,242 +56,265 @@ def rank_program(g, core, T, topo):
         return add
 
     vec, sca, pe, gp = adder("v"), adder("s"), adder("t"), adder("g")
-    y_dma, s_dma, g_dma, g_rem = adder("y", 16), adder("s", 16), adder("g", 16), adder("g", 0)
+    y_dma, s_dma, g_rem = adder("y", 16), adder("s", 16), adder("g", 0)
 
-    def col(e):
-        return ZB + 512 * (e - 1) if e < 4 else WIN + ZB + 512 * (e // 4 - 1)
+    def slot(t, k):
+        return t[:, ZB + 512 * (k - 1):ZB + 512 * k]
 
-    def pt(e, lo=0, hi=512):
-        return T.TT[:, col(e) + lo:col(e) + hi]
+    def half(t, h, n=256):
+        return t[:, 0:2 * n] if h is None else t[:, n * h:n * h + n]
 
-    def half(t, h):
-        return t[:, 256 * h:256 * h + 256]
+    def tag(t, h):
+        return "%d" % t if h is None else "%d%d" % (t, h)
 
     es = topo.engines(core, [c for c in T.cores if c != core][0])
     n_arr = len(es)
     U = [None, T.U1, T.U2, T.U3, T.W]
     vs = [T.vbf, T.vs1, T.vs2, T.vs3]
     bank_l = ["psL%d" % (2 * (n % 2) + h) for n in range(3) for h in (0, 1)]
-    bank_a = ["psL%d" % (2 + t % 2) for t in range(5)]
+    bank_a = ["psL2", "psL3"]
     bank_b = ["psL%d" % (t % 2) for t in range(6)]
     bank_p = {2: "psT", 3: "psE2", 4: "psE0"}
+    tables_a, tables_b = "z0 z1 P1 P2 P3", "zb P4 P80 P81 P120 P121"
 
-    def term(name):
-        which, t = name[0], int(name[1])
-        own = t == 0 or name == "a5"
-        c = 32 * t + (16 if which == "a" else 0)
-        w = T.TT[:, WIN:2 * WIN] if which == "b" else T.TT[:, 0:WIN + ZB]
-        i = w.indirect((T.XU if own else T.XR)[:, c:c + 16])
-        deps = "z1 P4 P8a P8b P12a P12b" if which == "b" else "z0 z1 P1 P2 P3"
-        deps += {"b0": " X", "a0": " X0", "a5": " X5"}.get(name, "")
-        rem = [] if own else [("r%s%d" % ("p" if which == "a" else "q", t), n_arr if name == "b1" else n_arr // 2)]
-        o = T["r" + name]
-        if which == "b" or t == 0:
-            sca("r" + name, lambda: S.activation(o[:, :], i, AF.Copy), deps, rem)
-        else:
-            vec("r" + name, lambda: V.tensor_tensor(o[:, :], i, T["rb%d" % t][:, :], Op.add), deps + " rb%d" % t, rem)
-
-    y_dma("nx16", lambda: Y.dma_start(T.nx16[0:16, :], T.nx[:, :]))
+    y_dma("nx32", lambda: Y.dma_start(T.nx32[0:32, :], T.nx[:, :]))
+    y_dma("nxl1", lambda: Y.dma_start(T.nxl[:, 16:32], T.nx[1::2, :]))
     y_dma("e", lambda: Y.dma_start(T.ex[:, 0:96], T.e[:, :]))
-    y_dma("x", lambda: Y.dma_start(T.ex[:, 96:112], T.x[:, :]))
-    y_dma("y", lambda: Y.dma_start(T.y[:, :], T.yb[:, :]), "yb")
-    y_dma("end", [], "y")
+    y_dma("y0", lambda: Y.dma_start(T.y[:, 0:128], T.yb[:, 0:128]), "yb0")
+    y_dma("end", [], "y0 y1")
 
-    def scan(name, out, b, deps):
-        vec(name, lambda: V.tensor_tensor_scan(out, T.D4[:, :], T[b][:, 0:64], 0.0, Op.mult, Op.max), "D4 " + deps)
+    def scan(name, out, b, deps, k=4):
+        vec(name, lambda: V.tensor_tensor_scan(out, T["D%d" % k][:, :], T[b][:, 0:64], 0.0, Op.mult, Op.max), "D%d " % k + deps)
 
-    vec("odd0", lambda: V.memset(T.odd[0:16, :], 1.0))
     vec("ones", lambda: V.memset(T.ones[:, :], 1.0))
-    vec("odd1", lambda: V.memset(T.odd[0:16, 0::2], 0.0), "odd0")
-    vec("odd2", lambda: V.memset(T.odd[0:16, 15::16], 0.0))
+    vec("Gb0", lambda: V.memset(T.Gb[0:32, 0::2], 0.0))
     vec("idr0", lambda: V.tensor_tensor_scan(T.idr[:, 0:256], T.ones[:, :], T.ones[:, :], -257.0, Op.mult, Op.add), "ones")
     vec("ci", lambda: V.tensor_scalar(T.ci[:, :], T.pc[:, :], 15, None, Op.bitwise_and), "pc")
     vec("c3", lambda: V.tensor_scalar(T.c3[:, :], T.pc[:, 1:2], 3, None, Op.bitwise_and))
     for n in range(1, 4):
         vec("bt%d" % n, lambda n=n: V.tensor_scalar(T.bt[:, n:n + 1], T.pc[:, 0:1], n, 1, Op.logical_shift_right, Op.bitwise_and))
+    vec("c15", lambda: V.tensor_scalar(T.c15[:, :], T.ci[:, 1:2], 0.0, None, Op.is_equal), "ci")
+    vec("n15", lambda: V.tensor_scalar(T.n15[:, :], T.ci[:, 1:2], 1.0, None, Op.is_ge))
     vec("setc", lambda: V.tensor_scalar(T.setc[:, :], T.c3[:, :], 0.0, FR, Op.is_equal, Op.mult), "c3")
     vec("ocol", lambda: V.tensor_scalar(T.ocol[:, :], T.c3[:, :], 512.0, None, Op.mult))
-    vec("n15", lambda: V.tensor_scalar(T.n15[:, :], T.ci[:, 1:2], 1.0, None, Op.is_ge), "ci")
-    vec("c15", lambda: V.tensor_scalar(T.c15[:, :], T.ci[:, 1:2], 0.0, None, Op.is_equal))
     vec("icol", lambda: V.tensor_copy(T.icol[:, :], T.ci[:, 1:2]))
     vec("en", lambda: V.tensor_tensor_scan(T.en[:, :], T.ones[:, 0:16], T.ones[:, 0:16], -1.0, Op.mult, Op.add))
     vec("acol", lambda: V.tensor_scalar(T.acol[:, 1:4], T.bt[:, 1:4], T.n15[:, 0:1], None, Op.mult), "n15 bt1 bt2 bt3")
-    vec("nxb", lambda: V.tensor_scalar(T.nxb[0:16, :], T.nx16[0:16, :], -256.0, None, Op.add), "nx16")
+    vec("nxb", lambda: V.tensor_scalar(T.nxb[0:32, :], T.nx32[0:32, :], -256.0, None, Op.add), "nx32")
     vec("DM0", lambda: V.tensor_scalar(T.DM[:, :], T.D4[:, 0:16], T.setc[:, 0:1], 1.0 / FR, Op.mult, Op.mult), "D4 setc")
     vec("m1", lambda: V.tensor_scalar(T.m1[:, :], T.en[:, :], T.icol[:, 0:1], None, Op.is_equal), "en icol")
+    vec("CV0", lambda: V.memset(T.CV[:, :], 0.0))
     vec("nxt", lambda: V.transpose(T.nxt[:, :], T.nxl[:, :]), "nxl0 nxl1")
     vec("DM", lambda: V.tensor_scalar(T.DM[:, 1::4], T.DM[:, 1::4], 1.0 / FR, None, Op.mult), "DM0")
+    vec("C20", lambda: V.memset(T.C2[:, :], 0.0))
     vec("lst0", lambda: V.tensor_copy(T.lst0[:, :], T.nxt[:, :]), "nxt")
+    vec("A0b", lambda: V.tensor_scalar(half(T.A0, 1), T.psE1[:, 0:256], T.n15[:, 0:1], None, Op.mult), "nx1 n15")
     vec("MT", lambda: V.tensor_tensor_scan(T.MT[:, :], T.DM[:, :], T.m1[:, :], 0.0, Op.mult, Op.add), "DM m1")
-    vec("A0b", lambda: V.tensor_copy(half(T.A0, 1), T.psE1[:, 0:256]), "nx1")
-
-    def compose(n, h):
-        A, B, L = T["A%d" % n], T["B%d" % n], T["lst%d" % n]
-        vec("U%d%d" % (n + 1, h), lambda: V.tensor_tensor(half(U[n + 1], h), A[:, :].indirect(L[:, 16 * h:16 * h + 16]), half(B, h), Op.add),
-            "A0a A0b B0 lst0" if n == 0 else "A%d0 A%d1 B%d%d lst%d%d" % (n, n, n, h, n, h))
-
-    def window(m, h):
-        vec("A%d%d" % (m, h), lambda: V.tensor_scalar(half(T["A%d" % m], h), half(U[m], h), T.acol[:, m:m + 1], None, Op.mult),
-            "U%d%d acol" % (m, h))
-
-    def scan_l(m, h):
-        scan("scl%d%d" % (m, h), T["scl%d" % m][:, 64 * h:64 * h + 64], bank_l[2 * m - 2 + h], "xl%d%d" % (m, h))
-
-    def to_list(m, h):
-        vec("lst%d%d" % (m, h), lambda: V.tensor_copy(T["lst%d" % m][:, 16 * h:16 * h + 16], T["scl%d" % m][:, 64 * h + 3:64 * h + 64:4]),
-            "scl%d%d" % (m, h))
-
-    for n in range(4):
-        for a in OPT["LV"].split():
-            m, h = n + 1 - (a[-1] == "p"), int(a[1])
-            if a[0] == "g":
-                compose(n, h)
-            elif 0 < m < 4:
-                {"A": window, "s": scan_l, "l": to_list}[a[0]](m, h)
-        if n == 1:
-            vec("eu", lambda: V.tensor_copy(T.eu[:, 0:112], T.ex[:, 0:112]), "e x")
-
-    def visit(t):
-        Wt = T.W if t in (0, 5) else T["Wl%d" % t]
-        pl = T.pr[:, :] if t == 5 else T["pl%d" % t][:, :] if t else T.eu[:, 96:112]
-        vec("R%d" % t, lambda: V.tensor_tensor(T["R%d" % t][:, :], Wt[:, :].indirect(pl), half(T.mask, t), Op.mult),
-            "U40 U41 %s mask%d" % ("pl%d" % t if 0 < t < 5 else "eu", t),
-            [(s, n_arr) for s in {0: [], 1: ["w1a", "w1"], 5: ["p5"]}.get(t, ["w%d" % t])])
-
-    def scan_a(t):
-        scan("sa%d" % t, T["sa%d" % t][:, :], bank_a[t], "xa%d" % t)
-
-    def place(t):
-        vec("pl%d" % (t + 1), lambda: V.tensor_scalar(T["pl%d" % (t + 1)][:, :], T["sa%d" % t][:, 3::4], 0.25, None, Op.add), "sa%d" % t)
-
-    def add_a(t):
-        vec("sc%d" % t, lambda: V.tensor_tensor(T["sb%d" % t][:, 67::4], T["sa%d" % t][:, 3::4], T.EE[:, 16 * t + 16:16 * t + 32], Op.add),
-            "sa%d EE" % t)
-
-    def scan_b(t):
-        scan("sb%d" % t, T["sb%d" % t][:, 0:64], bank_b[t], "xb%d" % t)
-
-    def offsets(t):
-        sbt, c, n = T["sb%d" % t], 32 * t + 16, 128 if t < 5 else 64
-        vec("X%d" % t, lambda: V.tensor_scalar(T.XU[:, c:c + n // 4], sbt[:, 3:n:4], ZB - 511.75, float(WIN), Op.add, Op.min),
-            "sb%d" % t + (" sc%d" % t if t < 5 else ""))
-
-    def add4(e, h):
-        o = pt(e, 256 * h, 256 * h + 256)
-        vec("P%d%s" % (e, "ab"[h]), lambda: V.tensor_tensor(o, o, half(T.psE0, h), Op.add), "M%d P4" % e)
 
     small = {
+        "eu": lambda: vec("eu", lambda: V.tensor_copy(T.eu[:, 0:112], T.ex[:, 0:112]), "e x"),
         "ea": lambda: vec("ea", lambda: V.tensor_scalar(T.ea[:, :], T.ex[:, 0:96], 2, None, Op.logical_shift_right), "e"),
         "EE": lambda: vec("EE", lambda: V.tensor_scalar(T.EE[:, :], T.ea[:, :], 512.0, None, Op.mult), "ea"),
         "xf": lambda: vec("xf0", lambda: V.tensor_tensor(T.xf0[:, :], T.ex[:, 96:112], T.EE[:, 0:16], Op.add), "x EE"),
         "X": lambda: vec("X", lambda: V.tensor_scalar(T.XU[:, 0:16], T.xf0[:, :], ZB - 511.75, None, Op.add), "xf0"),
         "e5": lambda: vec("eu5", lambda: V.tensor_copy(T.eu[:, 112:128], T.ex[:, 112:128]), "", [("e5", n_arr)]),
     }
+
+    def u(m, h):
+        return "U%d%d" % (m, h) + (" U%d0q" % m if h == 0 and m > 1 else "")
+
+    def compose(n, h, q=None):
+        A, B, L = T["A%d" % n], T["B%d" % n], T["lst%d" % n]
+        lo, w = (256 * h, 256) if q is None else (256 * h + 128 * q, 128)
+        vec("U%d%d" % (n + 1, h) + ("q" if q == 0 else ""),
+            lambda: V.tensor_tensor(U[n + 1][:, lo:lo + w], A[:, :].indirect(L[:, lo // 16:(lo + w) // 16]), B[:, lo:lo + w], Op.add),
+            "A0a A0b B0 lst0" if n == 0 else "A%d0 A%d1 B%d%d lst%d%d" % (n, n, n, h, n, h))
+
+    def window(m, h):
+        vec("A%d%d" % (m, h), lambda: V.tensor_scalar(half(T["A%d" % m], h), half(U[m], h), T.acol[:, m:m + 1], None, Op.mult),
+            u(m, h) + " acol")
+
+    def scan_l(m, h):
+        scan("scl%d%d" % (m, h), half(T["scl%d" % m], h, 64), bank_l[2 * m - 2 + h], "xl%d%d" % (m, h))
+
+    def to_list(m, h):
+        vec("lst%d%d" % (m, h), lambda: V.tensor_copy(half(T["lst%d" % m], h, 16), half(T["scl%d" % m], h, 64)[:, 3::4]), "scl%d%d" % (m, h))
+
+    for n in range(4):
+        for a in OPT["LV"].split():
+            if a == "f":
+                small[OPT["FILL"][n]]()
+            elif a[0] == "g":
+                if n:
+                    compose(n, *[int(x) for x in a[1:]])
+                elif a != "g01":
+                    compose(n, int(a[1]))
+            elif 0 < n + 1 - (a[-1] == "p") < 4:
+                {"A": window, "s": scan_l, "l": to_list}[a[0]](n + 1 - (a[-1] == "p"), int(a[1]))
+
+    def visit(t, h=None):
+        Wt = T.W if t in (0, 5) else T["Wl%d" % t]
+        pl = half(T.pr[:, :] if t == 5 else T["pl%d" % t][:, :] if t else T.eu[:, 96:112], h, 8)
+        vec("R" + tag(t, h), lambda: V.tensor_tensor(half(T["R%d" % t], h, 128), Wt[:, :].indirect(pl), half(half(T.mask, t), h, 128), Op.mult),
+            u(4, 0) + " U41 mask%d " % t + {0: "eu", 4: "pl40 pl41", 5: ""}.get(t, "pl" + tag(t, h)),
+            [(s, n_arr) for s in {0: [], 1: ["w1a", "w1"], 5: ["p5"]}.get(t, ["w%d" % t])])
+
+    def places(t, h=None):
+        return T.sa4[:, 3:64:4] if t == 4 else half(T["sa%d" % t], h, 64)[:, 7::8]
+
+    def scan_a(t, h=None):
+        scan("sa" + tag(t, h), half(T["sa%d" % t], h or 0, 64), bank_a[h or 0], "xa" + tag(t, h), 4 if h is None else 8)
+
+    def place(t, h=None):
+        vec("pl" + tag(t + 1, h), lambda: V.tensor_scalar(half(T["pl%d" % (t + 1)], h, 8), places(t, h), 0.25, None, Op.add), "sa" + tag(t, h))
+
+    def add_a(t):
+        vec("sc%d" % t, lambda: V.tensor_tensor(T["sb%d" % t][:, 67::4], places(t), T.EE[:, 16 * t + 16:16 * t + 32], Op.add),
+            "EE " + ("sa4" if t == 4 else "sa%d0 sa%d1" % (t, t)))
+
+    def scan_b(t):
+        scan("sb%d" % t, T["sb%d" % t][:, 0:64], bank_b[t], "xb%d" % t)
+
+    def offsets(t):
+        c, n = 32 * t + 16, 128 if t < 5 else 64
+        vec("X%d" % t, lambda: V.tensor_scalar(T.XU[:, c:c + n // 4], T["sb%d" % t][:, 3:n:4], ZB - 511.75, float(WIN), Op.add, Op.min),
+            "sb%d sc%d" % (t, t) if t < 5 else "sb5")
+
+    def term_a(t, h=None):
+        i = half((T.XU if t == 5 else T.XR)[:, 32 * t + 16:32 * t + 32], h, 8)
+        vec("ra" + tag(t, h), lambda: V.tensor_tensor(half(T["ra%d" % t], h, 128), T.TA[:, :].indirect(i), half(T["rb%d" % t], h, 128), Op.add),
+            tables_a + " rb%d" % t + (" X5" if t == 5 else ""), [("rp%d" % t, n_arr // 2)] if t < 5 else [])
+
+    def add4(e, h):
+        o = half(slot(T.TB, e // 4), h)
+        vec("P%d%d" % (e, h), lambda: V.tensor_tensor(o, o, half(T.psE0, h), Op.add), "M%d P4" % e)
+
     for a in OPT["VO"].split():
         if a in small:
             small[a]()
-        elif a[0] == "P":
-            add4(int(a[1:-1]), "ab".index(a[-1]))
-        elif a[0] == "a":
-            term(a)
         else:
-            {"R": visit, "s": scan_a, "p": place, "c": add_a, "b": scan_b, "X": offsets}[a[0]](int(a[1]))
-    last = "acc"
-    for t in OPT["LT"]:
-        o = T.psE1[:, 0:256] if t != "5" else T.yb[:, :]
-        name = "acc" + t if t != "5" else "yb"
-        vec(name, lambda o=o, t=t: V.tensor_tensor(o, T.psE1[:, 0:256], T["rl" + t][:, :], Op.add), last, [("rs" + t, n_arr)])
-        last = name
+            {"R": visit, "s": scan_a, "p": place, "c": add_a, "b": scan_b, "X": offsets, "a": term_a,
+             "P": lambda h: add4(8, h), "Q": lambda h: add4(12, h)}[a[0]](*[int(x) for x in a[1:]])
+    for t in (3, 4, 5):
+        for h in (0, 1):
+            o, name = (T.psE1, "acc%d%d" % (t, h)) if t < 5 else (T.yb, "yb%d" % h)
+            vec(name, lambda o=o, t=t, h=h: V.tensor_tensor(half(o, h, 128), half(T.psE1, h, 128), half(T["rl%d" % t], h, 128), Op.add),
+                "acc" if t == 3 else "acc%d%d" % (t - 1, h), [("rs%d" % t + ("ab"[h] if t == 5 else ""), n_arr)])
 
-    def act(name, out, in_, deps, **k):
-        sca(name, lambda: S.activation(out, in_, AF.Copy, **k), deps)
+    def act(name, out, in_, deps, rem=(), **k):
+        sca(name, lambda: S.activation(out, in_, AF.Copy, **k), deps, rem)
 
     def mask(t):
         c = 16 * t if t < 5 else 112
         act("mask%d" % t, half(T.mask, t), T.MT[:, :].indirect(T.eu[:, c:c + 16]), "MT eu" if t < 5 else "MT eu5")
 
     def keep(k):
-        act("P%d" % k, pt(k), T[bank_p[k]][:, :], "sum%d%d" % (k, k - 1))
+        act("P%d" % k, slot(T.TA, k) if k < 4 else slot(T.TB, 1), T[bank_p[k]][:, :] if k > 1 else T.vbf[:, :],
+            "sum%d%d" % (k, k - 1) if k > 1 else "vs0")
 
     def moved(e):
-        act("M%d" % e, pt(e), pt(e - 4).indirect(T.lst2[:, :]), "P4 lst20 lst21" if e == 8 else "P8a P8b")
+        act("M%d" % e, slot(T.TB, e // 4), slot(T.TB, e // 4 - 1).indirect(T.lst2[:, :]), "P4 lst20 lst21" if e == 8 else "P80 P81")
+
+    def consts(_):
+        act("CB", T.CB[:, :], T.CV[:, :], "CV setc", scale=T.setc[:, 0:1])
+        act("CO", T.CO[:, :], T.CV[:, :], "ocol", scale=T.ocol[:, 0:1])
+
+    def step_v(m):
+        act("vs%d" % m, vs[m][:, :], vs[m - 1][:, :].indirect(T.lst0[:, :]), "lst0 vs%d" % (m - 1))
+
+    def rest(mh):
+        m, h = divmod(mh, 10)
+        act("B%d" % mh, half(T["B%d" % m], h), half(U[m], h), u(m, h) + " bcol", scale=T.bcol[:, m:m + 1])
+
+    def term_b(t):
+        act("rb%d" % t, T["rb%d" % t][:, :], T.TB[:, :].indirect((T.XR if t else T.XU)[:, 32 * t:32 * t + 16]),
+            tables_b + ("" if t else " X"), [("rq%d" % t, n_arr // (2 if t > 1 else 1))] if t else [])
 
     s_dma("nxl0", lambda: S.dma_start(T.nxl[:, 0:16], T.nx[0::2, :]))
-    s_dma("nxl1", lambda: S.dma_start(T.nxl[:, 16:32], T.nx[1::2, :]))
     s_dma("vs0", lambda: S.dma_start(T.vbf[:, :], T.v[:, :]))
+    s_dma("x", lambda: S.dma_start(T.ex[:, 96:112], T.x[:, :]))
     act("ID10", T.ID1[0:1, :], T.ones[0:1, 0:128], "ones")
-    act("C70", T.C7[:, :], T.ones[:, 0:144], "", scale=0.0)
+    act("D40", T.D4[:, :], T.ones[:, 0:64], "")
+    act("c256", T.c256[0:8, :], T.ones[0:8, 0:64], "", bias=256.0, scale=0.0)
     act("ID1", T.ID1[0:1, 1::2], T.ones[0:1, 0:64], "ID10", scale=0.0)
     act("idr1", T.idr[:, 256:512], T.idr[:, 0:256], "idr0", bias=256.0)
-    act("CV0", T.CV[:, :], T.ones[:, 0:144], "", scale=0.0)
-    act("D40", T.D4[:, :], T.ones[:, 0:64], "")
-    act("c256", T.c256[0:4, :], T.ones[0:4, 0:64], "", bias=256.0, scale=0.0)
     act("D4", T.D4[:, 0::4], T.ones[:, 0:16], "D40", scale=0.0)
-    act("z0", T.TT[:, 0:ZB], T.ones[:, 0:ZB], "", scale=0.0)
-    act("z1", T.TT[:, WIN:WIN + ZB], T.ones[:, 0:ZB], "", scale=0.0)
-    act("bcol", T.bcol[:, 1:4], T.acol[:, 1:4], "acol", bias=1.0, scale=-1.0)
+    act("C70", T.C7[:, :], T.ones[:, 0:144], "", scale=0.0)
     act("B0", T.B0[:, :], T.idr[:, :], "c15 idr0 idr1", scale=T.c15[:, 0:1])
-    act("A0a", half(T.A0, 0), T.psE0[:, 0:256], "nx0")
-    for m in (1, 2, 3):
-        if m == 3:
-            act("CB", T.CB[:, :], T.CV[:, :], "CV setc", scale=T.setc[:, 0:1])
-            act("CO", T.CO[:, :], T.CV[:, :], "ocol", scale=T.ocol[:, 0:1])
-        act("vs%d" % m, vs[m][:, :], vs[m - 1][:, :].indirect(T.lst0[:, :]), "lst0 vs%d" % (m - 1))
-        for h in (0, 1):
-            act("B%d%d" % (m, h), half(T["B%d" % m], h), half(U[m], h), "U%d%d bcol" % (m, h), scale=T.bcol[:, m:m + 1])
+    act("D80", T.D8[:, :], T.ones[:, 0:64], "")
+    act("bcol", T.bcol[:, 1:4], T.acol[:, 1:4], "acol", bias=1.0, scale=-1.0)
+    act("A0a", half(T.A0, 0), T.psE0[:, 0:256], "nx0 n15", scale=T.n15[:, 0:1])
+    act("D8", T.D8[:, 0::8], T.ones[:, 0:8], "D80", scale=0.0)
+    act("z0", T.TA[:, 0:ZB], T.ones[:, 0:ZB], "", scale=0.0)
+    act("z1", T.TA[:, WIN:WIN + ZB], T.ones[:, 0:ZB], "", scale=0.0)
+    act("zb", T.TB[:, 0:ZB], T.ones[:, 0:ZB], "", scale=0.0)
     for a in OPT["SO"].split():
-        if a[0] in "ab":
-            term(a)
+        if a == "a0":
+            act("ra0", T.ra0[:, :], T.TA[:, :].indirect(T.XU[:, 16:32]), tables_a + " X0")
         else:
-            {"m": mask, "k": keep, "M": moved}[a[0]](int(a[1:]))
+            {"m": mask, "k": keep, "M": moved, "v": step_v, "B": rest, "C": consts, "b": term_b}[a[0]](int(a[1:]))
+    s_dma("y1", lambda: S.dma_start(T.y[:, 128:256], T.yb[:, 128:256]), "yb1")
 
-    def bias(b, deps=""):
-        pe(None, lambda: P.matmul(T[b][:, 0:64], T.L4[0:4, :], T.bV[0:4, :], start=True, stop=False), deps)
+    def bias(b, deps="", k=4):
+        pe(None, lambda: P.matmul(T[b][:, 0:64], T["L%d" % k][0:k, :], T["b%d" % k][0:k, :], start=True, stop=False),
+           "L%d b%d %s" % (k, k, deps))
 
-    def extract(name, b, rows, c, deps, stop=True):
-        pe(name, [lambda s=s: P.matmul(T[b][:, 0:64], c[:, 3 - s:131 - s], rows[:, s::4], start=False, stop=(stop and s == 3))
-                  for s in range(4)], deps)
+    def extract(name, b, rows, c, deps, stop=True, n=4):
+        pe(name, [lambda s=s: P.matmul(T[b][:, 0:64], c[:, n - 1 - s:n + 127 - s], rows[:, s::n], start=False, stop=(stop and s == n - 1))
+                  for s in range(n)], deps)
 
     def plus(k, i, deps=""):
         pe("sum%d%d" % (k, i), lambda: P.matmul(T[bank_p[k]][:, :], T.IDN[:, :], vs[i][:, :], start=(i == 0), stop=(i == k - 1)),
            "IDN vs%d %s" % (i, deps))
 
+    def total(r, name=None):
+        pe(name, lambda: P.matmul(T.psE1[:, 0:256], T.IDF[:, :], T[r][:, :], start=(r == "ra0"), stop=bool(name)),
+           "IDF A0b" + ("" if r[1] == "l" else " " + r), [("rs" + r[2], n_arr)] if r[1] == "l" else [])
+
     for h in (0, 1):
         pe(None, lambda h=h: P.matmul(T["psE%d" % h][:, 0:256], T.ID1[0:1, :], T.idr[0:1, 256 * h:256 * h + 256], start=True, stop=False),
            "ID1 idr%d" % h)
     for h in (0, 1):
-        pe("nx%d" % h, lambda h=h: P.matmul(T["psE%d" % h][:, 0:256], T.Gb[0:16, 128 * h:128 * h + 128], T.nxb[0:16, :],
-                                            start=False, stop=True), "nxb Gb")
-    plus(4, 0, "A0a")
+        pe("nx%d" % h, [lambda h=h, q=q: P.matmul(half(T["psE%d" % h], q, 128), half(T.Gb[0:32, :], 2 * h + q, 128), T.nxb[0:32, :],
+                                                  start=False, stop=(q == 1)) for q in (0, 1)], "nxb Gb Gb0")
     for k in range(4):
-        bias("psL%d" % k, "L4 bV")
+        bias("psL%d" % k)
+    plus(4, 0, "A0a")
     for n in range(3):
         for h in (0, 1):
-            extract("xl%d%d" % (n + 1, h), bank_l[2 * n + h], half(U[n + 1], h), T.C7, "U%d%d C7" % (n + 1, h))
+            extract("xl%d%d" % (n + 1, h), bank_l[2 * n + h], half(U[n + 1], h), T.C7, u(n + 1, h) + " C7")
         plus(4, n + 1)
         for h in (0, 1):
-            bias(bank_l[2 * n + h], "scl%d%d" % (n + 1, h))
+            if n != 1:
+                bias(bank_l[2 * n + h], "scl%d%d" % (n + 1, h))
+    for h in (0, 1):
+        bias(bank_a[h], "scl2%d" % h, 8)
     for t in range(6):
         extract(None, bank_b[t], half(T.mask, t), T.CO, "mask%d CO" % t, stop=False)
         if t == 0:
             plus(2, 0)
             plus(2, 1)
             plus(3, 0)
-        if t < 5:
-            extract("xa%d" % t, bank_a[t], T["R%d" % t], T.CV, "R%d CV" % t)
-        extract("xb%d" % t, bank_b[t], T["R%d" % t], T.CB, "R%d CB" % t)
+        if t < 4:
+            for h in (0, 1):
+                extract("xa%d%d" % (t, h), bank_a[h], half(T["R%d" % t], h, 128), T.C2, "R%d%d C2" % (t, h), n=2)
+            extract("xb%d" % t, bank_b[t], T["R%d" % t], T.CB, "CB")
+            bias(bank_a[0], "sa%d0" % t, 8 if t < 3 else 4)
+            if t < 3:
+                bias(bank_a[1], "sa%d1" % t, 8)
+        elif t == 4:
+            extract("xa4", bank_a[0], T.R4, T.CV, "R4 CV")
+            extract("xb4", bank_b[4], T.R4, T.CB, "")
+        else:
+            total("ra0")
+            extract("xb5", bank_b[5], T.R5, T.CB, "R5")
         if 0 < t < 5:
             bias(bank_b[t + 1], "sb%d" % (t - 1))
-        if t < 3:
-            bias(bank_a[t], "sa%d" % t)
-        if t == 0:
-            plus(3, 1)
-            plus(3, 2)
-        for r in OPT["PT"].get(t, "").split():
-            first, end = r == "ra0", r == OPT["PT"][5].split()[-1]
-            pe("acc" if end else None,
-               lambda r=r, first=first, end=end: P.matmul(T.psE1[:, 0:256], T.IDF[:, :], T[r][:, :], start=first, stop=end),
-               "IDF A0b" + ("" if r[1] == "l" else " " + r), [("rs" + r[2], n_arr)] if r[1] == "l" else [])
+        if t < 2:
+            plus(3, t + 1)
+    total("rb0")
+    total("rl1")
+    total("rl2", "acc")
 
     loc = [0]
 
@@ -302,6 +325,8 @@ def rank_program(g, core, T, topo):
         g_rem(None, lambda: g.remote_dma(out, in_, T.sem[sem], T.sem.loc, pid, rid, topo.mask(core, d)), deps)
 
     def ask(t):
+        if t == 0:
+            return send(rank + 1, T.XR[:, 32:48], T.XU[:, 32:48], "rq1", "X0")
         n, trs = n_arr // 2, []
         for k in (0, 1):
             rid, pid, _ = topo.addr(T.cores[(rank + t + k) % NR])
@@ -314,28 +339,36 @@ def rank_program(g, core, T, topo):
     def select(name, out, in_, pattern, op, fill, base, cm, deps):
         gp(name, lambda: g.affine_select(out, in_, pattern, op, fill, base, cm), deps)
 
+    def same_group(name, n):
+        c = T[name][:, n - 1:128:n]
+        select(name + "1", c, T.ones[:, 0:128 // n], [[-16, 8], [0, 16 // n]], Op.is_ge, 0.0, 0, 1, name + "0")
+        select(name, c, c, [[16, 8], [0, 16 // n]], Op.is_ge, 0.0, 15, -1, name + "1")
+
     gp("pc", lambda: g.iota(T.pc[:, :], [[1, 2]], 0, 1))
-    select("Gb", T.Gb[0:16, :], T.odd[0:16, :], [[-1, 2], [-2, 8], [0, 16]], Op.is_equal, 0.0, 0, 1, "odd1 odd2")
-    select("IDN", T.IDN[:, :], T.ones[:, 0:128], [[-1, 128]], Op.is_equal, 0.0, 0, 1, "ones")
+    select("Gb", T.Gb[0:32, 1::2], T.ones[0:32, :], [[-1, 4], [-4, 8], [0, 8]], Op.is_equal, 0.0, 0, 1, "ones")
     select("L4", T.L4[0:4, :], T.ones[0:4, 0:128], [[0, 8], [-1, 4], [0, 4]], Op.is_equal, 0.0, 0, 1, "")
-    select("bV", T.bV[0:4, :], T.c256[0:4, :], [[0, 16], [-1, 4]], Op.is_equal, -512.0 * FR, 0, 1, "c256")
-    select("CV1", T.CV[:, 3:128:4], T.ones[:, 0:32], [[-16, 8], [0, 4]], Op.is_ge, 0.0, 0, 1, "CV0")
+    select("b4", T.b4[0:4, :], T.c256[0:4, :], [[0, 16], [-1, 4]], Op.is_equal, -512.0 * FR, 0, 1, "c256")
+    select("IDN", T.IDN[:, :], T.ones[:, 0:128], [[-1, 128]], Op.is_equal, 0.0, 0, 1, "")
     select("C7", T.C7[:, 3:128:4], T.ones[:, 0:32], [[-16, 8], [0, 4]], Op.is_equal, 0.0, -7, 1, "C70")
-    select("CV", T.CV[:, 3:128:4], T.CV[:, 3:128:4], [[16, 8], [0, 4]], Op.is_ge, 0.0, 15, -1, "CV1")
+    same_group("CV", 4)
     send(rank + 5, T.ex[:, 112:128], T.ex[:, 80:96], "e5", "e")
-    g_dma("P1", lambda: g.dma_start(pt(1), T.v[:, :]))
-    select("IDF", T.IDF[:, :], T.ones[:, 0:128], [[-1, 128]], Op.is_equal, 0.0, 0, 1, "")
-    send(rank - 1, half(T.Wl1, 0), half(T.W, 0), "w1a", "U40")
+    select("L8", T.L8[0:8, :], T.ones[0:8, 0:128], [[0, 8], [-1, 8], [0, 2]], Op.is_equal, 0.0, 0, 1, "")
+    select("b8", T.b8[0:8, :], T.c256[0:8, :], [[0, 8], [-1, 8]], Op.is_equal, -512.0 * FR, 0, 1, "")
+    same_group("C2", 2)
+    send(rank - 1, half(T.Wl1, 0), half(T.W, 0), "w1a", u(4, 0))
     send(rank - 1, half(T.Wl1, 1), half(T.W, 1), "w1", "U41")
-    for t in (2, 3, 4):
-        send(rank - t, T["Wl%d" % t][:, :], T.W[:, :], "w%d" % t, "U40 U41")
-    send(rank + 1, T.XR[:, 32:48], T.XU[:, 32:48], "rq1", "X0")
     for a in OPT["G"].split():
-        t = int(a[1])
+        t = int(a[1:])
         if a[0] == "a":
             ask(t)
+        elif a[0] == "c":
+            select("IDF", T.IDF[:, :], T.ones[:, 0:128], [[-1, 128]], Op.is_equal, 0.0, 0, 1, "")
+        elif a[0] == "w":
+            send(rank - t, T["Wl%d" % t][:, :], T.W[:, :], "w%d" % t, u(4, 0) + " U41")
         elif a[0] == "p":
             send(rank + 5, T.pr[:, :], T.pl5[:, :], "p5", "pl5")
+        elif a[0] == "l":
+            send(rank - 5, half(T.rl5, t, 128), half(T.ra5, t, 128), "rs5" + "ab"[t], "ra5%d" % t)
         else:
             send(rank - t, T["rl%d" % t][:, :], T["ra%d" % t][:, :], "rs%d" % t, "ra%d" % t)
 

@@ -3,42 +3,51 @@ from concourse.bass import DstId, RemoteDMATransfer
 from concourse.mybir import dt, AluOpType, AxisListType, ActivationFunctionType
 
 OPT = dict(
-    LV="g00 l1p g01 g1 A0 s0 A1 l0 f s1", FILL=("eu", "ea", "EE", "xf"),
-    VO="R00 R01 X s00 P0 s01 p00 b0 p01  R10 R11 P1 s10 c0 s11 p10 X0 b1 p11  R20 R21 c1 e5 s20 X1 Q0 s21 p20 b2 p21  "
-       "R30 R31 c2 Q1 s30 s31 X2 p30 p31  c3 b3 R4 X3 a1 s4 b4 p4 c4 X4 a2 a3  R5 a4 b5 X5 a50 a51",
-    SO="v1 B10 B11 v2 B20 m0 B21 v3 B30 C0 B31 k4 M8 m1 m2 k1 M12 m3 k2 m4 k3 b1 m5 b2 b3 a0 b4 b0 b5",
-    G="w2 w3 w4 c1 a0 a1 a2 a3 p5 a4 r1 r2 r3 r4 l0 l1")
+    LY="nx32 nxl1 e", LS="nxl0 vs0 x",
+    CUT=(0, 256, 512),
+    TO="40 x10 x11 41 i10 i11 x20 J00 x21 i20 42 43 J01 i21 x30 x31 I0 o0 20 I1 21 30 31 32  a00 a01 b0 J10 o1 J11 c0 sx  "
+       "a10 a11 b1 J20 I2 o2 J21 c1  a20 a21 b2 J30 I3 o3 J31 c2  a30 a31 b3 J40 I4 o4 J41 c3  a40 a41 b4 I5 o5 c4  rb0 ra0 b5 rl1 rl2",
+    VO="ones Gb0 idr0 bt1 ci bt2 bt3 ID1 cz lowf lowt cq nxb icol low set1 bq nxt oc0 lst0 A0b  "
+       "g00 g01 B10 S10 B11 m1 l10 eu S11  g100 l11 g101 g11 S20 B20 MT l20 B21 S21  g200 l21 g201 g21 S30 EE l30 B31 S31  g300 l31 g301 g31  "
+       "P0 R00 R01 P1 s00 xc s01 p00 b0 p01  R10 R11 X0 s10 Q0 s11 p10 b1 p11  R20 R21 X1 s20 Q1 s21 p20 b2 p21  "
+       "R30 R31 X2 a10 s30 a11 s31 p30 b3 p31  R40 R41 X3 a20 s40 s41 b4 p4 c4 X40 a21 X41  R5 a3 b5 a40 X5 a41 a5",
+    YO="ra5 rl3 rl4",
+    SO="D40 C70 CV0 idr1 z0 D4 C20 B0 DM0 A0a bcol v1 k1 ocol DM v2 setc C1 v3 m0 k4 B30 M8 D80 zb m1 D8 C0 m2 M12 k2 m3 k3 IDF "
+       "zc zd t1 m4 t0 t2 m5 a0 t3 t4 t5",
+    G="Gb L4 C7 b4 IDN CV1 CV L8 b8 C21 C2 T1 w10 w11 w2 w3 w4 q1 U1 w5 p1+q2 U2 T2 p2+q3 U3 r1 p3+q4 T3 p4 r2 r3 r40 r41")
 NR = 6
-NPOOL = 120
+NPOOL = 112
 ZB = 16
 WIN = ZB + 3 * 512
 FR = 4096.0
+E0 = 129 * 512.0
+UP = 65536.0
 BF, F32, I32, U16 = "bfloat16", "float32", "int32", "uint16"
 SCRATCH = {}
-for _n, _c, _d in (("nx32", 128, I32), ("nxb", 128, BF), ("nxl", 32, I32), ("nxt", 32, I32), ("ex", 128, I32), ("eu", 128, U16),
-                   ("pr", 16, U16), ("xf0", 16, F32), ("vbf", 512, BF), ("ones", 256, BF), ("c256", 64, BF),
+for _n, _c, _d in (("nx32", 128, I32), ("nxb", 128, BF), ("nxl", 32, I32), ("nxt", 32, I32), ("ex", 128, I32), ("eu", 128, U16), ("pr", 16, U16),
+                   ("vbf", 512, BF), ("vl", 512, BF), ("TC", WIN, F32), ("TD", WIN, F32), ("ones", 256, BF), ("c256", 64, BF), ("c0", 64, BF),
                    ("Gb", 512, BF), ("ID1", 128, BF), ("idr", 512, BF),
                    ("CV", 144, BF), ("CB", 144, BF), ("CO", 144, BF), ("C7", 144, BF), ("C2", 144, BF),
                    ("L4", 128, BF), ("b4", 64, BF), ("D4", 64, F32), ("L8", 128, BF), ("b8", 64, BF), ("D8", 64, F32),
-                   ("IDN", 128, BF), ("IDF", 128, F32), ("pc", 2, I32), ("ci", 2, I32), ("bt", 4, I32), ("c3", 1, I32),
-                   ("icol", 1, F32), ("n15", 1, F32), ("c15", 1, F32), ("setc", 1, F32), ("ocol", 1, F32), ("acol", 4, F32),
-                   ("bcol", 4, F32), ("en", 16, F32), ("m1", 16, F32), ("DM", 16, F32), ("MT", 16, BF), ("ea", 96, I32),
-                   ("EE", 96, F32), ("XU", 192, U16), ("XR", 192, U16), ("W", 512, BF), ("mask", 1536, BF),
-                   ("TA", WIN + ZB, F32), ("TB", WIN, F32), ("yb", 256, F32)):
+                   ("IDN", 128, BF), ("IDF", 128, F32), ("pc", 2, I32), ("ci", 1, I32), ("bt", 4, I32), ("c3", 1, I32),
+                   ("icol", 1, F32), ("low", 5, F32), ("c15", 1, F32), ("setc", 2, F32), ("ocol", 2, F32), ("bq", 4, F32),
+                   ("bcol", 4, F32), ("en", 16, F32), ("m1", 16, F32), ("DM", 16, F32), ("MT", 16, BF),
+                   ("XU", 192, U16), ("XR", 192, U16), ("W", 512, BF), ("mask", 1536, BF),
+                   ("TA", WIN, F32), ("TB", WIN, F32), ("yb", 256, F32)):
     SCRATCH[_n] = ("sbuf", [128, _c], _d)
 for _n in range(6):
-    for _b, _c, _d, _k in (("A", 512, BF, (0, 1, 2, 3)), ("B", 512, BF, (0, 1, 2, 3)), ("U", 512, BF, (1, 2, 3)),
+    for _b, _c, _d, _k in (("A", 512, BF, (0,)), ("B", 512, BF, (0, 1, 2, 3)), ("U", 512, BF, (1, 2, 3)),
                            ("vs", 512, BF, (1, 2, 3)), ("scl", 128, F32, (1, 2, 3)), ("lst", 32, U16, (0, 1, 2, 3)),
-                           ("Wl", 512, BF, (1, 2, 3, 4)), ("ra", 256, F32, range(6)), ("rb", 256, F32, range(6)),
-                           ("pl", 16, U16, range(1, 6)), ("R", 256, BF, range(6)), ("sa", 128, F32, range(5)), ("sb", 128, F32, range(6)),
-                           ("rl", 256, F32, range(1, 6))):
+                           ("Wl", 512, BF, range(1, 6)), ("ra", 256, F32, range(6)), ("rb", 256, F32, range(6)),
+                           ("pl", 16, U16, range(1, 6)), ("R", 256, BF, range(6)), ("sa", 128, BF, range(5)),
+                           ("rl", 256, F32, range(1, 6)), ("rm", 256, F32, (4, 5))):
         if _n in _k:
             SCRATCH["%s%d" % (_b, _n)] = ("sbuf", [128, _c], _d)
 for _n in ("psL0", "psL1", "psL2", "psL3", "psE0", "psE1", "psE2", "psT"):
     SCRATCH[_n] = ("psum", [128, 512], F32)
 
-SEMAPHORES = (["s%d" % k for k in range(NPOOL)] + ["loc", "e5", "p5", "w1a", "rs5a", "rs5b"] + ["w%d" % k for k in range(1, 5)]
-              + ["rp%d" % k for k in range(1, 5)] + ["rq%d" % k for k in range(1, 6)] + ["rs%d" % k for k in range(1, 5)])
+SEMAPHORES = (["s%d" % k for k in range(NPOOL)] + ["loc", "e5", "n5", "U1", "U2", "U3", "T1", "T2", "T3", "w10", "w11", "r40", "r41", "r50", "r51"]
+              + ["%s%d" % (a, k) for a in "wpqr" for k in range(1, 6)])
 
 
 def rank_program(g, core, T, topo):
@@ -69,207 +78,258 @@ def rank_program(g, core, T, topo):
 
     es = topo.engines(core, [c for c in T.cores if c != core][0])
     n_arr = len(es)
-    U = [None, T.U1, T.U2, T.U3, T.W]
+    U = [T.A0, T.U1, T.U2, T.U3, T.W]
     vs = [T.vbf, T.vs1, T.vs2, T.vs3]
-    bank_l = ["psL%d" % (2 * (n % 2) + h) for n in range(3) for h in (0, 1)]
+    CUT = OPT["CUT"]
+    NP = len(CUT) - 1
+
+    def piece(t, k, n=1):
+        return t[:, CUT[k] // n:CUT[k + 1] // n]
+
     bank_a = ["psL2", "psL3"]
     bank_b = ["psL%d" % (t % 2) for t in range(6)]
     bank_p = {2: "psT", 3: "psE2", 4: "psE0"}
-    tables_a, tables_b = "z0 z1 P1 P2 P3", "zb P4 P80 P81 P120 P121"
+    p8, p12 = [" ".join("P%d%d" % (e, h) + (" P%d%dq" % (e, h) if "%s%d0" % (c, h) in OPT["VO"].split() else "") for h in (0, 1))
+               for e, c in ((8, "P"), (12, "Q"))]
+    tables_a, tables_b = "z0 P1 P2 P3", "zb P4 " + p8 + " " + p12
 
-    y_dma("nx32", lambda: Y.dma_start(T.nx32[0:32, :], T.nx[:, :]))
-    y_dma("nxl1", lambda: Y.dma_start(T.nxl[:, 16:32], T.nx[1::2, :]))
-    y_dma("e", lambda: Y.dma_start(T.ex[:, 0:96], T.e[:, :]))
+    tc, td = "T2" in OPT["G"], "U2" in OPT["G"]
+    share = {}
+    for a in OPT["G"].split():
+        names = a.split("+")
+        for k, x in enumerate(names):
+            share[x] = n_arr // {1: 1, 2: 2, 3: 2 if k == 0 else 4, 4: 4}[len(names)]
+
+    def got(a):
+        return a, share[a]
+
+    def arrival(r, h=None):
+        if r[1] in "ab":
+            return r, []
+        return "", [got("r" + r[2] + ("%d" % h if "r" + r[2] + "0" in share else ""))]
+
+    def term(queue, a):
+        a, _, more = a.partition("+")
+        kind, t, h = a[0], int(a[1]), int(a[2]) if len(a) > 2 else None
+        c = 32 * t + 16 * (kind == "a")
+        at_home = t == 0 or (kind, t) == ("a", 5) or (t == 5 and td)
+        i = half((T.XU if at_home else T.XR)[:, c:c + 16], h, 8)
+        name = ("ra" if kind == "a" else "rb") + "%d" % t
+        win = (T.TA if kind == "a" else T.TB)[:, :]
+        deps = (tables_a if kind == "a" else tables_b) + " " + {"a0": "X0", "t0": "X0"}.get(a[:2], "")
+        rem = [] if at_home else [got(("p%d" if kind == "a" else "q%d") % t)]
+        if a[:2] == "a5" and tc:
+            win, deps, rem = T.TC[:, :], "zc X5" + ("" if "T1" in share else " Pc1"), [got(x) for x in share if x[0] == "T"]
+        elif a[:2] == "a5":
+            deps += " X5"
+        elif a[:2] == "t5" and td:
+            win, deps, rem = T.TD[:, :], "zd X41", [got(x) for x in share if x[0] == "U"]
+        out = half(T[name], h, 128)
+        if queue == "s":
+            return sca("r" + "ab"[kind == "t"] + tag(t, h), lambda: S.activation(out, win.indirect(i), AF.Copy), deps, rem)
+        more = more or "rb%d" % t
+        d, r = arrival(more)
+        vec("r" + "ab"[kind == "t"] + tag(t, h), lambda: V.tensor_tensor(out, win.indirect(i), half(T[more], h, 128), Op.add), deps + " " + d, rem + r)
+
+    loads = {"nx32": (T.nx32[0:32, :], T.nx[:, :]), "nxl0": (T.nxl[:, 0:16], T.nx[0::2, :]), "nxl1": (T.nxl[:, 16:32], T.nx[1::2, :]),
+             "vs0": (T.vbf[:, :], T.v[:, :]), "e": (T.ex[:, 0:96], T.e[:, :]), "x": (T.ex[:, 96:112], T.x[:, :])}
+    for a in OPT["LY"].split():
+        y_dma(a, lambda a=a: Y.dma_start(*loads[a]))
     y_dma("y0", lambda: Y.dma_start(T.y[:, 0:128], T.yb[:, 0:128]), "yb0")
     y_dma("end", [], "y0 y1")
 
-    def scan(name, out, b, deps, k=4):
-        vec(name, lambda: V.tensor_tensor_scan(out, T["D%d" % k][:, :], T[b][:, 0:64], 0.0, Op.mult, Op.max), "D%d " % k + deps)
+    def scan(name, out, b, deps, w=64):
+        vec(name, lambda: V.tensor_tensor_scan(out, T.D4[:, 0:w], T[b][:, 0:w], 0.0, Op.mult, Op.max), "D4 " + deps)
 
-    vec("ones", lambda: V.memset(T.ones[:, :], 1.0))
-    vec("Gb0", lambda: V.memset(T.Gb[0:32, 0::2], 0.0))
-    vec("idr0", lambda: V.tensor_tensor_scan(T.idr[:, 0:256], T.ones[:, :], T.ones[:, :], -257.0, Op.mult, Op.add), "ones")
-    vec("ci", lambda: V.tensor_scalar(T.ci[:, :], T.pc[:, :], 15, None, Op.bitwise_and), "pc")
-    vec("c3", lambda: V.tensor_scalar(T.c3[:, :], T.pc[:, 1:2], 3, None, Op.bitwise_and))
-    for n in range(1, 4):
-        vec("bt%d" % n, lambda n=n: V.tensor_scalar(T.bt[:, n:n + 1], T.pc[:, 0:1], n, 1, Op.logical_shift_right, Op.bitwise_and))
-    vec("c15", lambda: V.tensor_scalar(T.c15[:, :], T.ci[:, 1:2], 0.0, None, Op.is_equal), "ci")
-    vec("n15", lambda: V.tensor_scalar(T.n15[:, :], T.ci[:, 1:2], 1.0, None, Op.is_ge))
-    vec("setc", lambda: V.tensor_scalar(T.setc[:, :], T.c3[:, :], 0.0, FR, Op.is_equal, Op.mult), "c3")
-    vec("ocol", lambda: V.tensor_scalar(T.ocol[:, :], T.c3[:, :], 512.0, None, Op.mult))
-    vec("icol", lambda: V.tensor_copy(T.icol[:, :], T.ci[:, 1:2]))
-    vec("en", lambda: V.tensor_tensor_scan(T.en[:, :], T.ones[:, 0:16], T.ones[:, 0:16], -1.0, Op.mult, Op.add))
-    vec("acol", lambda: V.tensor_scalar(T.acol[:, 1:4], T.bt[:, 1:4], T.n15[:, 0:1], None, Op.mult), "n15 bt1 bt2 bt3")
-    vec("nxb", lambda: V.tensor_scalar(T.nxb[0:32, :], T.nx32[0:32, :], -256.0, None, Op.add), "nx32")
-    vec("DM0", lambda: V.tensor_scalar(T.DM[:, :], T.D4[:, 0:16], T.setc[:, 0:1], 1.0 / FR, Op.mult, Op.mult), "D4 setc")
-    vec("m1", lambda: V.tensor_scalar(T.m1[:, :], T.en[:, :], T.icol[:, 0:1], None, Op.is_equal), "en icol")
-    vec("CV0", lambda: V.memset(T.CV[:, :], 0.0))
-    vec("nxt", lambda: V.transpose(T.nxt[:, :], T.nxl[:, :]), "nxl0 nxl1")
-    vec("DM", lambda: V.tensor_scalar(T.DM[:, 1::4], T.DM[:, 1::4], 1.0 / FR, None, Op.mult), "DM0")
-    vec("C20", lambda: V.memset(T.C2[:, :], 0.0))
-    vec("lst0", lambda: V.tensor_copy(T.lst0[:, :], T.nxt[:, :]), "nxt")
-    vec("A0b", lambda: V.tensor_scalar(half(T.A0, 1), T.psE1[:, 0:256], T.n15[:, 0:1], None, Op.mult), "nx1 n15")
-    vec("MT", lambda: V.tensor_tensor_scan(T.MT[:, :], T.DM[:, :], T.m1[:, :], 0.0, Op.mult, Op.add), "DM m1")
+    def bit(n):
+        return lambda: V.tensor_scalar(T.bt[:, n:n + 1], T.pc[:, 0:1], n, 1, Op.logical_shift_right, Op.bitwise_and), "pc"
 
     small = {
-        "eu": lambda: vec("eu", lambda: V.tensor_copy(T.eu[:, 0:112], T.ex[:, 0:112]), "e x"),
-        "ea": lambda: vec("ea", lambda: V.tensor_scalar(T.ea[:, :], T.ex[:, 0:96], 2, None, Op.logical_shift_right), "e"),
-        "EE": lambda: vec("EE", lambda: V.tensor_scalar(T.EE[:, :], T.ea[:, :], 512.0, None, Op.mult), "ea"),
-        "xf": lambda: vec("xf0", lambda: V.tensor_tensor(T.xf0[:, :], T.ex[:, 96:112], T.EE[:, 0:16], Op.add), "x EE"),
-        "X": lambda: vec("X", lambda: V.tensor_scalar(T.XU[:, 0:16], T.xf0[:, :], ZB - 511.75, None, Op.add), "xf0"),
-        "e5": lambda: vec("eu5", lambda: V.tensor_copy(T.eu[:, 112:128], T.ex[:, 112:128]), "", [("e5", n_arr)]),
+        "ones": (lambda: V.memset(T.ones[:, :], 1.0), ""),
+        "Gb0": (lambda: V.memset(T.Gb[0:32, 0::2], 0.0), ""),
+        "idr0": (lambda: V.tensor_tensor_scan(T.idr[:, 0:256], T.ones[:, :], T.ones[:, :], -257.0, Op.mult, Op.add), "ones"),
+        "ID1": (lambda: V.tensor_tensor_scan(T.ID1[0:1, :], T.ones[0:1, 0:128], T.ones[0:1, 0:128], 0.0, Op.subtract, Op.mult), "ones"),
+        "ci": (lambda: V.tensor_scalar(T.ci[:, :], T.pc[:, 1:2], 15, None, Op.bitwise_and), "pc"),
+        "cq": (lambda: V.tensor_scalar(T.c3[:, :], T.pc[:, 1:2], 3, None, Op.bitwise_and), "pc"),
+        "bt1": bit(1), "bt2": bit(2), "bt3": bit(3),
+        "lowt": (lambda: V.tensor_scalar(T.low[:, 1:4], T.bt[:, 1:4], 1.0 - 1.0 / UP, 1.0 / UP, Op.mult, Op.add), "bt1 bt2 bt3"),
+        "lowf": (lambda: V.tensor_scalar(T.low[:, 0:1], T.ci[:, :], 1.0, UP ** -4, Op.min, Op.max), "ci"),
+        "low": (lambda: V.tensor_reduce(T.low[:, 4:5], T.low[:, 0:4], AxisListType.X, Op.mult), "lowt lowf"),
+        "bq": (lambda: V.tensor_scalar(T.bq[:, 1:4], T.low[:, 1:4], T.low[:, 0:1], 0.5, Op.mult, Op.is_lt), "lowt lowf"),
+        "cz": (lambda: V.tensor_scalar(T.c15[:, :], T.ci[:, :], 0.0, UP ** -3, Op.is_equal, Op.mult), "ci"),
+        "set1": (lambda: V.tensor_scalar(T.setc[:, 1:2], T.c3[:, :], 0.0, None, Op.is_equal), "cq"),
+        "oc0": (lambda: V.tensor_scalar(T.ocol[:, 1:2], T.c3[:, :], 512.0, E0, Op.mult, Op.add), "cq"),
+        "icol": (lambda: V.tensor_copy(T.icol[:, :], T.ci[:, :]), "ci"),
+        "m1": (lambda: V.tensor_scalar(T.m1[:, :], T.idr[:, 256:272], T.icol[:, 0:1], None, Op.is_equal), "idr1 icol"),
+        "MT": (lambda: V.tensor_tensor_scan(T.MT[:, :], T.DM[:, :], T.m1[:, :], 0.0, Op.mult, Op.add), "DM m1"),
+        "nxb": (lambda: V.tensor_scalar(T.nxb[0:32, :], T.nx32[0:32, :], -256.0, None, Op.add), "nx32"),
+        "nxt": (lambda: V.transpose(T.nxt[:, :], T.nxl[:, :]), "nxl0 nxl1"),
+        "lst0": (lambda: V.tensor_copy(T.lst0[:, :], T.nxt[:, :]), "nxt"),
+        "A0b": (lambda: V.tensor_scalar(half(T.A0, 1), T.psE1[:, 0:256], T.low[:, 4:5], None, Op.mult), "nx1 low"),
+        "eu": (lambda: V.tensor_copy(T.eu[:, 0:112], T.ex[:, 0:112]), "e x"),
+        "EE": (lambda: V.tensor_scalar(T.idr[:, 3:384:4], T.ex[:, 0:96], 128.0, E0 - 192.0, Op.mult, Op.add), "e B0 nx0 nx1 m1"),
+        "xc": (lambda: V.tensor_scalar(T.idr[:, 387:448:4], T.ex[:, 96:112], -256.0, None, Op.add), "x B0 nx0 nx1"),
+        "eu5": (lambda: V.tensor_copy(T.eu[:, 112:128], T.ex[:, 112:128]), "", [] if tc else [got("e5")]),
     }
 
-    def u(m, h):
-        return "U%d%d" % (m, h) + (" U%d0q" % m if h == 0 and m > 1 else "")
+    def u(m, h=None):
+        if h is None:
+            return " ".join(u(m, k) for k in range(NP))
+        return "U%d%d" % (m, h) + (" U%d%dq" % (m, h) if "g%d%d0" % (m - 1, h) in OPT["VO"].split() else "")
 
     def compose(n, h, q=None):
-        A, B, L = T["A%d" % n], T["B%d" % n], T["lst%d" % n]
-        lo, w = (256 * h, 256) if q is None else (256 * h + 128 * q, 128)
+        B, L = T["B%d" % n], T["lst%d" % n]
+        lo, w = CUT[h], CUT[h + 1] - CUT[h]
+        if q is not None:
+            lo, w = lo + w // 2 * q, w // 2
         vec("U%d%d" % (n + 1, h) + ("q" if q == 0 else ""),
-            lambda: V.tensor_tensor(U[n + 1][:, lo:lo + w], A[:, :].indirect(L[:, lo // 16:(lo + w) // 16]), B[:, lo:lo + w], Op.add),
-            "A0a A0b B0 lst0" if n == 0 else "A%d0 A%d1 B%d%d lst%d%d" % (n, n, n, h, n, h))
+            lambda: V.tensor_tensor(U[n + 1][:, lo:lo + w], U[n][:, :].indirect(L[:, lo // 16:(lo + w) // 16]), B[:, lo:lo + w], Op.add),
+            "A0a A0b B0 lst0" if n == 0 else "%s B%d%d lst%d%d" % (u(n), n, h, n, h))
 
     def window(m, h):
-        vec("A%d%d" % (m, h), lambda: V.tensor_scalar(half(T["A%d" % m], h), half(U[m], h), T.acol[:, m:m + 1], None, Op.mult),
-            u(m, h) + " acol")
+        vec("B%d%d" % (m, h), lambda: V.tensor_scalar(piece(T["B%d" % m], h), piece(U[m], h), T.bcol[:, m:m + 1], None, Op.mult),
+            u(m, h) + " bcol")
+
+    def keep_v(k, q):
+        vec("P%d" % k + ("" if q == 3 else "q%d" % q), lambda: V.tensor_copy(half(slot(T.TA, k), q, 128), half(T[bank_p[k]], q, 128)),
+            "sum%d%d" % (k, k - 1) + ("" if q < 3 else " P%dq0 P%dq1 P%dq2" % (k, k, k)))
+
+    def consts_v(k):
+        c, col = (("CB", "setc"), ("CO", "ocol"))[k]
+        vec(c, lambda: V.tensor_scalar(T[c][:, :], T.CV[:, :], T[col][:, 0:1], None, Op.mult), "CV " + col)
 
     def scan_l(m, h):
-        scan("scl%d%d" % (m, h), half(T["scl%d" % m], h, 64), bank_l[2 * m - 2 + h], "xl%d%d" % (m, h))
+        scan("scl%d%d" % (m, h), piece(T["scl%d" % m], h, 4), "psL%d" % h, "xl%d%d" % (m, h), w=(CUT[h + 1] - CUT[h]) // 4)
 
     def to_list(m, h):
-        vec("lst%d%d" % (m, h), lambda: V.tensor_copy(half(T["lst%d" % m], h, 16), half(T["scl%d" % m], h, 64)[:, 3::4]), "scl%d%d" % (m, h))
-
-    for n in range(4):
-        for a in OPT["LV"].split():
-            if a == "f":
-                small[OPT["FILL"][n]]()
-            elif a[0] == "g":
-                if n:
-                    compose(n, *[int(x) for x in a[1:]])
-                elif a != "g01":
-                    compose(n, int(a[1]))
-            elif 0 < n + 1 - (a[-1] == "p") < 4:
-                {"A": window, "s": scan_l, "l": to_list}[a[0]](n + 1 - (a[-1] == "p"), int(a[1]))
+        vec("lst%d%d" % (m, h), lambda: V.tensor_copy(piece(T["lst%d" % m], h, 16), piece(T["scl%d" % m], h, 4)[:, 3::4]), "scl%d%d" % (m, h))
 
     def visit(t, h=None):
-        Wt = T.W if t in (0, 5) else T["Wl%d" % t]
-        pl = half(T.pr[:, :] if t == 5 else T["pl%d" % t][:, :] if t else T.eu[:, 96:112], h, 8)
+        Wt = T["Wl%d" % t] if t else T.W
+        pl = half(T["pl%d" % t][:, :] if t else T.eu[:, 96:112], h, 8)
+        if t == 5 and not tc:
+            return vec("R5", lambda: V.tensor_tensor(T.R5[:, :], T.W[:, :].indirect(T.pr[:, :]), half(T.mask, 5), Op.mult),
+                       "mask5 " + u(4), [got("n5")])
         vec("R" + tag(t, h), lambda: V.tensor_tensor(half(T["R%d" % t], h, 128), Wt[:, :].indirect(pl), half(half(T.mask, t), h, 128), Op.mult),
-            u(4, 0) + " U41 mask%d " % t + {0: "eu", 4: "pl40 pl41", 5: ""}.get(t, "pl" + tag(t, h)),
-            [(s, n_arr) for s in {0: [], 1: ["w1a", "w1"], 5: ["p5"]}.get(t, ["w%d" % t])])
+            "mask%d " % t + ("pl" + tag(t, h) if t else u(4) + " eu"),
+            [got(s) for s in share if s[:2] == "w%d" % t])
 
-    def places(t, h=None):
-        return T.sa4[:, 3:64:4] if t == 4 else half(T["sa%d" % t], h, 64)[:, 7::8]
-
-    def scan_a(t, h=None):
-        scan("sa" + tag(t, h), half(T["sa%d" % t], h or 0, 64), bank_a[h or 0], "xa" + tag(t, h), 4 if h is None else 8)
+    def scan_a(t, h):
+        vec("sa" + tag(t, h), lambda: V.tensor_tensor_scan(half(T["sa%d" % t], h, 64), T.D8[:, :], T[bank_a[h]][:, 0:64], 0.0, Op.add, Op.max),
+            "D8 xa" + tag(t, h))
 
     def place(t, h=None):
-        vec("pl" + tag(t + 1, h), lambda: V.tensor_scalar(half(T["pl%d" % (t + 1)], h, 8), places(t, h), 0.25, None, Op.add), "sa" + tag(t, h))
-
-    def add_a(t):
-        vec("sc%d" % t, lambda: V.tensor_tensor(T["sb%d" % t][:, 67::4], places(t), T.EE[:, 16 * t + 16:16 * t + 32], Op.add),
-            "EE " + ("sa4" if t == 4 else "sa%d0 sa%d1" % (t, t)))
+        vec("pl" + tag(t + 1, h), lambda: V.tensor_scalar(half(T["pl%d" % (t + 1)], h, 8), half(T["sa%d" % t], h, 64)[:, 7::8], 256.25, None, Op.add),
+            "sa" + tag(t, h) if h is not None else "sa%d0 sa%d1" % (t, t))
 
     def scan_b(t):
-        scan("sb%d" % t, T["sb%d" % t][:, 0:64], bank_b[t], "xb%d" % t)
+        scan("sb%d" % t, T[bank_b[t]][:, 128:192], bank_b[t], "xb%d" % t)
 
-    def offsets(t):
-        c, n = 32 * t + 16, 128 if t < 5 else 64
-        vec("X%d" % t, lambda: V.tensor_scalar(T.XU[:, c:c + n // 4], T["sb%d" % t][:, 3:n:4], ZB - 511.75, float(WIN), Op.add, Op.min),
-            "sb%d sc%d" % (t, t) if t < 5 else "sb5")
+    def add_v(t):
+        vec("sc%d" % t, lambda: V.tensor_tensor(T[bank_b[t]][:, 195:256:4], T["sa%d" % t][:, 7::8], T.idr[:, 64 * t + 67:64 * t + 128:4], Op.add),
+            "EE xb%d sa%d0 sa%d1" % (t, t, t))
 
-    def term_a(t, h=None):
-        i = half((T.XU if t == 5 else T.XR)[:, 32 * t + 16:32 * t + 32], h, 8)
-        vec("ra" + tag(t, h), lambda: V.tensor_tensor(half(T["ra%d" % t], h, 128), T.TA[:, :].indirect(i), half(T["rb%d" % t], h, 128), Op.add),
-            tables_a + " rb%d" % t + (" X5" if t == 5 else ""), [("rp%d" % t, n_arr // 2)] if t < 5 else [])
+    def offsets(t, h=None):
+        lo, hi = (192 if h == 1 else 64 if t == 0 else 128), (192 if t == 5 or h == 0 else 256)
+        c = 32 * t - 16
+        vec("X" + tag(t, h), lambda: V.tensor_scalar(T.XU[:, c + lo // 4:c + hi // 4], T[bank_b[t]][:, lo + 3:hi:4], ZB - 255.75 - E0, None, Op.add),
+            "sb%d" % t + (" sc%d" % t if hi == 256 else "") + (" sx" if t == 0 else ""))
 
-    def add4(e, h):
-        o = half(slot(T.TB, e // 4), h)
-        vec("P%d%d" % (e, h), lambda: V.tensor_tensor(o, o, half(T.psE0, h), Op.add), "M%d P4" % e)
+    def add4(e, h, q=None):
+        o, p = [half(half(t, h), q, 128) for t in (slot(T.TB, e // 4), T.psE0)]
+        vec("P%d%d" % (e, h) + ("q" if q == 0 else ""), lambda: V.tensor_tensor(o, o, p, Op.add), "M%d P4" % e)
 
     for a in OPT["VO"].split():
         if a in small:
-            small[a]()
+            vec(a, *small[a])
+        elif a[0] in "at":
+            term("v", a)
         else:
-            {"R": visit, "s": scan_a, "p": place, "c": add_a, "b": scan_b, "X": offsets, "a": term_a,
-             "P": lambda h: add4(8, h), "Q": lambda h: add4(12, h)}[a[0]](*[int(x) for x in a[1:]])
-    for t in (3, 4, 5):
-        for h in (0, 1):
-            o, name = (T.psE1, "acc%d%d" % (t, h)) if t < 5 else (T.yb, "yb%d" % h)
-            vec(name, lambda o=o, t=t, h=h: V.tensor_tensor(half(o, h, 128), half(T.psE1, h, 128), half(T["rl%d" % t], h, 128), Op.add),
-                "acc" if t == 3 else "acc%d%d" % (t - 1, h), [("rs%d" % t + ("ab"[h] if t == 5 else ""), n_arr)])
+            {"g": compose, "B": window, "S": scan_l, "l": to_list, "k": keep_v, "C": consts_v, "R": visit, "c": add_v, "s": scan_a, "p": place, "b": scan_b, "X": offsets,
+             "P": lambda *h: add4(8, *h), "Q": lambda *h: add4(12, *h)}[a[0]](*[int(x) for x in a[1:]])
+    last = {0: "acc", 1: "acc"}
+    adds = OPT["YO"].split()
+    for k, r in enumerate(adds):
+        for h in (1,) if r == "rm5" else (0, 1):
+            o, name = (T.psE1, "acc%d%d" % (k, h)) if k < len(adds) - 1 else (T.yb, "yb%d" % h)
+            d, rem = arrival(r, h)
+            vec(name, lambda o=o, r=r, h=h: V.tensor_tensor(half(o, h, 128), half(T.psE1, h, 128), half(T[r], h, 128), Op.add), last[h] + " " + d, rem)
+            last[h] = name
 
     def act(name, out, in_, deps, rem=(), **k):
         sca(name, lambda: S.activation(out, in_, AF.Copy, **k), deps, rem)
 
     def mask(t):
-        c = 16 * t if t < 5 else 112
-        act("mask%d" % t, half(T.mask, t), T.MT[:, :].indirect(T.eu[:, c:c + 16]), "MT eu" if t < 5 else "MT eu5")
+        c = 16 * t if t < 5 or tc else 112
+        act("mask%d" % t, half(T.mask, t), T.MT[:, :].indirect(T.eu[:, c:c + 16]), "MT eu" if c < 112 else "MT eu5")
 
     def keep(k):
         act("P%d" % k, slot(T.TA, k) if k < 4 else slot(T.TB, 1), T[bank_p[k]][:, :] if k > 1 else T.vbf[:, :],
             "sum%d%d" % (k, k - 1) if k > 1 else "vs0")
 
     def moved(e):
-        act("M%d" % e, slot(T.TB, e // 4), slot(T.TB, e // 4 - 1).indirect(T.lst2[:, :]), "P4 lst20 lst21" if e == 8 else "P80 P81")
+        act("M%d" % e, slot(T.TB, e // 4), slot(T.TB, e // 4 - 1).indirect(T.lst2[:, :]), "P4 " + " ".join("lst2%d" % k for k in range(NP)) if e == 8 else p8)
 
-    def consts(_):
-        act("CB", T.CB[:, :], T.CV[:, :], "CV setc", scale=T.setc[:, 0:1])
-        act("CO", T.CO[:, :], T.CV[:, :], "ocol", scale=T.ocol[:, 0:1])
+    def consts(n):
+        c, col = (("CB", "setc"), ("CO", "ocol"))[n]
+        act(c, T[c][:, :], T.CV[:, :], "CV " + col, scale=T[col][:, 0:1])
 
     def step_v(m):
         act("vs%d" % m, vs[m][:, :], vs[m - 1][:, :].indirect(T.lst0[:, :]), "lst0 vs%d" % (m - 1))
 
     def rest(mh):
         m, h = divmod(mh, 10)
-        act("B%d" % mh, half(T["B%d" % m], h), half(U[m], h), u(m, h) + " bcol", scale=T.bcol[:, m:m + 1])
+        act("B%d" % mh, piece(T["B%d" % m], h), piece(U[m], h), u(m, h) + " bcol", scale=T.bcol[:, m:m + 1])
 
-    def term_b(t):
-        act("rb%d" % t, T["rb%d" % t][:, :], T.TB[:, :].indirect((T.XR if t else T.XU)[:, 32 * t:32 * t + 16]),
-            tables_b + ("" if t else " X"), [("rq%d" % t, n_arr // (2 if t > 1 else 1))] if t else [])
-
-    s_dma("nxl0", lambda: S.dma_start(T.nxl[:, 0:16], T.nx[0::2, :]))
-    s_dma("vs0", lambda: S.dma_start(T.vbf[:, :], T.v[:, :]))
-    s_dma("x", lambda: S.dma_start(T.ex[:, 96:112], T.x[:, :]))
-    act("ID10", T.ID1[0:1, :], T.ones[0:1, 0:128], "ones")
-    act("D40", T.D4[:, :], T.ones[:, 0:64], "")
-    act("c256", T.c256[0:8, :], T.ones[0:8, 0:64], "", bias=256.0, scale=0.0)
-    act("ID1", T.ID1[0:1, 1::2], T.ones[0:1, 0:64], "ID10", scale=0.0)
-    act("idr1", T.idr[:, 256:512], T.idr[:, 0:256], "idr0", bias=256.0)
-    act("D4", T.D4[:, 0::4], T.ones[:, 0:16], "D40", scale=0.0)
-    act("C70", T.C7[:, :], T.ones[:, 0:144], "", scale=0.0)
-    act("B0", T.B0[:, :], T.idr[:, :], "c15 idr0 idr1", scale=T.c15[:, 0:1])
-    act("D80", T.D8[:, :], T.ones[:, 0:64], "")
-    act("bcol", T.bcol[:, 1:4], T.acol[:, 1:4], "acol", bias=1.0, scale=-1.0)
-    act("A0a", half(T.A0, 0), T.psE0[:, 0:256], "nx0 n15", scale=T.n15[:, 0:1])
-    act("D8", T.D8[:, 0::8], T.ones[:, 0:8], "D80", scale=0.0)
-    act("z0", T.TA[:, 0:ZB], T.ones[:, 0:ZB], "", scale=0.0)
-    act("z1", T.TA[:, WIN:WIN + ZB], T.ones[:, 0:ZB], "", scale=0.0)
-    act("zb", T.TB[:, 0:ZB], T.ones[:, 0:ZB], "", scale=0.0)
+    for a in OPT["LS"].split():
+        s_dma(a, lambda a=a: S.dma_start(*loads[a]))
+    fills = {
+        "D40": (T.D4[:, :], T.ones[:, 0:64], "ones", {}), "D4": (T.D4[:, 0::4], T.ones[:, 0:16], "D40", dict(scale=0.0)),
+        "D80": (T.D8[:, :], T.ones[:, 0:64], "ones", dict(scale=0.0)), "D8": (T.D8[:, 0::8], T.ones[:, 0:8], "D80", dict(scale=-1024.0 * FR)),
+        "idr1": (T.idr[:, 256:512], T.idr[:, 0:256], "idr0", dict(bias=256.0)),
+        "C70": (T.C7[:, :], T.ones[:, 0:144], "ones", dict(scale=0.0)), "CV0": (T.CV[:, :], T.ones[:, 0:144], "ones", dict(scale=0.0)),
+        "C20": (T.C2[:, :], T.ones[:, 0:144], "ones", dict(scale=0.0)),
+        "B0": (T.B0[:, :], T.idr[:, :], "cz idr0 idr1", dict(scale=T.c15[:, 0:1])),
+        "bcol": (T.bcol[:, 1:4], T.bq[:, 1:4], "bq", dict(scale=UP)), "setc": (T.setc[:, 0:1], T.setc[:, 1:2], "set1", dict(scale=FR)),
+        "DM0": (T.DM[:, :], T.D4[:, 0:16], "D4 set1", dict(scale=T.setc[:, 1:2])), "DM": (T.DM[:, 1::4], T.DM[:, 1::4], "DM0", dict(scale=1.0 / FR)),
+        "A0a": (half(T.A0, 0), T.psE0[:, 0:256], "nx0 low", dict(scale=T.low[:, 4:5])),
+        "z0": (T.TA[:, 0:ZB], T.ones[:, 0:ZB], "ones", dict(scale=0.0)), "zb": (T.TB[:, 0:ZB], T.ones[:, 0:ZB], "ones", dict(scale=0.0)),
+        "zc": (T.TC[:, 0:ZB], T.ones[:, 0:ZB], "ones", dict(scale=0.0)), "zd": (T.TD[:, 0:ZB], T.ones[:, 0:ZB], "ones", dict(scale=0.0)),
+    }
     for a in OPT["SO"].split():
-        if a == "a0":
-            act("ra0", T.ra0[:, :], T.TA[:, :].indirect(T.XU[:, 16:32]), tables_a + " X0")
+        if a in fills:
+            act(a, *fills[a][:3], **fills[a][3])
+        elif a == "K1":
+            act("Pc1", slot(T.TC, 1), T.vl[:, :], "", [got("e5")])
+        elif a == "IDF":
+            act("IDF", T.IDF[:, :], T.IDN[:, :], "IDN")
+        elif a == "ocol":
+            sca(a, lambda: S.activation(T.ocol[:, 0:1], T.setc[:, 1:2], AF.Identity, bias=T.ocol[:, 1:2], scale=-256.0 * FR - E0), "set1 oc0")
+        elif a[0] in "at":
+            term("s", a)
         else:
-            {"m": mask, "k": keep, "M": moved, "v": step_v, "B": rest, "C": consts, "b": term_b}[a[0]](int(a[1:]))
+            {"m": mask, "k": keep, "M": moved, "v": step_v, "B": rest, "C": consts}[a[0]](int(a[1:]))
     s_dma("y1", lambda: S.dma_start(T.y[:, 128:256], T.yb[:, 128:256]), "yb1")
 
-    def bias(b, deps="", k=4):
-        pe(None, lambda: P.matmul(T[b][:, 0:64], T["L%d" % k][0:k, :], T["b%d" % k][0:k, :], start=True, stop=False),
+    def bias(b, deps="", k=4, w=64):
+        pe(None, lambda: P.matmul(T[b][:, 0:w], T["L%d" % k][0:k, :], T["b%d" % k][0:k, 0:w], start=True, stop=False),
            "L%d b%d %s" % (k, k, deps))
 
-    def extract(name, b, rows, c, deps, stop=True, n=4):
-        pe(name, [lambda s=s: P.matmul(T[b][:, 0:64], c[:, n - 1 - s:n + 127 - s], rows[:, s::n], start=False, stop=(stop and s == n - 1))
+    def extract(name, b, rows, c, deps, stop=True, n=4, w=64):
+        pe(name, [lambda s=s: P.matmul(T[b][:, 0:w], c[:, n - 1 - s:n + 127 - s], rows[:, s::n], start=False, stop=(stop and s == n - 1))
                   for s in range(n)], deps)
 
-    def plus(k, i, deps=""):
-        pe("sum%d%d" % (k, i), lambda: P.matmul(T[bank_p[k]][:, :], T.IDN[:, :], vs[i][:, :], start=(i == 0), stop=(i == k - 1)),
-           "IDN vs%d %s" % (i, deps))
+    taken = {2: 0, 3: 0, 4: 0}
 
-    def total(r, name=None):
-        pe(name, lambda: P.matmul(T.psE1[:, 0:256], T.IDF[:, :], T[r][:, :], start=(r == "ra0"), stop=bool(name)),
-           "IDF A0b" + ("" if r[1] == "l" else " " + r), [("rs" + r[2], n_arr)] if r[1] == "l" else [])
+    def plus(k, i):
+        n = taken[k]
+        taken[k] += 1
+        pe("sum%d%d" % (k, n), lambda: P.matmul(T[bank_p[k]][:, :], T.IDN[:, :], vs[i][:, :], start=(n == 0), stop=(n == k - 1)),
+           "IDN vs%d %s" % (i, "A0a" if k == 4 else ""))
+
+    def add_a(name, t, c, places, v, deps):
+        pe(name, [lambda k=k, r=r: P.matmul(T[bank_b[t]][:, c:c + 64], T.IDN[:, :], r, start=(k == 0), stop=(k == 1))
+                  for k, r in enumerate((T.idr[:, 64 * v:64 * v + 64], places))], "EE " + deps)
 
     for h in (0, 1):
         pe(None, lambda h=h: P.matmul(T["psE%d" % h][:, 0:256], T.ID1[0:1, :], T.idr[0:1, 256 * h:256 * h + 256], start=True, stop=False),
@@ -277,100 +337,117 @@ def rank_program(g, core, T, topo):
     for h in (0, 1):
         pe("nx%d" % h, [lambda h=h, q=q: P.matmul(half(T["psE%d" % h], q, 128), half(T.Gb[0:32, :], 2 * h + q, 128), T.nxb[0:32, :],
                                                   start=False, stop=(q == 1)) for q in (0, 1)], "nxb Gb Gb0")
-    for k in range(4):
-        bias("psL%d" % k)
-    plus(4, 0, "A0a")
-    for n in range(3):
-        for h in (0, 1):
-            extract("xl%d%d" % (n + 1, h), bank_l[2 * n + h], half(U[n + 1], h), T.C7, u(n + 1, h) + " C7")
-        plus(4, n + 1)
-        for h in (0, 1):
-            if n != 1:
-                bias(bank_l[2 * n + h], "scl%d%d" % (n + 1, h))
-    for h in (0, 1):
-        bias(bank_a[h], "scl2%d" % h, 8)
-    for t in range(6):
-        extract(None, bank_b[t], half(T.mask, t), T.CO, "mask%d CO" % t, stop=False)
-        if t == 0:
-            plus(2, 0)
-            plus(2, 1)
-            plus(3, 0)
-        if t < 4:
-            for h in (0, 1):
-                extract("xa%d%d" % (t, h), bank_a[h], half(T["R%d" % t], h, 128), T.C2, "R%d%d C2" % (t, h), n=2)
-            extract("xb%d" % t, bank_b[t], T["R%d" % t], T.CB, "CB")
-            bias(bank_a[0], "sa%d0" % t, 8 if t < 3 else 4)
-            if t < 3:
-                bias(bank_a[1], "sa%d1" % t, 8)
-        elif t == 4:
-            extract("xa4", bank_a[0], T.R4, T.CV, "R4 CV")
-            extract("xb4", bank_b[4], T.R4, T.CB, "")
+    opened = {k: 0 for k in range(NP)}
+    for k in range(NP):
+        bias("psL%d" % k, w=(CUT[k + 1] - CUT[k]) // 4)
+    to = OPT["TO"].split()
+    sums = [r for r in to if r[0] == "r"]
+    for n, a in enumerate(to):
+        done = to[:n]
+        if a[0] == "r":
+            d, rem = arrival(a)
+            pe("acc" if a == sums[-1] else None,
+               lambda a=a: P.matmul(T.psE1[:, 0:256], T.IDF[:, :], T[a][:, :], start=(a == sums[0]), stop=(a == sums[-1])), "IDF A0b " + d, rem)
+            continue
+        if a == "sx":
+            add_a("sx", 0, 64, T.idr[:, 384:448], 0, "xc sb0")
+            continue
+        m, k = int(a[1]), int(a[-1])
+        if a[0] == "x":
+            assert opened[k] == m - 1
+            extract("xl%d%d" % (m, k), "psL%d" % k, piece(U[m], k), T.C7, u(m, k) + " C7", w=(CUT[k + 1] - CUT[k]) // 4)
+        elif a[0] == "i":
+            opened[k] = m
+            bias("psL%d" % k, "scl%d%d" % (m, k), w=(CUT[k + 1] - CUT[k]) // 4)
+        elif a[0] == "I":
+            bias(bank_b[m], "X%d" % (m - 2) if m > 1 else "scl3%d" % m)
+        elif a[0] == "J":
+            bias(bank_a[k], "sa%d%d" % (m - 1, k) if m else "scl3%d" % (2 + k) if 2 + k < NP else "", 8)
+        elif a[0] == "o":
+            assert "I%d" % m in done
+            extract(None, bank_b[m], half(T.mask, m), T.CO, "mask%d CO" % m, stop=False)
+        elif a[0] == "a":
+            assert "J" + a[1:] in done
+            extract("x" + a, bank_a[k], half(T["R%d" % m], k, 128), T.C2, "R%s C2" % a[1:], n=2)
+        elif a[0] == "b":
+            assert "o%d" % m in done
+            extract("x" + a, bank_b[m], T["R%d" % m], T.CB, "CB " + ("R5" if m == 5 else "R%d0 R%d1" % (m, m)))
+        elif a[0] == "c":
+            if a not in OPT["VO"].split():
+                add_a("sc%d" % m, m, 192, T["sa%d" % m][:, 1::2], m + 1, "sa%d0 sa%d1 sb%d" % (m, m, m) + (" X40" if m == 4 and "X40" in OPT["VO"] else ""))
         else:
-            total("ra0")
-            extract("xb5", bank_b[5], T.R5, T.CB, "R5")
-        if 0 < t < 5:
-            bias(bank_b[t + 1], "sb%d" % (t - 1))
-        if t < 2:
-            plus(3, t + 1)
-    total("rb0")
-    total("rl1")
-    total("rl2", "acc")
+            plus(int(a[0]), k)
 
     loc = [0]
 
-    def send(dst_rank, out, in_, sem, deps):
-        d = T.cores[dst_rank % NR]
-        rid, pid, _ = topo.addr(d)
-        loc[0] += n_arr
-        g_rem(None, lambda: g.remote_dma(out, in_, T.sem[sem], T.sem.loc, pid, rid, topo.mask(core, d)), deps)
+    def write(a):
+        t, h = int(a[1]), int(a[2]) if len(a) > 2 else None
+        if a[0] == "e":
+            return (rank - 5, T.vl[:, :], [T.vbf[:, :]], "vs0") if tc else (rank + 5, T.ex[:, 112:128], [T.ex[:, 80:96]], "e")
+        if a[0] == "w":
+            lo, hi = {None: (0, NP), 0: (0, NP - 1), 1: (NP - 1, NP)}[h]
+            return rank - t, T["Wl%d" % t][:, CUT[lo]:CUT[hi]], [T.W[:, CUT[lo]:CUT[hi]]], " ".join(u(4, k) for k in range(lo, hi))
+        if a[0] in "pq":
+            c = 32 * t + 16 * (a[0] == "p")
+            return rank + t, T.XR[:, c:c + 16], [T.XU[:, c:c + 16]], "X%d" % (t - (a[0] == "q")) + ("0" if a == "p4" and "X40" in OPT["VO"] else "1" if a == "q5" and "X41" in OPT["VO"] else "")
+        if a[0] == "n":
+            return rank + 5, T.pr[:, :], [T.pl5[:, :]], "pl5" if "p4" in OPT["VO"].split() else "pl50 pl51"
+        if a[0] == "T":
+            return rank - 5, slot(T.TC, t), [slot(T.TA, t)], "P%d" % t
+        if a[0] == "U":
+            return rank - 5, slot(T.TD, t), [slot(T.TB, t)], ("P4", p8, p12)[t - 1]
+        r = "rb5" if t == 5 and tc else "ra%d" % t
+        deps = "%s0 %s1" % (r, r) if h is None and ("t50" if r == "rb5" else "a%d0" % t) in (OPT["VO"] + " " + OPT["SO"]).split() else r + a[2:]
+        if "a" + a[1:] in OPT["SO"].split():
+            return rank - t, half(T["rl%d" % t], h, 128), [half(T[r], h, 128), half(T["rb%d" % t], h, 128)], deps + " rb%d" % t
+        return rank - t, half(T["rl%d" % t], h, 128), [half(T[r], h, 128)], deps
 
-    def ask(t):
-        if t == 0:
-            return send(rank + 1, T.XR[:, 32:48], T.XU[:, 32:48], "rq1", "X0")
-        n, trs = n_arr // 2, []
-        for k in (0, 1):
-            rid, pid, _ = topo.addr(T.cores[(rank + t + k) % NR])
-            c = 32 * t + 16 + 16 * k
-            trs.append(RemoteDMATransfer(dst_ids=[DstId(rid=rid, pnc=pid)], dma_engine_mask=sum(1 << x for x in es[n * k:n * k + n]),
-                                         remote_sem=T.sem["r%s%d" % ("pq"[k], t + k)], srcs=[T.XU[:, c:c + 16]], dsts=[T.XR[:, c:c + 16]]))
-        loc[0] += n_arr
-        g_rem(None, lambda: g.remote_dma_fused(trs, local_sem=T.sem.loc), "X%d" % t)
+    def send(names):
+        trs, deps, k = [], [], 0
+        for a in names:
+            dst_rank, out, srcs, d = write(a)
+            rid, pid, _ = topo.addr(T.cores[dst_rank % NR])
+            n = got(a)[1]
+            trs.append(RemoteDMATransfer(dst_ids=[DstId(rid=rid, pnc=pid)], dma_engine_mask=sum(1 << x for x in es[k:k + n]),
+                                         remote_sem=T.sem[a], srcs=srcs, dsts=[out], alu_op=len(srcs) - 1))
+            deps.append(d)
+            k += n
+        loc[0] += k
+        if len(names) == 1 and len(srcs) == 1:
+            g_rem(None, lambda: g.remote_dma(out, srcs[0], T.sem[a], T.sem.loc, pid, rid, sum(1 << x for x in es)), d)
+        else:
+            g_rem(None, lambda: g.remote_dma_fused(trs, local_sem=T.sem.loc), " ".join(deps))
 
     def select(name, out, in_, pattern, op, fill, base, cm, deps):
         gp(name, lambda: g.affine_select(out, in_, pattern, op, fill, base, cm), deps)
 
-    def same_group(name, n):
-        c = T[name][:, n - 1:128:n]
-        select(name + "1", c, T.ones[:, 0:128 // n], [[-16, 8], [0, 16 // n]], Op.is_ge, 0.0, 0, 1, name + "0")
-        select(name, c, c, [[16, 8], [0, 16 // n]], Op.is_ge, 0.0, 15, -1, name + "1")
-
+    big = -512.0 * FR
+    made = {
+        "Gb": (T.Gb[0:32, 1::2], T.ones[0:32, :], [[-1, 4], [-4, 8], [0, 8]], Op.is_equal, 0.0, 0, 1, "ones"),
+        "L4": (T.L4[0:4, :], T.Gb[0:4, 0:256:2], [[0, 8], [-1, 4], [0, 4]], Op.not_equal, big, 0, 1, "Gb0"),
+        "b4": (T.b4[0:4, :], T.ones[0:4, 0:64], [[0, 16], [-1, 4]], Op.not_equal, 256.0 / big, 0, 1, "ones"),
+        "L8": (T.L8[0:8, :], T.Gb[0:8, 0:256:2], [[0, 8], [-1, 8], [0, 2]], Op.not_equal, big, 0, 1, "Gb0"),
+        "b8": (T.b8[0:8, :], T.ones[0:8, 0:64], [[0, 8], [-1, 8]], Op.not_equal, 0.0, 0, 1, "ones"),
+        "IDN": (T.IDN[:, :], T.ones[:, 0:128], [[-1, 128]], Op.is_equal, 0.0, 0, 1, "ones"),
+        "C7": (T.C7[:, 3:128:4], T.C7[:, 3:128:4], [[-16, 8], [0, 4]], Op.not_equal, UP, -7, 1, "C70"),
+        "CV1": (T.CV[:, 3:128:4], T.ones[:, 0:32], [[-16, 8], [0, 4]], Op.is_ge, 0.0, 0, 1, "CV0"),
+        "CV": (T.CV[:, 3:128:4], T.CV[:, 3:128:4], [[16, 8], [0, 4]], Op.is_ge, 0.0, 15, -1, "CV1"),
+        "C21": (T.C2[:, 1:128:2], T.ones[:, 0:64], [[-16, 8], [0, 8]], Op.is_ge, 0.0, 0, 1, "C20"),
+        "C2": (T.C2[:, 1:128:2], T.C2[:, 1:128:2], [[16, 8], [0, 8]], Op.is_ge, 0.0, 15, -1, "C21"),
+    }
     gp("pc", lambda: g.iota(T.pc[:, :], [[1, 2]], 0, 1))
-    select("Gb", T.Gb[0:32, 1::2], T.ones[0:32, :], [[-1, 4], [-4, 8], [0, 8]], Op.is_equal, 0.0, 0, 1, "ones")
-    select("L4", T.L4[0:4, :], T.ones[0:4, 0:128], [[0, 8], [-1, 4], [0, 4]], Op.is_equal, 0.0, 0, 1, "")
-    select("b4", T.b4[0:4, :], T.c256[0:4, :], [[0, 16], [-1, 4]], Op.is_equal, -512.0 * FR, 0, 1, "c256")
-    select("IDN", T.IDN[:, :], T.ones[:, 0:128], [[-1, 128]], Op.is_equal, 0.0, 0, 1, "")
-    select("C7", T.C7[:, 3:128:4], T.ones[:, 0:32], [[-16, 8], [0, 4]], Op.is_equal, 0.0, -7, 1, "C70")
-    same_group("CV", 4)
-    send(rank + 5, T.ex[:, 112:128], T.ex[:, 80:96], "e5", "e")
-    select("L8", T.L8[0:8, :], T.ones[0:8, 0:128], [[0, 8], [-1, 8], [0, 2]], Op.is_equal, 0.0, 0, 1, "")
-    select("b8", T.b8[0:8, :], T.c256[0:8, :], [[0, 8], [-1, 8]], Op.is_equal, -512.0 * FR, 0, 1, "")
-    same_group("C2", 2)
-    send(rank - 1, half(T.Wl1, 0), half(T.W, 0), "w1a", u(4, 0))
-    send(rank - 1, half(T.Wl1, 1), half(T.W, 1), "w1", "U41")
     for a in OPT["G"].split():
-        t = int(a[1:])
-        if a[0] == "a":
-            ask(t)
-        elif a[0] == "c":
-            select("IDF", T.IDF[:, :], T.ones[:, 0:128], [[-1, 128]], Op.is_equal, 0.0, 0, 1, "")
-        elif a[0] == "w":
-            send(rank - t, T["Wl%d" % t][:, :], T.W[:, :], "w%d" % t, u(4, 0) + " U41")
-        elif a[0] == "p":
-            send(rank + 5, T.pr[:, :], T.pl5[:, :], "p5", "pl5")
-        elif a[0] == "l":
-            send(rank - 5, half(T.rl5, t, 128), half(T.ra5, t, 128), "rs5" + "ab"[t], "ra5%d" % t)
+        if a in made:
+            select(a, *made[a])
+            continue
+        if a == "IDF":
+            select("IDF", T.IDF[:, :], T.ones[:, 0:128], [[-1, 128]], Op.is_equal, 0.0, 0, 1, "ones")
+        elif a == "k1":
+            select("P1", slot(T.TA, 1), T.vbf[:, :], [[0, 512]], Op.is_ge, 0.0, 0, 0, "vs0")
+        elif a == "K1":
+            gp("Pc1", lambda: g.affine_select(slot(T.TC, 1), T.vl[:, :], [[0, 512]], Op.is_ge, 0.0, 0, 0), "", [got("e5")])
         else:
-            send(rank - t, T["rl%d" % t][:, :], T["ra%d" % t][:, :], "rs%d" % t, "ra%d" % t)
+            send(a.split("+"))
 
     ops, index, head = [], {}, {q: 0 for q in queues}
     while any(head[q] < len(order[q]) for q in queues):

import numpy as np
from concourse.bass import DstId, RemoteDMATransfer
from concourse.mybir import dt, AluOpType, AxisListType, ActivationFunctionType

OPT = dict(
    LY="nx32 nxl1 e", LS="nxl0 vs0 x",
    CUT=(0, 256, 512),
    TO="40 x10 x11 41 i10 i11 x20 J00 x21 i20 42 43 J01 i21 x30 x31 I0 o0 20 I1 21 30 31 32  a00 a01 b0 J10 o1 J11 c0 sx  "
       "a10 a11 b1 J20 I2 o2 J21 c1  a20 a21 b2 J30 I3 o3 J31 c2  a30 a31 b3 J40 I4 o4 J41 c3  a40 a41 b4 I5 o5 c4  rb0 ra0 b5 rl1 rl2",
    VO="ones Gb0 idr0 bt1 ci bt2 bt3 ID1 cz lowf lowt cq nxb icol low set1 bq nxt oc0 lst0 A0b  "
       "g00 g01 B10 S10 B11 m1 l10 eu S11  g100 l11 g101 g11 S20 B20 MT l20 B21 S21  g200 l21 g201 g21 S30 EE l30 B31 S31  g300 l31 g301 g31  "
       "P0 R00 R01 P1 s00 xc s01 p00 b0 p01  R10 R11 X0 s10 Q0 s11 p10 b1 p11  R20 R21 X1 s20 Q1 s21 p20 b2 p21  "
       "R30 R31 X2 a10 s30 a11 s31 p30 b3 p31  R40 R41 X3 a20 s40 s41 b4 p4 c4 X40 a21 X41  R5 a3 b5 a40 X5 a41 a5",
    YO="ra5 rl3 rl4",
    SO="D40 C70 CV0 idr1 z0 D4 C20 B0 DM0 A0a bcol v1 k1 ocol DM v2 setc C1 v3 m0 k4 B30 M8 D80 zb m1 D8 C0 m2 M12 k2 m3 k3 IDF "
       "zc zd t1 m4 t0 t2 m5 a0 t3 t4 t5",
    G="Gb L4 C7 b4 IDN CV1 CV L8 b8 C21 C2 T1 w10 w11 w2 w3 w4 q1 U1 w5 p1+q2 U2 T2 p2+q3 U3 r1 p3+q4 T3 p4 r2 r3 r40 r41")
NR = 6
NPOOL = 112
ZB = 16
WIN = ZB + 3 * 512
FR = 4096.0
E0 = 129 * 512.0
UP = 65536.0
BF, F32, I32, U16 = "bfloat16", "float32", "int32", "uint16"
SCRATCH = {}
for _n, _c, _d in (("nx32", 128, I32), ("nxb", 128, BF), ("nxl", 32, I32), ("nxt", 32, I32), ("ex", 128, I32), ("eu", 128, U16), ("pr", 16, U16),
                   ("vbf", 512, BF), ("vl", 512, BF), ("TC", WIN, F32), ("TD", WIN, F32), ("ones", 256, BF), ("c256", 64, BF), ("c0", 64, BF),
                   ("Gb", 512, BF), ("ID1", 128, BF), ("idr", 512, BF),
                   ("CV", 144, BF), ("CB", 144, BF), ("CO", 144, BF), ("C7", 144, BF), ("C2", 144, BF),
                   ("L4", 128, BF), ("b4", 64, BF), ("D4", 64, F32), ("L8", 128, BF), ("b8", 64, BF), ("D8", 64, F32),
                   ("IDN", 128, BF), ("IDF", 128, F32), ("pc", 2, I32), ("ci", 1, I32), ("bt", 4, I32), ("c3", 1, I32),
                   ("icol", 1, F32), ("low", 5, F32), ("c15", 1, F32), ("setc", 2, F32), ("ocol", 2, F32), ("bq", 4, F32),
                   ("bcol", 4, F32), ("en", 16, F32), ("m1", 16, F32), ("DM", 16, F32), ("MT", 16, BF),
                   ("XU", 192, U16), ("XR", 192, U16), ("W", 512, BF), ("mask", 1536, BF),
                   ("TA", WIN, F32), ("TB", WIN, F32), ("yb", 256, F32)):
    SCRATCH[_n] = ("sbuf", [128, _c], _d)
for _n in range(6):
    for _b, _c, _d, _k in (("A", 512, BF, (0,)), ("B", 512, BF, (0, 1, 2, 3)), ("U", 512, BF, (1, 2, 3)),
                           ("vs", 512, BF, (1, 2, 3)), ("scl", 128, F32, (1, 2, 3)), ("lst", 32, U16, (0, 1, 2, 3)),
                           ("Wl", 512, BF, range(1, 6)), ("ra", 256, F32, range(6)), ("rb", 256, F32, range(6)),
                           ("pl", 16, U16, range(1, 6)), ("R", 256, BF, range(6)), ("sa", 128, BF, range(5)),
                           ("rl", 256, F32, range(1, 6)), ("rm", 256, F32, (4, 5))):
        if _n in _k:
            SCRATCH["%s%d" % (_b, _n)] = ("sbuf", [128, _c], _d)
for _n in ("psL0", "psL1", "psL2", "psL3", "psE0", "psE1", "psE2", "psT"):
    SCRATCH[_n] = ("psum", [128, 512], F32)

SEMAPHORES = (["s%d" % k for k in range(NPOOL)] + ["loc", "e5", "n5", "U1", "U2", "U3", "T1", "T2", "T3", "w10", "w11", "r40", "r41", "r50", "r51"]
              + ["%s%d" % (a, k) for a in "wpqr" for k in range(1, 6)])


def rank_program(g, core, T, topo):
    rank = T.rank_of(core)
    if rank is None:
        return
    V, S, P, Y = g.vector, g.scalar, g.tensor, g.sync
    Op, AF = AluOpType, ActivationFunctionType
    queues = {"g": g, "v": V, "s": S, "t": P, "y": Y}
    order = {q: [] for q in queues}

    def adder(q, step=1):
        def add(name, calls, deps="", rem=(), step=step):
            order[q].append((name, calls if isinstance(calls, list) else [calls], deps.split(), list(rem), step))
        return add

    vec, sca, pe, gp = adder("v"), adder("s"), adder("t"), adder("g")
    y_dma, s_dma, g_rem = adder("y", 16), adder("s", 16), adder("g", 0)

    def slot(t, k):
        return t[:, ZB + 512 * (k - 1):ZB + 512 * k]

    def half(t, h, n=256):
        return t[:, 0:2 * n] if h is None else t[:, n * h:n * h + n]

    def tag(t, h):
        return "%d" % t if h is None else "%d%d" % (t, h)

    es = topo.engines(core, [c for c in T.cores if c != core][0])
    n_arr = len(es)
    U = [T.A0, T.U1, T.U2, T.U3, T.W]
    vs = [T.vbf, T.vs1, T.vs2, T.vs3]
    CUT = OPT["CUT"]
    NP = len(CUT) - 1

    def piece(t, k, n=1):
        return t[:, CUT[k] // n:CUT[k + 1] // n]

    bank_a = ["psL2", "psL3"]
    bank_b = ["psL%d" % (t % 2) for t in range(6)]
    bank_p = {2: "psT", 3: "psE2", 4: "psE0"}
    p8, p12 = [" ".join("P%d%d" % (e, h) + (" P%d%dq" % (e, h) if "%s%d0" % (c, h) in OPT["VO"].split() else "") for h in (0, 1))
               for e, c in ((8, "P"), (12, "Q"))]
    tables_a, tables_b = "z0 P1 P2 P3", "zb P4 " + p8 + " " + p12

    tc, td = "T2" in OPT["G"], "U2" in OPT["G"]
    share = {}
    for a in OPT["G"].split():
        names = a.split("+")
        for k, x in enumerate(names):
            share[x] = n_arr // {1: 1, 2: 2, 3: 2 if k == 0 else 4, 4: 4}[len(names)]

    def got(a):
        return a, share[a]

    def arrival(r, h=None):
        if r[1] in "ab":
            return r, []
        return "", [got("r" + r[2] + ("%d" % h if "r" + r[2] + "0" in share else ""))]

    def term(queue, a):
        a, _, more = a.partition("+")
        kind, t, h = a[0], int(a[1]), int(a[2]) if len(a) > 2 else None
        c = 32 * t + 16 * (kind == "a")
        at_home = t == 0 or (kind, t) == ("a", 5) or (t == 5 and td)
        i = half((T.XU if at_home else T.XR)[:, c:c + 16], h, 8)
        name = ("ra" if kind == "a" else "rb") + "%d" % t
        win = (T.TA if kind == "a" else T.TB)[:, :]
        deps = (tables_a if kind == "a" else tables_b) + " " + {"a0": "X0", "t0": "X0"}.get(a[:2], "")
        rem = [] if at_home else [got(("p%d" if kind == "a" else "q%d") % t)]
        if a[:2] == "a5" and tc:
            win, deps, rem = T.TC[:, :], "zc X5" + ("" if "T1" in share else " Pc1"), [got(x) for x in share if x[0] == "T"]
        elif a[:2] == "a5":
            deps += " X5"
        elif a[:2] == "t5" and td:
            win, deps, rem = T.TD[:, :], "zd X41", [got(x) for x in share if x[0] == "U"]
        out = half(T[name], h, 128)
        if queue == "s":
            return sca("r" + "ab"[kind == "t"] + tag(t, h), lambda: S.activation(out, win.indirect(i), AF.Copy), deps, rem)
        more = more or "rb%d" % t
        d, r = arrival(more)
        vec("r" + "ab"[kind == "t"] + tag(t, h), lambda: V.tensor_tensor(out, win.indirect(i), half(T[more], h, 128), Op.add), deps + " " + d, rem + r)

    loads = {"nx32": (T.nx32[0:32, :], T.nx[:, :]), "nxl0": (T.nxl[:, 0:16], T.nx[0::2, :]), "nxl1": (T.nxl[:, 16:32], T.nx[1::2, :]),
             "vs0": (T.vbf[:, :], T.v[:, :]), "e": (T.ex[:, 0:96], T.e[:, :]), "x": (T.ex[:, 96:112], T.x[:, :])}
    for a in OPT["LY"].split():
        y_dma(a, lambda a=a: Y.dma_start(*loads[a]))
    y_dma("y0", lambda: Y.dma_start(T.y[:, 0:128], T.yb[:, 0:128]), "yb0")
    y_dma("end", [], "y0 y1")

    def scan(name, out, b, deps, w=64):
        vec(name, lambda: V.tensor_tensor_scan(out, T.D4[:, 0:w], T[b][:, 0:w], 0.0, Op.mult, Op.max), "D4 " + deps)

    def bit(n):
        return lambda: V.tensor_scalar(T.bt[:, n:n + 1], T.pc[:, 0:1], n, 1, Op.logical_shift_right, Op.bitwise_and), "pc"

    small = {
        "ones": (lambda: V.memset(T.ones[:, :], 1.0), ""),
        "Gb0": (lambda: V.memset(T.Gb[0:32, 0::2], 0.0), ""),
        "idr0": (lambda: V.tensor_tensor_scan(T.idr[:, 0:256], T.ones[:, :], T.ones[:, :], -257.0, Op.mult, Op.add), "ones"),
        "ID1": (lambda: V.tensor_tensor_scan(T.ID1[0:1, :], T.ones[0:1, 0:128], T.ones[0:1, 0:128], 0.0, Op.subtract, Op.mult), "ones"),
        "ci": (lambda: V.tensor_scalar(T.ci[:, :], T.pc[:, 1:2], 15, None, Op.bitwise_and), "pc"),
        "cq": (lambda: V.tensor_scalar(T.c3[:, :], T.pc[:, 1:2], 3, None, Op.bitwise_and), "pc"),
        "bt1": bit(1), "bt2": bit(2), "bt3": bit(3),
        "lowt": (lambda: V.tensor_scalar(T.low[:, 1:4], T.bt[:, 1:4], 1.0 - 1.0 / UP, 1.0 / UP, Op.mult, Op.add), "bt1 bt2 bt3"),
        "lowf": (lambda: V.tensor_scalar(T.low[:, 0:1], T.ci[:, :], 1.0, UP ** -4, Op.min, Op.max), "ci"),
        "low": (lambda: V.tensor_reduce(T.low[:, 4:5], T.low[:, 0:4], AxisListType.X, Op.mult), "lowt lowf"),
        "bq": (lambda: V.tensor_scalar(T.bq[:, 1:4], T.low[:, 1:4], T.low[:, 0:1], 0.5, Op.mult, Op.is_lt), "lowt lowf"),
        "cz": (lambda: V.tensor_scalar(T.c15[:, :], T.ci[:, :], 0.0, UP ** -3, Op.is_equal, Op.mult), "ci"),
        "set1": (lambda: V.tensor_scalar(T.setc[:, 1:2], T.c3[:, :], 0.0, None, Op.is_equal), "cq"),
        "oc0": (lambda: V.tensor_scalar(T.ocol[:, 1:2], T.c3[:, :], 512.0, E0, Op.mult, Op.add), "cq"),
        "icol": (lambda: V.tensor_copy(T.icol[:, :], T.ci[:, :]), "ci"),
        "m1": (lambda: V.tensor_scalar(T.m1[:, :], T.idr[:, 256:272], T.icol[:, 0:1], None, Op.is_equal), "idr1 icol"),
        "MT": (lambda: V.tensor_tensor_scan(T.MT[:, :], T.DM[:, :], T.m1[:, :], 0.0, Op.mult, Op.add), "DM m1"),
        "nxb": (lambda: V.tensor_scalar(T.nxb[0:32, :], T.nx32[0:32, :], -256.0, None, Op.add), "nx32"),
        "nxt": (lambda: V.transpose(T.nxt[:, :], T.nxl[:, :]), "nxl0 nxl1"),
        "lst0": (lambda: V.tensor_copy(T.lst0[:, :], T.nxt[:, :]), "nxt"),
        "A0b": (lambda: V.tensor_scalar(half(T.A0, 1), T.psE1[:, 0:256], T.low[:, 4:5], None, Op.mult), "nx1 low"),
        "eu": (lambda: V.tensor_copy(T.eu[:, 0:112], T.ex[:, 0:112]), "e x"),
        "EE": (lambda: V.tensor_scalar(T.idr[:, 3:384:4], T.ex[:, 0:96], 128.0, E0 - 192.0, Op.mult, Op.add), "e B0 nx0 nx1 m1"),
        "xc": (lambda: V.tensor_scalar(T.idr[:, 387:448:4], T.ex[:, 96:112], -256.0, None, Op.add), "x B0 nx0 nx1"),
        "eu5": (lambda: V.tensor_copy(T.eu[:, 112:128], T.ex[:, 112:128]), "", [] if tc else [got("e5")]),
    }

    def u(m, h=None):
        if h is None:
            return " ".join(u(m, k) for k in range(NP))
        return "U%d%d" % (m, h) + (" U%d%dq" % (m, h) if "g%d%d0" % (m - 1, h) in OPT["VO"].split() else "")

    def compose(n, h, q=None):
        B, L = T["B%d" % n], T["lst%d" % n]
        lo, w = CUT[h], CUT[h + 1] - CUT[h]
        if q is not None:
            lo, w = lo + w // 2 * q, w // 2
        vec("U%d%d" % (n + 1, h) + ("q" if q == 0 else ""),
            lambda: V.tensor_tensor(U[n + 1][:, lo:lo + w], U[n][:, :].indirect(L[:, lo // 16:(lo + w) // 16]), B[:, lo:lo + w], Op.add),
            "A0a A0b B0 lst0" if n == 0 else "%s B%d%d lst%d%d" % (u(n), n, h, n, h))

    def window(m, h):
        vec("B%d%d" % (m, h), lambda: V.tensor_scalar(piece(T["B%d" % m], h), piece(U[m], h), T.bcol[:, m:m + 1], None, Op.mult),
            u(m, h) + " bcol")

    def keep_v(k, q):
        vec("P%d" % k + ("" if q == 3 else "q%d" % q), lambda: V.tensor_copy(half(slot(T.TA, k), q, 128), half(T[bank_p[k]], q, 128)),
            "sum%d%d" % (k, k - 1) + ("" if q < 3 else " P%dq0 P%dq1 P%dq2" % (k, k, k)))

    def consts_v(k):
        c, col = (("CB", "setc"), ("CO", "ocol"))[k]
        vec(c, lambda: V.tensor_scalar(T[c][:, :], T.CV[:, :], T[col][:, 0:1], None, Op.mult), "CV " + col)

    def scan_l(m, h):
        scan("scl%d%d" % (m, h), piece(T["scl%d" % m], h, 4), "psL%d" % h, "xl%d%d" % (m, h), w=(CUT[h + 1] - CUT[h]) // 4)

    def to_list(m, h):
        vec("lst%d%d" % (m, h), lambda: V.tensor_copy(piece(T["lst%d" % m], h, 16), piece(T["scl%d" % m], h, 4)[:, 3::4]), "scl%d%d" % (m, h))

    def visit(t, h=None):
        Wt = T["Wl%d" % t] if t else T.W
        pl = half(T["pl%d" % t][:, :] if t else T.eu[:, 96:112], h, 8)
        if t == 5 and not tc:
            return vec("R5", lambda: V.tensor_tensor(T.R5[:, :], T.W[:, :].indirect(T.pr[:, :]), half(T.mask, 5), Op.mult),
                       "mask5 " + u(4), [got("n5")])
        vec("R" + tag(t, h), lambda: V.tensor_tensor(half(T["R%d" % t], h, 128), Wt[:, :].indirect(pl), half(half(T.mask, t), h, 128), Op.mult),
            "mask%d " % t + ("pl" + tag(t, h) if t else u(4) + " eu"),
            [got(s) for s in share if s[:2] == "w%d" % t])

    def scan_a(t, h):
        vec("sa" + tag(t, h), lambda: V.tensor_tensor_scan(half(T["sa%d" % t], h, 64), T.D8[:, :], T[bank_a[h]][:, 0:64], 0.0, Op.add, Op.max),
            "D8 xa" + tag(t, h))

    def place(t, h=None):
        vec("pl" + tag(t + 1, h), lambda: V.tensor_scalar(half(T["pl%d" % (t + 1)], h, 8), half(T["sa%d" % t], h, 64)[:, 7::8], 256.25, None, Op.add),
            "sa" + tag(t, h) if h is not None else "sa%d0 sa%d1" % (t, t))

    def scan_b(t):
        scan("sb%d" % t, T[bank_b[t]][:, 128:192], bank_b[t], "xb%d" % t)

    def add_v(t):
        vec("sc%d" % t, lambda: V.tensor_tensor(T[bank_b[t]][:, 195:256:4], T["sa%d" % t][:, 7::8], T.idr[:, 64 * t + 67:64 * t + 128:4], Op.add),
            "EE xb%d sa%d0 sa%d1" % (t, t, t))

    def offsets(t, h=None):
        lo, hi = (192 if h == 1 else 64 if t == 0 else 128), (192 if t == 5 or h == 0 else 256)
        c = 32 * t - 16
        vec("X" + tag(t, h), lambda: V.tensor_scalar(T.XU[:, c + lo // 4:c + hi // 4], T[bank_b[t]][:, lo + 3:hi:4], ZB - 255.75 - E0, None, Op.add),
            "sb%d" % t + (" sc%d" % t if hi == 256 else "") + (" sx" if t == 0 else ""))

    def add4(e, h, q=None):
        o, p = [half(half(t, h), q, 128) for t in (slot(T.TB, e // 4), T.psE0)]
        vec("P%d%d" % (e, h) + ("q" if q == 0 else ""), lambda: V.tensor_tensor(o, o, p, Op.add), "M%d P4" % e)

    for a in OPT["VO"].split():
        if a in small:
            vec(a, *small[a])
        elif a[0] in "at":
            term("v", a)
        else:
            {"g": compose, "B": window, "S": scan_l, "l": to_list, "k": keep_v, "C": consts_v, "R": visit, "c": add_v, "s": scan_a, "p": place, "b": scan_b, "X": offsets,
             "P": lambda *h: add4(8, *h), "Q": lambda *h: add4(12, *h)}[a[0]](*[int(x) for x in a[1:]])
    last = {0: "acc", 1: "acc"}
    adds = OPT["YO"].split()
    for k, r in enumerate(adds):
        for h in (1,) if r == "rm5" else (0, 1):
            o, name = (T.psE1, "acc%d%d" % (k, h)) if k < len(adds) - 1 else (T.yb, "yb%d" % h)
            d, rem = arrival(r, h)
            vec(name, lambda o=o, r=r, h=h: V.tensor_tensor(half(o, h, 128), half(T.psE1, h, 128), half(T[r], h, 128), Op.add), last[h] + " " + d, rem)
            last[h] = name

    def act(name, out, in_, deps, rem=(), **k):
        sca(name, lambda: S.activation(out, in_, AF.Copy, **k), deps, rem)

    def mask(t):
        c = 16 * t if t < 5 or tc else 112
        act("mask%d" % t, half(T.mask, t), T.MT[:, :].indirect(T.eu[:, c:c + 16]), "MT eu" if c < 112 else "MT eu5")

    def keep(k):
        act("P%d" % k, slot(T.TA, k) if k < 4 else slot(T.TB, 1), T[bank_p[k]][:, :] if k > 1 else T.vbf[:, :],
            "sum%d%d" % (k, k - 1) if k > 1 else "vs0")

    def moved(e):
        act("M%d" % e, slot(T.TB, e // 4), slot(T.TB, e // 4 - 1).indirect(T.lst2[:, :]), "P4 " + " ".join("lst2%d" % k for k in range(NP)) if e == 8 else p8)

    def consts(n):
        c, col = (("CB", "setc"), ("CO", "ocol"))[n]
        act(c, T[c][:, :], T.CV[:, :], "CV " + col, scale=T[col][:, 0:1])

    def step_v(m):
        act("vs%d" % m, vs[m][:, :], vs[m - 1][:, :].indirect(T.lst0[:, :]), "lst0 vs%d" % (m - 1))

    def rest(mh):
        m, h = divmod(mh, 10)
        act("B%d" % mh, piece(T["B%d" % m], h), piece(U[m], h), u(m, h) + " bcol", scale=T.bcol[:, m:m + 1])

    for a in OPT["LS"].split():
        s_dma(a, lambda a=a: S.dma_start(*loads[a]))
    fills = {
        "D40": (T.D4[:, :], T.ones[:, 0:64], "ones", {}), "D4": (T.D4[:, 0::4], T.ones[:, 0:16], "D40", dict(scale=0.0)),
        "D80": (T.D8[:, :], T.ones[:, 0:64], "ones", dict(scale=0.0)), "D8": (T.D8[:, 0::8], T.ones[:, 0:8], "D80", dict(scale=-1024.0 * FR)),
        "idr1": (T.idr[:, 256:512], T.idr[:, 0:256], "idr0", dict(bias=256.0)),
        "C70": (T.C7[:, :], T.ones[:, 0:144], "ones", dict(scale=0.0)), "CV0": (T.CV[:, :], T.ones[:, 0:144], "ones", dict(scale=0.0)),
        "C20": (T.C2[:, :], T.ones[:, 0:144], "ones", dict(scale=0.0)),
        "B0": (T.B0[:, :], T.idr[:, :], "cz idr0 idr1", dict(scale=T.c15[:, 0:1])),
        "bcol": (T.bcol[:, 1:4], T.bq[:, 1:4], "bq", dict(scale=UP)), "setc": (T.setc[:, 0:1], T.setc[:, 1:2], "set1", dict(scale=FR)),
        "DM0": (T.DM[:, :], T.D4[:, 0:16], "D4 set1", dict(scale=T.setc[:, 1:2])), "DM": (T.DM[:, 1::4], T.DM[:, 1::4], "DM0", dict(scale=1.0 / FR)),
        "A0a": (half(T.A0, 0), T.psE0[:, 0:256], "nx0 low", dict(scale=T.low[:, 4:5])),
        "z0": (T.TA[:, 0:ZB], T.ones[:, 0:ZB], "ones", dict(scale=0.0)), "zb": (T.TB[:, 0:ZB], T.ones[:, 0:ZB], "ones", dict(scale=0.0)),
        "zc": (T.TC[:, 0:ZB], T.ones[:, 0:ZB], "ones", dict(scale=0.0)), "zd": (T.TD[:, 0:ZB], T.ones[:, 0:ZB], "ones", dict(scale=0.0)),
    }
    for a in OPT["SO"].split():
        if a in fills:
            act(a, *fills[a][:3], **fills[a][3])
        elif a == "K1":
            act("Pc1", slot(T.TC, 1), T.vl[:, :], "", [got("e5")])
        elif a == "IDF":
            act("IDF", T.IDF[:, :], T.IDN[:, :], "IDN")
        elif a == "ocol":
            sca(a, lambda: S.activation(T.ocol[:, 0:1], T.setc[:, 1:2], AF.Identity, bias=T.ocol[:, 1:2], scale=-256.0 * FR - E0), "set1 oc0")
        elif a[0] in "at":
            term("s", a)
        else:
            {"m": mask, "k": keep, "M": moved, "v": step_v, "B": rest, "C": consts}[a[0]](int(a[1:]))
    s_dma("y1", lambda: S.dma_start(T.y[:, 128:256], T.yb[:, 128:256]), "yb1")

    def bias(b, deps="", k=4, w=64):
        pe(None, lambda: P.matmul(T[b][:, 0:w], T["L%d" % k][0:k, :], T["b%d" % k][0:k, 0:w], start=True, stop=False),
           "L%d b%d %s" % (k, k, deps))

    def extract(name, b, rows, c, deps, stop=True, n=4, w=64):
        pe(name, [lambda s=s: P.matmul(T[b][:, 0:w], c[:, n - 1 - s:n + 127 - s], rows[:, s::n], start=False, stop=(stop and s == n - 1))
                  for s in range(n)], deps)

    taken = {2: 0, 3: 0, 4: 0}

    def plus(k, i):
        n = taken[k]
        taken[k] += 1
        pe("sum%d%d" % (k, n), lambda: P.matmul(T[bank_p[k]][:, :], T.IDN[:, :], vs[i][:, :], start=(n == 0), stop=(n == k - 1)),
           "IDN vs%d %s" % (i, "A0a" if k == 4 else ""))

    def add_a(name, t, c, places, v, deps):
        pe(name, [lambda k=k, r=r: P.matmul(T[bank_b[t]][:, c:c + 64], T.IDN[:, :], r, start=(k == 0), stop=(k == 1))
                  for k, r in enumerate((T.idr[:, 64 * v:64 * v + 64], places))], "EE " + deps)

    for h in (0, 1):
        pe(None, lambda h=h: P.matmul(T["psE%d" % h][:, 0:256], T.ID1[0:1, :], T.idr[0:1, 256 * h:256 * h + 256], start=True, stop=False),
           "ID1 idr%d" % h)
    for h in (0, 1):
        pe("nx%d" % h, [lambda h=h, q=q: P.matmul(half(T["psE%d" % h], q, 128), half(T.Gb[0:32, :], 2 * h + q, 128), T.nxb[0:32, :],
                                                  start=False, stop=(q == 1)) for q in (0, 1)], "nxb Gb Gb0")
    opened = {k: 0 for k in range(NP)}
    for k in range(NP):
        bias("psL%d" % k, w=(CUT[k + 1] - CUT[k]) // 4)
    to = OPT["TO"].split()
    sums = [r for r in to if r[0] == "r"]
    for n, a in enumerate(to):
        done = to[:n]
        if a[0] == "r":
            d, rem = arrival(a)
            pe("acc" if a == sums[-1] else None,
               lambda a=a: P.matmul(T.psE1[:, 0:256], T.IDF[:, :], T[a][:, :], start=(a == sums[0]), stop=(a == sums[-1])), "IDF A0b " + d, rem)
            continue
        if a == "sx":
            add_a("sx", 0, 64, T.idr[:, 384:448], 0, "xc sb0")
            continue
        m, k = int(a[1]), int(a[-1])
        if a[0] == "x":
            assert opened[k] == m - 1
            extract("xl%d%d" % (m, k), "psL%d" % k, piece(U[m], k), T.C7, u(m, k) + " C7", w=(CUT[k + 1] - CUT[k]) // 4)
        elif a[0] == "i":
            opened[k] = m
            bias("psL%d" % k, "scl%d%d" % (m, k), w=(CUT[k + 1] - CUT[k]) // 4)
        elif a[0] == "I":
            bias(bank_b[m], "X%d" % (m - 2) if m > 1 else "scl3%d" % m)
        elif a[0] == "J":
            bias(bank_a[k], "sa%d%d" % (m - 1, k) if m else "scl3%d" % (2 + k) if 2 + k < NP else "", 8)
        elif a[0] == "o":
            assert "I%d" % m in done
            extract(None, bank_b[m], half(T.mask, m), T.CO, "mask%d CO" % m, stop=False)
        elif a[0] == "a":
            assert "J" + a[1:] in done
            extract("x" + a, bank_a[k], half(T["R%d" % m], k, 128), T.C2, "R%s C2" % a[1:], n=2)
        elif a[0] == "b":
            assert "o%d" % m in done
            extract("x" + a, bank_b[m], T["R%d" % m], T.CB, "CB " + ("R5" if m == 5 else "R%d0 R%d1" % (m, m)))
        elif a[0] == "c":
            if a not in OPT["VO"].split():
                add_a("sc%d" % m, m, 192, T["sa%d" % m][:, 1::2], m + 1, "sa%d0 sa%d1 sb%d" % (m, m, m) + (" X40" if m == 4 and "X40" in OPT["VO"] else ""))
        else:
            plus(int(a[0]), k)

    loc = [0]

    def write(a):
        t, h = int(a[1]), int(a[2]) if len(a) > 2 else None
        if a[0] == "e":
            return (rank - 5, T.vl[:, :], [T.vbf[:, :]], "vs0") if tc else (rank + 5, T.ex[:, 112:128], [T.ex[:, 80:96]], "e")
        if a[0] == "w":
            lo, hi = {None: (0, NP), 0: (0, NP - 1), 1: (NP - 1, NP)}[h]
            return rank - t, T["Wl%d" % t][:, CUT[lo]:CUT[hi]], [T.W[:, CUT[lo]:CUT[hi]]], " ".join(u(4, k) for k in range(lo, hi))
        if a[0] in "pq":
            c = 32 * t + 16 * (a[0] == "p")
            return rank + t, T.XR[:, c:c + 16], [T.XU[:, c:c + 16]], "X%d" % (t - (a[0] == "q")) + ("0" if a == "p4" and "X40" in OPT["VO"] else "1" if a == "q5" and "X41" in OPT["VO"] else "")
        if a[0] == "n":
            return rank + 5, T.pr[:, :], [T.pl5[:, :]], "pl5" if "p4" in OPT["VO"].split() else "pl50 pl51"
        if a[0] == "T":
            return rank - 5, slot(T.TC, t), [slot(T.TA, t)], "P%d" % t
        if a[0] == "U":
            return rank - 5, slot(T.TD, t), [slot(T.TB, t)], ("P4", p8, p12)[t - 1]
        r = "rb5" if t == 5 and tc else "ra%d" % t
        deps = "%s0 %s1" % (r, r) if h is None and ("t50" if r == "rb5" else "a%d0" % t) in (OPT["VO"] + " " + OPT["SO"]).split() else r + a[2:]
        if "a" + a[1:] in OPT["SO"].split():
            return rank - t, half(T["rl%d" % t], h, 128), [half(T[r], h, 128), half(T["rb%d" % t], h, 128)], deps + " rb%d" % t
        return rank - t, half(T["rl%d" % t], h, 128), [half(T[r], h, 128)], deps

    def send(names):
        trs, deps, k = [], [], 0
        for a in names:
            dst_rank, out, srcs, d = write(a)
            rid, pid, _ = topo.addr(T.cores[dst_rank % NR])
            n = got(a)[1]
            trs.append(RemoteDMATransfer(dst_ids=[DstId(rid=rid, pnc=pid)], dma_engine_mask=sum(1 << x for x in es[k:k + n]),
                                         remote_sem=T.sem[a], srcs=srcs, dsts=[out], alu_op=len(srcs) - 1))
            deps.append(d)
            k += n
        loc[0] += k
        if len(names) == 1 and len(srcs) == 1:
            g_rem(None, lambda: g.remote_dma(out, srcs[0], T.sem[a], T.sem.loc, pid, rid, sum(1 << x for x in es)), d)
        else:
            g_rem(None, lambda: g.remote_dma_fused(trs, local_sem=T.sem.loc), " ".join(deps))

    def select(name, out, in_, pattern, op, fill, base, cm, deps):
        gp(name, lambda: g.affine_select(out, in_, pattern, op, fill, base, cm), deps)

    big = -512.0 * FR
    made = {
        "Gb": (T.Gb[0:32, 1::2], T.ones[0:32, :], [[-1, 4], [-4, 8], [0, 8]], Op.is_equal, 0.0, 0, 1, "ones"),
        "L4": (T.L4[0:4, :], T.Gb[0:4, 0:256:2], [[0, 8], [-1, 4], [0, 4]], Op.not_equal, big, 0, 1, "Gb0"),
        "b4": (T.b4[0:4, :], T.ones[0:4, 0:64], [[0, 16], [-1, 4]], Op.not_equal, 256.0 / big, 0, 1, "ones"),
        "L8": (T.L8[0:8, :], T.Gb[0:8, 0:256:2], [[0, 8], [-1, 8], [0, 2]], Op.not_equal, big, 0, 1, "Gb0"),
        "b8": (T.b8[0:8, :], T.ones[0:8, 0:64], [[0, 8], [-1, 8]], Op.not_equal, 0.0, 0, 1, "ones"),
        "IDN": (T.IDN[:, :], T.ones[:, 0:128], [[-1, 128]], Op.is_equal, 0.0, 0, 1, "ones"),
        "C7": (T.C7[:, 3:128:4], T.C7[:, 3:128:4], [[-16, 8], [0, 4]], Op.not_equal, UP, -7, 1, "C70"),
        "CV1": (T.CV[:, 3:128:4], T.ones[:, 0:32], [[-16, 8], [0, 4]], Op.is_ge, 0.0, 0, 1, "CV0"),
        "CV": (T.CV[:, 3:128:4], T.CV[:, 3:128:4], [[16, 8], [0, 4]], Op.is_ge, 0.0, 15, -1, "CV1"),
        "C21": (T.C2[:, 1:128:2], T.ones[:, 0:64], [[-16, 8], [0, 8]], Op.is_ge, 0.0, 0, 1, "C20"),
        "C2": (T.C2[:, 1:128:2], T.C2[:, 1:128:2], [[16, 8], [0, 8]], Op.is_ge, 0.0, 15, -1, "C21"),
    }
    gp("pc", lambda: g.iota(T.pc[:, :], [[1, 2]], 0, 1))
    for a in OPT["G"].split():
        if a in made:
            select(a, *made[a])
            continue
        if a == "IDF":
            select("IDF", T.IDF[:, :], T.ones[:, 0:128], [[-1, 128]], Op.is_equal, 0.0, 0, 1, "ones")
        elif a == "k1":
            select("P1", slot(T.TA, 1), T.vbf[:, :], [[0, 512]], Op.is_ge, 0.0, 0, 0, "vs0")
        elif a == "K1":
            gp("Pc1", lambda: g.affine_select(slot(T.TC, 1), T.vl[:, :], [[0, 512]], Op.is_ge, 0.0, 0, 0), "", [got("e5")])
        else:
            send(a.split("+"))

    ops, index, head = [], {}, {q: 0 for q in queues}
    while any(head[q] < len(order[q]) for q in queues):
        before = len(ops)
        for q in queues:
            while head[q] < len(order[q]) and all(d in index for d in order[q][head[q]][2]):
                name, calls, deps, rem, step = order[q][head[q]]
                index[name] = len(ops)
                ops.append((q, calls, [index[d] for d in deps], rem, step))
                head[q] += 1
        assert len(ops) > before
    known = {q: set() for q in queues}
    seen_rem = {q: set() for q in queues}
    waits, at_issue = [], []
    for k, (q, calls, deps, rem, step) in enumerate(ops):
        w = []
        for d in deps:
            if d not in known[q]:
                w.append(d)
                known[q] |= at_issue[d]
                known[q].add(d)
        w = [d for d in w if not any(d in at_issue[o] for o in w if o != d)]
        waits.append(w)
        at_issue.append(set(known[q]))
    wanted = set(d for w in waits for d in w)
    count, last, sem_of, owner = {}, {}, {}, {}
    free = list(range(NPOOL))
    for k, (q, calls, deps, rem, step) in enumerate(ops):
        eq = queues[q]
        for d in waits[k]:
            eq.wait_ge(T.sem["s%d" % sem_of[d][0]], sem_of[d][1])
        for name, val in rem:
            if name not in seen_rem[q]:
                eq.wait_ge(T.sem[name], val)
                seen_rem[q].add(name)
        if k in wanted:
            s = None
            if step == 1:
                for c in owner.get(q, []):
                    if last[c] in at_issue[k]:
                        s = c
                        break
            if s is None:
                s = free.pop(0)
                count[s] = 0
                if step == 1:
                    owner.setdefault(q, []).append(s)
            for fn in calls:
                fn().then_inc(T.sem["s%d" % s], step)
                count[s] += step
            last[s] = k
            sem_of[k] = (s, count[s])
        else:
            for fn in calls:
                fn()
    g.wait_ge(T.sem.loc, loc[0])
